import numpy as np
import ml_dtypes


def mxq(x, axis, fmt="e4m3"):
    dtype, down = {"e4m3": (ml_dtypes.float8_e4m3fn, 7), "e5m2": (ml_dtypes.float8_e5m2, 14)}[fmt]
    v = np.moveaxis(np.asarray(x, np.float32).astype(ml_dtypes.bfloat16).astype(np.float64), axis, -1)
    blocks = v.reshape(v.shape[:-1] + (-1, 32))
    amax = np.abs(blocks).max(-1, keepdims=True)
    byte = np.maximum(np.where(amax > 0, np.frexp(amax)[1] - 1 + 127, 0) - down, 1)
    scale = np.exp2(byte - 127.0)
    codes = (blocks / scale).astype(np.float32).astype(dtype).astype(np.float64)
    return np.moveaxis((codes * scale).reshape(v.shape), -1, axis)


WIDE = False


def mx_kscale(k):
    if not WIDE:
        return np.ones(k)
    levels = np.array([10, -10, 5, -5, 0])
    if k % 512:
        return np.exp2(np.random.permutation(np.resize(levels, k // 32))).repeat(32)
    a = np.empty((k // 512, 16))
    for p in range(k // 512):
        a[p, :8] = np.random.permutation(np.resize(levels, 8))
        for g in range(8):
            far = levels[np.abs(levels - a[p, g]) >= 10]
            a[p, g + 8] = far[np.random.randint(len(far))]
    return np.exp2(a.ravel()).repeat(32)


def f64(x):
    return np.asarray(x).astype(np.float64)


def striped(idx):
    return np.tile(idx.reshape(-1, 16).T, (8, 1)).astype(np.uint16)


def unstriped(offs):
    return offs[:16].T.reshape(-1).astype(np.int64)


E2M1 = np.array([0.0, 0.5, 1.0, 1.5, 2.0, 3.0, 4.0, 6.0, -0.0, -0.5, -1.0, -1.5, -2.0, -3.0, -4.0, -6.0])


def pack_weight(w, fmt):
    k, n = w.shape
    w = f64(np.asarray(w, np.float32).astype(ml_dtypes.bfloat16)).reshape(k // 32, 32, n)
    amax = np.abs(w).max(1)
    if fmt == "e4m3":
        byte = np.frexp(amax)[1] - 1 + 127 - 7
    else:
        mant, ex = np.frexp(amax / 6.0)
        byte = np.where(mant > 0.5, ex, ex - 1) + 127
    byte = np.clip(np.where(amax > 0, byte, 1), 1, 254)
    scaled = (w * np.exp2(127.0 - byte)[:, None, :]).reshape(k, n).astype(np.float32)
    by_word = np.ascontiguousarray(scaled.reshape(k // 512, 128, 4, n).transpose(0, 1, 3, 2))
    if fmt == "e4m3":
        words = by_word.astype(ml_dtypes.float8_e4m3fn).view(np.uint8)
    else:
        c = by_word.astype(ml_dtypes.float4_e2m1fn).view(np.uint8) & 0xF
        words = (c[..., 0::2] | (c[..., 1::2] << 4)).reshape(k // 512, 128, 2 * n)
    return np.ascontiguousarray(words), np.ascontiguousarray(byte.astype(np.uint8).reshape(k // 512, 16, n))


def unpack_weight(words, scales, fmt):
    g, _, n = scales.shape
    words = np.ascontiguousarray(words).reshape(g, 128, n, -1)
    if fmt == "e4m3":
        vals = words.view(ml_dtypes.float8_e4m3fn).astype(np.float64)
    else:
        nib = np.empty((g, 128, n, 4), np.uint8)
        nib[..., 0::2] = words & 0xF
        nib[..., 1::2] = words >> 4
        vals = E2M1[nib]
    vals = vals * np.repeat(np.exp2(scales.astype(np.float64) - 127.0), 8, axis=1)[..., None]
    return vals.transpose(0, 1, 3, 2).reshape(g * 512, n)


def gelu(v):
    return 0.5 * v * (1.0 + np.tanh(np.sqrt(2.0 / np.pi) * (v + 0.044715 * v**3)))


K, K2, H, N, T, T2, S, P = 1024, 512, 1024, 256, 2048, 2048, 1024, 1024

def setup_inputs():
    n = np.random.standard_normal
    s = mx_kscale(K)[:, None]
    s2 = mx_kscale(K2)[:, None]
    u = mx_kscale(H)[:, None]
    tab_words, tab_scales = pack_weight(n((K, T)) * s, "e4m3")
    wl_words, wl_scales = pack_weight(n((K, H)) / np.sqrt(K) / s, "e2m1")
    wo_words, wo_scales = pack_weight(1.5 * n((H, N)) / np.sqrt(H) / u, "e4m3")
    return {
        "tab_words": tab_words, "tab_scales": tab_scales,
        "offs": striped(np.random.permutation(T)[:P]),
        "xs": (np.round(16 * n((K2, S))) / 16 * s2).astype(np.float32),
        "base": (n((K2, T2)) * s2).astype(np.float32),
        "offs2": striped(np.random.permutation(T2)[:S]),
        "offs3": striped(np.random.permutation(T2)[:P]),
        "wa": (n((K2, H)) / np.sqrt(K2) / s2 * u.T).astype(np.float32),
        "wl_words": wl_words, "wl_scales": wl_scales,
        "bl": (0.5 * n(H)).astype(np.float32),
        "wo_words": wo_words, "wo_scales": wo_scales,
        "wr": (n((K, N)) / np.sqrt(K) / s).astype(np.float32),
        "bo": (0.5 * n(N)).astype(np.float32),
    }

def reference(tab_words, tab_scales, offs, xs, base, offs2, offs3, wa,
              wl_words, wl_scales, bl, wo_words, wo_scales, wr, bo):
    v = unpack_weight(tab_words, tab_scales, "e4m3")[:, unstriped(offs)]
    page = f64(base).copy()
    page[:, unstriped(offs2)] = f64(xs)
    a = mxq(f64(wa), 0, "e4m3").T @ mxq(page, 0, "e4m3")
    b = unpack_weight(wl_words, wl_scales, "e2m1").T @ v
    gate = 1.0 / (1.0 + np.exp(-(b + f64(bl)[:, None])))
    z = mxq(a[:, unstriped(offs3)] * gate, 0, "e4m3")
    y = (unpack_weight(wo_words, wo_scales, "e4m3").T @ z
              + mxq(f64(wr), 0, "e4m3").T @ v)
    return y + f64(bo)[:, None]

@@ -1,0 +1,330 @@
+from contextlib import ExitStack
+
+import concourse.mybir as mybir
+
+K, K2, H, N, T, S = 1024, 512, 1024, 256, 2048, 1024
+FLOPS = 5368709120
+
+F32 = mybir.dt.float32
+BF16 = mybir.dt.bfloat16
+I32 = mybir.dt.int32
+U32 = mybir.dt.uint32
+U16 = mybir.dt.uint16
+U8 = mybir.dt.uint8
+FP8X4 = mybir.dt.float8_e4m3fn_x4
+FP4X4 = mybir.dt.float4_e2m1fn_x4
+ACT = mybir.ActivationFunctionType
+ALU = mybir.AluOpType
+
+P = 128
+BANK = 512
+
+
+def tile_list_lane_agent_update_kernel(
+    tc, tab_words, tab_scales, offs, xs, base, offs2, offs3, wa,
+    wl_words, wl_scales, bl, wo_words, wo_scales, wr, bo, out,
+):
+    nc = tc.nc
+    with ExitStack() as ctx:
+        lists = ctx.enter_context(tc.tile_pool(name="lists", bufs=1))
+        keep = ctx.enter_context(tc.tile_pool(name="keep", bufs=1))
+        psum = ctx.enter_context(tc.psum_pool(name="psum", bufs=1))
+
+        def tile(name, shape, dtype, tag=None):
+            return keep.tile(shape, dtype, name=name, tag=tag or name, align_bytes=64)
+
+        idx = lists.tile([P, S // 16], U16, name="idx")
+        idx2 = lists.tile([P, S // 16], U16, name="idx2")
+        idx3 = lists.tile([P, S // 16], U16, name="idx3")
+
+        tab_sc = tile("tab_sc", [P, T], U8)
+        wl_sc_raw = tile("wl_sc_raw", [P, 2, H], U8)
+        v_sc1 = tile("v_sc1", [P, S], U8)
+        wo_sc = tile("wo_sc", [P, 2, N], U8)
+        nc.gpsimd.memset(tab_sc[:].bitcast(I32), 0)
+        nc.gpsimd.memset(wl_sc_raw[:].bitcast(I32), 0)
+        nc.gpsimd.memset(v_sc1[:].bitcast(I32), 0)
+        nc.gpsimd.memset(wo_sc[:].bitcast(I32), 0)
+
+        nc.sync.dma_start(idx[:], offs)
+        wl_raw = tile("wl_raw", [P, 2, 2 * H], U8)
+        nc.sync.dma_start(wl_raw[:].bitcast(I32), wl_words.rearrange("a p c -> p a c").bitcast(I32))
+        for q in range(4):
+            nc.sync.dma_start(tab_sc[32 * q : 32 * q + 8, :].bitcast(I32), tab_scales[:, 4 * q : 4 * q + 4, :].bitcast(I32))
+        tab = []
+        for a in range(2):
+            tab.append(tile("tab%d" % a, [P, T], I32))
+            nc.sync.dma_start(tab[a][:], tab_words[a].rearrange("p n i -> p (n i)").bitcast(I32))
+        for q in range(4):
+            nc.sync.dma_start(
+                wl_sc_raw[32 * q : 32 * q + 4, :, :].bitcast(I32),
+                wl_scales[:, 4 * q : 4 * q + 4, :].rearrange("a r c -> r a c").bitcast(I32),
+            )
+        nc.sync.dma_start(idx2[:], offs2)
+        bl_sb = tile("bl_sb", [P, 2, 4], F32)
+        nc.sync.dma_start(bl_sb[:], bl.rearrange("(b p t) -> p b t", b=2, t=4))
+
+        base_rows = base.rearrange("(p t) c -> t p c", t=4)
+        xs_rows = xs.rearrange("(p t) c -> t p c", t=4)
+        wa_rows = wa.rearrange("(p j) c -> p j c", j=4)
+        page = [tile("page%d" % t, [P, T], F32) for t in range(4)]
+        xs_sb = [tile("xs%d" % u, [P, 2, S], F32, tag="ring%d" % u) for u in range(2)]
+        wa_raw = [tile("wa_raw%d" % b, [P, 4, BANK], F32, tag="ring%d" % (2 + b)) for b in range(2)]
+        wr_raw = tile("wr_raw", [P, 2, 4, N], F32, tag="wr_raw")
+
+        def load_plane(t):
+            nc.sync.dma_start(page[t][:], base_rows[t])
+            nc.sync.dma_start(xs_sb[t // 2][:, t % 2, :], xs_rows[t])
+
+        load_plane(0)
+        nc.sync.dma_start(wa_raw[0][:], wa_rows[:, :, 0:BANK])
+        load_plane(1)
+        nc.sync.dma_start(wa_raw[1][:], wa_rows[:, :, BANK : 2 * BANK])
+        load_plane(2)
+        load_plane(3)
+        nc.sync.dma_start(idx3[:], offs3)
+        nc.sync.dma_start(wr_raw[:], wr.rearrange("(a p j) n -> p a j n", a=2, j=4))
+        wo_sb = tile("wo_sb", [P, 2, N], I32)
+        nc.sync.dma_start(wo_sb[:], wo_words.rearrange("a p n i -> p a (n i)").bitcast(I32))
+        for q in range(4):
+            nc.sync.dma_start(
+                wo_sc[32 * q : 32 * q + 4, :, :].bitcast(I32),
+                wo_scales[:, 4 * q : 4 * q + 4, :].rearrange("a r c -> r a c").bitcast(I32),
+            )
+        bo_sb = tile("bo_sb", [P, 2], F32)
+        with nc.allow_non_contiguous_dma(reason="one bias value for each partition"):
+            nc.sync.dma_start(bo_sb[:], bo.rearrange("(h p) -> p h", p=P))
+
+        wl_perm = tile("wl_perm", [P, 2, 2 * H], U8)
+        for a in range(2):
+            nc.vector.tensor_copy(
+                wl_perm[:, a, :].bitcast(U16).rearrange("p (b t m) -> p b t m", b=2, t=4),
+                wl_raw[:, a, :].bitcast(U16).rearrange("p (b m t) -> p b t m", b=2, t=4),
+            )
+        v_sc0 = tile("v_sc0", [P, S], U8)
+        nc.vector.tensor_copy(v_sc0[:], tab_sc[:].indirect(idx[:]))
+        for q in range(4):
+            nc.scalar.dma_start(v_sc1[32 * q : 32 * q + 4, :].bitcast(I32), v_sc0[32 * q + 4 : 32 * q + 8, :].bitcast(I32))
+        v_sc = [v_sc0, v_sc1]
+        v = [tile("v%d" % a, [P, S], U32) for a in range(2)]
+        nc.vector.tensor_copy(v[0][:], tab[0][:].bitcast(U32).indirect(idx[:]))
+        wl_sc = tile("wl_sc", [P, 2, H], U8)
+        nc.vector.tensor_copy(
+            wl_sc[:].rearrange("p a (b t m) -> p (a b) t m", b=2, t=4),
+            wl_sc_raw[:].rearrange("p a (b m t) -> p (a b) t m", b=2, t=4),
+        )
+        for h in range(2):
+            nc.vector.tensor_copy(
+                v[1][:, h * BANK : (h + 1) * BANK], tab[1][:].bitcast(U32).indirect(idx[:, 32 * h : 32 * (h + 1)])
+            )
+
+        gate = [[tile("gate%d_%d" % (s, h), [P, BANK], F32) for h in range(2)] if s == 7 else None for s in range(8)]
+        for s in range(7):
+            whole = tile("gate%d" % s, [P, S], F32)
+            gate[s] = [whole[:, 0:BANK], whole[:, BANK:S], whole]
+        for h in range(2):
+            for s in range(8):
+                cols = slice(h * BANK, (h + 1) * BANK)
+                acc = psum.tile([P, BANK], F32, name="acc", tag="bank%d" % s)
+                for a in range(2):
+                    nc.tensor.matmul_mx(
+                        out=acc[:],
+                        lhsT=wl_perm[:, a, 2 * P * s : 2 * P * (s + 1)].bitcast(FP4X4),
+                        lhsT_scale=wl_sc[:, a, P * s : P * (s + 1)],
+                        rhs=v[a][:, cols].bitcast(FP8X4),
+                        rhs_scale=v_sc[a][:, cols],
+                        start=(a == 0),
+                        stop=(a == 1),
+                    )
+                nc.scalar.activation(gate[s][h][:], acc[:], ACT.Sigmoid, bias=bl_sb[:, s // 4, s % 4 : s % 4 + 1])
+
+        wa_codes = tile("wa_codes", [P, H], U32)
+        wa_sc = tile("wa_sc", [P, H], U8)
+        wa_bf = [tile("wa_bf%d" % b, [P, 4 * BANK], BF16, tag="wabf%d" % b) for b in range(2)]
+
+        def round_wa(b):
+            nc.scalar.copy(
+                wa_bf[b][:].rearrange("p (t m j) -> p m j t", t=4, j=4),
+                wa_raw[b][:].rearrange("p j (m t) -> p m j t", t=4),
+            )
+
+        def quantise_wa(b):
+            cols = slice(b * BANK, (b + 1) * BANK)
+            nc.vector.quantize_mx(out=wa_codes[:, cols].bitcast(FP8X4), scales=wa_sc[:, cols], in_=wa_bf[b][:])
+
+        stage = [tile("stage%d" % u, [P, 2, T], BF16, tag="zf%d" % u) for u in range(2)]
+        page_bf = [tile("page_bf%d" % c, [P, BANK, 4], BF16, tag="bf%d" % c) for c in range(4)]
+
+        def scatter(t):
+            nc.vector.tensor_copy(page[t][:].indirect(idx2[:]), xs_sb[t // 2][:, t % 2, :])
+
+        def copy_on(engine, dst, src):
+            if engine == "vector":
+                nc.vector.tensor_copy(dst, src)
+            else:
+                nc.scalar.copy(dst, src)
+
+        def weave_pair(engine, u, c):
+            copy_on(
+                engine,
+                page_bf[c][:, :, 2 * u : 2 * u + 2],
+                stage[u][:, :, c * BANK : (c + 1) * BANK].rearrange("p e c -> p c e"),
+            )
+
+        scatter(0)
+        round_wa(0)
+        nc.scalar.copy(stage[0][:, 0, :], page[0][:])
+        scatter(1)
+        quantise_wa(0)
+        round_wa(1)
+        nc.scalar.copy(stage[0][:, 1, :], page[1][:])
+        for c in range(4):
+            weave_pair("scalar", 0, c)
+        scatter(2)
+        quantise_wa(1)
+        nc.scalar.copy(stage[1][:, 0, :], page[2][:])
+        scatter(3)
+        nc.vector.tensor_copy(stage[1][:, 1, 0 : T // 2], page[3][:, 0 : T // 2])
+        nc.scalar.copy(stage[1][:, 1, T // 2 : T], page[3][:, T // 2 : T])
+        page_codes = tile("page_codes", [P, T], U32)
+        page_sc = tile("page_sc", [P, T], U8)
+
+        def quantise_page(c):
+            cols = slice(c * BANK, (c + 1) * BANK)
+            nc.vector.quantize_mx(
+                out=page_codes[:, cols].bitcast(FP8X4), scales=page_sc[:, cols],
+                in_=page_bf[c][:].rearrange("p c t -> p (c t)"),
+            )
+
+        weave_pair("vector", 1, 0)
+        weave_pair("vector", 1, 1)
+        weave_pair("scalar", 1, 2)
+        weave_pair("scalar", 1, 3)
+        for c in range(4):
+            quantise_page(c)
+
+        a_sb = []
+        a_tags = ["ring2", "ring3", "ring0", "ring1", "ring4"]
+
+        def project(s):
+            a_sb.append(tile("a%d" % s, [P, T], F32, tag=a_tags[s % 5]))
+            for c in range(4):
+                cols = slice(c * BANK, (c + 1) * BANK)
+                acc = psum.tile([P, BANK], F32, name="acc", tag="bank%d" % c)
+                nc.tensor.matmul_mx(
+                    out=acc[:],
+                    lhsT=wa_codes[:, P * s : P * (s + 1)].bitcast(FP8X4),
+                    lhsT_scale=wa_sc[:, P * s : P * (s + 1)],
+                    rhs=page_codes[:, cols].bitcast(FP8X4),
+                    rhs_scale=page_sc[:, cols],
+                    start=True,
+                    stop=True,
+                )
+                copy_on("vector" if (s, c) == (0, 3) else "scalar", a_sb[s][:, cols], acc[:])
+
+        def pick(s, z_f32, j0, j1):
+            g = gate[s][2][:] if j1 - j0 == S else gate[s][j0 // BANK][:, j0 % BANK : j0 % BANK + j1 - j0]
+            nc.vector.tensor_tensor(
+                z_f32[:, s % 4, :], a_sb[s][:].indirect(idx3[:, j0 // 16 : j1 // 16]), g, ALU.mult
+            )
+
+        z_codes = tile("z_codes", [P, 2, S], U32, tag="page_codes")
+        z_sc = tile("z_sc", [P, 2, S], U8, tag="page_sc")
+
+        def round_z(engine, z_bf, z_f32):
+            copy_on(
+                engine,
+                z_bf.rearrange("p (c i) t -> p c t i", i=4),
+                z_f32.rearrange("p t (c i) -> p c t i", i=4),
+            )
+
+        def quantise_z(b, j0, j1, z_bf):
+            nc.vector.quantize_mx(
+                out=z_codes[:, b, j0:j1].bitcast(FP8X4), scales=z_sc[:, b, j0:j1],
+                in_=z_bf.rearrange("p c t -> p (c t)"),
+            )
+
+        wr_bf = [tile("wr_bf%d" % a, [P, N, 4], BF16, tag=("bf3", "wa_codes")[a]) for a in range(2)]
+        wr_codes = tile("wr_codes", [P, 2, N], U32)
+        wr_sc = tile("wr_sc", [P, 2, N], U8)
+
+        def round_wr(engine, a):
+            copy_on(
+                engine,
+                wr_bf[a][:].rearrange("p (c i) j -> p c j i", i=4),
+                wr_raw[:, a, :, :].rearrange("p j (c i) -> p c j i", i=4),
+            )
+
+        def quantise_wr(a):
+            nc.vector.quantize_mx(
+                out=wr_codes[:, a, :].bitcast(FP8X4), scales=wr_sc[:, a, :],
+                in_=wr_bf[a][:].rearrange("p n j -> p (n j)"),
+            )
+
+        round_wr("vector", 0)
+        z0 = tile("z0", [P, 4, S], F32, tag="zf0")
+        for s in range(4):
+            project(s)
+            pick(s, z0, 0, S)
+        z0_bf = [tile("z0_bf%d" % h, [P, BANK, 4], BF16, tag="bf%d" % h) for h in range(2)]
+        round_z("vector", z0_bf[0][:], z0[:, :, 0:BANK])
+        for s in range(4, 8):
+            project(s)
+        round_wr("scalar", 1)
+
+        pieces = [(0, 512), (512, 768), (768, 1024)]
+        z1_tags = ["zf1", "gate7_0", "bf2"]
+        z1 = {}
+        z1_bf = {}
+
+        def pick_piece(n):
+            j0, j1 = pieces[n]
+            z1[n] = tile("z1_%d" % n, [P, 4, j1 - j0], F32, tag=z1_tags[n])
+            for s in range(4, 8):
+                pick(s, z1[n], j0, j1)
+
+        def round_piece(engine, n):
+            j0, j1 = pieces[n]
+            z1_bf[n] = tile("z1_bf%d" % n, [P, j1 - j0, 4], BF16, tag="bf%d" % (2 + n))
+            round_z(engine, z1_bf[n][:], z1[n][:])
+
+        def finish(n):
+            j0, j1 = pieces[n]
+            for h in range(2):
+                rows = slice(h * P, (h + 1) * P)
+                acc = psum.tile([P, j1 - j0], F32, name="acc", tag="bank%d" % ((4 + 2 * n + h) % 8))
+                passes = [
+                    (wo_sb[:, 0, rows], wo_sc[:, 0, rows], z_codes[:, 0, j0:j1], z_sc[:, 0, j0:j1]),
+                    (wr_codes[:, 0, rows], wr_sc[:, 0, rows], v[0][:, j0:j1], v_sc[0][:, j0:j1]),
+                    (wr_codes[:, 1, rows], wr_sc[:, 1, rows], v[1][:, j0:j1], v_sc[1][:, j0:j1]),
+                    (wo_sb[:, 1, rows], wo_sc[:, 1, rows], z_codes[:, 1, j0:j1], z_sc[:, 1, j0:j1]),
+                ]
+                for i, (w, w_sc, x, x_sc) in enumerate(passes):
+                    nc.tensor.matmul_mx(
+                        out=acc[:], lhsT=w.bitcast(FP8X4), lhsT_scale=w_sc, rhs=x.bitcast(FP8X4), rhs_scale=x_sc,
+                        start=(i == 0), stop=(i == 3),
+                    )
+                res = tile("res%d_%d" % (n, h), [P, j1 - j0], F32, tag="wabf%d" % h if n == 0 else None)
+                if n == 2 and h == 1:
+                    nc.vector.tensor_scalar(res[:], acc[:], bo_sb[:, h : h + 1], None, ALU.add)
+                else:
+                    nc.scalar.activation(res[:], acc[:], ACT.Identity, bias=bo_sb[:, h : h + 1])
+                nc.sync.dma_start(out[rows, j0:j1], res[:])
+
+        pick_piece(0)
+        quantise_wr(0)
+        quantise_z(0, 0, BANK, z0_bf[0][:])
+        round_piece("scalar", 0)
+        round_z("scalar", z0_bf[1][:], z0[:, :, BANK:S])
+        pick_piece(1)
+        quantise_wr(1)
+        quantise_z(1, *pieces[0], z1_bf[0][:])
+        finish(0)
+        round_piece("scalar", 1)
+        pick_piece(2)
+        quantise_z(0, BANK, S, z0_bf[1][:])
+        quantise_z(1, *pieces[1], z1_bf[1][:])
+        round_piece("vector", 2)
+        finish(1)
+        quantise_z(1, *pieces[2], z1_bf[2][:])
+        finish(2)

@@ -41,14 +41,15 @@ def tile_list_lane_agent_update_kernel(
         wl_sc_raw = tile("wl_sc_raw", [P, 2, H], U8)
         v_sc1 = tile("v_sc1", [P, S], U8)
         wo_sc = tile("wo_sc", [P, 2, N], U8)
-        nc.gpsimd.memset(tab_sc[:].bitcast(I32), 0)
+        nc.vector.memset(tab_sc[:].bitcast(I32), 0)
         nc.gpsimd.memset(wl_sc_raw[:].bitcast(I32), 0)
-        nc.gpsimd.memset(v_sc1[:].bitcast(I32), 0)
-        nc.gpsimd.memset(wo_sc[:].bitcast(I32), 0)
+        nc.vector.memset(v_sc1[:].bitcast(I32), 0)
+        nc.vector.memset(wo_sc[:].bitcast(I32), 0)
 
         nc.sync.dma_start(idx[:], offs)
         wl_raw = tile("wl_raw", [P, 2, 2 * H], U8)
-        nc.sync.dma_start(wl_raw[:].bitcast(I32), wl_words.rearrange("a p c -> p a c").bitcast(I32))
+        for a in range(2):
+            nc.sync.dma_start(wl_raw[:, a, :].bitcast(I32), wl_words[a].bitcast(I32))
         for q in range(4):
             nc.sync.dma_start(tab_sc[32 * q : 32 * q + 8, :].bitcast(I32), tab_scales[:, 4 * q : 4 * q + 4, :].bitcast(I32))
         tab = []
@@ -63,37 +64,6 @@ def tile_list_lane_agent_update_kernel(
         nc.sync.dma_start(idx2[:], offs2)
         bl_sb = tile("bl_sb", [P, 2, 4], F32)
         nc.sync.dma_start(bl_sb[:], bl.rearrange("(b p t) -> p b t", b=2, t=4))
-
-        base_rows = base.rearrange("(p t) c -> t p c", t=4)
-        xs_rows = xs.rearrange("(p t) c -> t p c", t=4)
-        wa_rows = wa.rearrange("(p j) c -> p j c", j=4)
-        page = [tile("page%d" % t, [P, T], F32) for t in range(4)]
-        xs_sb = [tile("xs%d" % u, [P, 2, S], F32, tag="ring%d" % u) for u in range(2)]
-        wa_raw = [tile("wa_raw%d" % b, [P, 4, BANK], F32, tag="ring%d" % (2 + b)) for b in range(2)]
-        wr_raw = tile("wr_raw", [P, 2, 4, N], F32, tag="wr_raw")
-
-        def load_plane(t):
-            nc.sync.dma_start(page[t][:], base_rows[t])
-            nc.sync.dma_start(xs_sb[t // 2][:, t % 2, :], xs_rows[t])
-
-        load_plane(0)
-        nc.sync.dma_start(wa_raw[0][:], wa_rows[:, :, 0:BANK])
-        load_plane(1)
-        nc.sync.dma_start(wa_raw[1][:], wa_rows[:, :, BANK : 2 * BANK])
-        load_plane(2)
-        load_plane(3)
-        nc.sync.dma_start(idx3[:], offs3)
-        nc.sync.dma_start(wr_raw[:], wr.rearrange("(a p j) n -> p a j n", a=2, j=4))
-        wo_sb = tile("wo_sb", [P, 2, N], I32)
-        nc.sync.dma_start(wo_sb[:], wo_words.rearrange("a p n i -> p a (n i)").bitcast(I32))
-        for q in range(4):
-            nc.sync.dma_start(
-                wo_sc[32 * q : 32 * q + 4, :, :].bitcast(I32),
-                wo_scales[:, 4 * q : 4 * q + 4, :].rearrange("a r c -> r a c").bitcast(I32),
-            )
-        bo_sb = tile("bo_sb", [P, 2], F32)
-        with nc.allow_non_contiguous_dma(reason="one bias value for each partition"):
-            nc.sync.dma_start(bo_sb[:], bo.rearrange("(h p) -> p h", p=P))
 
         wl_perm = tile("wl_perm", [P, 2, 2 * H], U8)
         for a in range(2):
@@ -113,10 +83,38 @@ def tile_list_lane_agent_update_kernel(
             wl_sc[:].rearrange("p a (b t m) -> p (a b) t m", b=2, t=4),
             wl_sc_raw[:].rearrange("p a (b m t) -> p (a b) t m", b=2, t=4),
         )
-        for h in range(2):
-            nc.vector.tensor_copy(
-                v[1][:, h * BANK : (h + 1) * BANK], tab[1][:].bitcast(U32).indirect(idx[:, 32 * h : 32 * (h + 1)])
+        nc.vector.tensor_copy(v[1][:], tab[1][:].bitcast(U32).indirect(idx[:]))
+
+        base_rows = base.rearrange("(p t) c -> t p c", t=4)
+        xs_rows = xs.rearrange("(p t) c -> t p c", t=4)
+        wa_rows = wa.rearrange("(p j) c -> p j c", j=4)
+        page = [tile("page%d" % t, [P, T], F32) for t in range(4)]
+        xs_sb = [tile("xs%d" % t, [P, S], F32, tag=("ring0", "ring1", "ring4", "wa_codes")[t]) for t in range(4)]
+        wa_raw = [tile("wa_raw%d" % b, [P, 4, BANK], F32, tag="ring%d" % (2 + b)) for b in range(2)]
+        wr_raw = tile("wr_raw", [P, 2, 4, N], F32, tag="wr_raw")
+
+        def load_plane(t):
+            nc.sync.dma_start(page[t][:], base_rows[t])
+            nc.sync.dma_start(xs_sb[t][:], xs_rows[t])
+
+        load_plane(0)
+        nc.sync.dma_start(wa_raw[0][:], wa_rows[:, :, 0:BANK])
+        load_plane(1)
+        nc.sync.dma_start(wa_raw[1][:], wa_rows[:, :, BANK : 2 * BANK])
+        load_plane(2)
+        nc.sync.dma_start(wr_raw[:], wr.rearrange("(a p j) n -> p a j n", a=2, j=4))
+        load_plane(3)
+        nc.sync.dma_start(idx3[:], offs3)
+        wo_sb = tile("wo_sb", [P, 2, N], I32)
+        nc.sync.dma_start(wo_sb[:], wo_words.rearrange("a p n i -> p a (n i)").bitcast(I32))
+        for q in range(4):
+            nc.sync.dma_start(
+                wo_sc[32 * q : 32 * q + 4, :, :].bitcast(I32),
+                wo_scales[:, 4 * q : 4 * q + 4, :].rearrange("a r c -> r a c").bitcast(I32),
             )
+        bo_sb = tile("bo_sb", [P, 2], F32)
+        with nc.allow_non_contiguous_dma(reason="one bias value for each partition"):
+            nc.sync.dma_start(bo_sb[:], bo.rearrange("(h p) -> p h", p=P))
 
         gate = [[tile("gate%d_%d" % (s, h), [P, BANK], F32) for h in range(2)] if s == 7 else None for s in range(8)]
         for s in range(7):
@@ -140,7 +138,7 @@ def tile_list_lane_agent_update_kernel(
 
         wa_codes = tile("wa_codes", [P, H], U32)
         wa_sc = tile("wa_sc", [P, H], U8)
-        wa_bf = [tile("wa_bf%d" % b, [P, 4 * BANK], BF16, tag="wabf%d" % b) for b in range(2)]
+        wa_bf = [tile("wa_bf%d" % b, [P, 4 * BANK], BF16, tag=("wabf0", "ring2")[b]) for b in range(2)]
 
         def round_wa(b):
             nc.scalar.copy(
@@ -152,11 +150,11 @@ def tile_list_lane_agent_update_kernel(
             cols = slice(b * BANK, (b + 1) * BANK)
             nc.vector.quantize_mx(out=wa_codes[:, cols].bitcast(FP8X4), scales=wa_sc[:, cols], in_=wa_bf[b][:])
 
-        stage = [tile("stage%d" % u, [P, 2, T], BF16, tag="zf%d" % u) for u in range(2)]
+        stage = [tile("stage%d" % u, [P, 4, T // 2], BF16, tag=("ring3", "wr_raw")[u]) for u in range(2)]
         page_bf = [tile("page_bf%d" % c, [P, BANK, 4], BF16, tag="bf%d" % c) for c in range(4)]
 
         def scatter(t):
-            nc.vector.tensor_copy(page[t][:].indirect(idx2[:]), xs_sb[t // 2][:, t % 2, :])
+            nc.vector.tensor_copy(page[t][:].indirect(idx2[:]), xs_sb[t][:])
 
         def copy_on(engine, dst, src):
             if engine == "vector":
@@ -164,28 +162,32 @@ def tile_list_lane_agent_update_kernel(
             else:
                 nc.scalar.copy(dst, src)
 
-        def weave_pair(engine, u, c):
+        def round_plane(engine, t, u):
+            copy_on(engine, stage[u][:, t, :], page[t][:, u * T // 2 : (u + 1) * T // 2])
+
+        def weave(engine, c, c0, c1):
+            first = (c % 2) * BANK
             copy_on(
                 engine,
-                page_bf[c][:, :, 2 * u : 2 * u + 2],
-                stage[u][:, :, c * BANK : (c + 1) * BANK].rearrange("p e c -> p c e"),
+                page_bf[c][:, c0:c1, :].rearrange("p (c i) t -> p c t i", i=4),
+                stage[c // 2][:, :, first + c0 : first + c1].rearrange("p t (c i) -> p c t i", i=4),
             )
 
-        scatter(0)
+        wr_bf = tile("wr_bf", [P, 2, N, 4], BF16, tag="wl_raw")
         round_wa(0)
-        nc.scalar.copy(stage[0][:, 0, :], page[0][:])
-        scatter(1)
-        quantise_wa(0)
         round_wa(1)
-        nc.scalar.copy(stage[0][:, 1, :], page[1][:])
-        for c in range(4):
-            weave_pair("scalar", 0, c)
-        scatter(2)
-        quantise_wa(1)
-        nc.scalar.copy(stage[1][:, 0, :], page[2][:])
+        for a in range(2):
+            nc.scalar.copy(
+                wr_bf[:, a, :, :].rearrange("p (c i) j -> p c j i", i=4),
+                wr_raw[:, a, :, :].rearrange("p j (c i) -> p c j i", i=4),
+            )
+        for t in range(3):
+            scatter(t)
+            for u in range(2):
+                round_plane("scalar", t, u)
         scatter(3)
-        nc.vector.tensor_copy(stage[1][:, 1, 0 : T // 2], page[3][:, 0 : T // 2])
-        nc.scalar.copy(stage[1][:, 1, T // 2 : T], page[3][:, T // 2 : T])
+        round_plane("vector", 3, 0)
+        round_plane("scalar", 3, 1)
         page_codes = tile("page_codes", [P, T], U32)
         page_sc = tile("page_sc", [P, T], U8)
 
@@ -196,21 +198,32 @@ def tile_list_lane_agent_update_kernel(
                 in_=page_bf[c][:].rearrange("p c t -> p (c t)"),
             )
 
-        weave_pair("vector", 1, 0)
-        weave_pair("vector", 1, 1)
-        weave_pair("scalar", 1, 2)
-        weave_pair("scalar", 1, 3)
-        for c in range(4):
-            quantise_page(c)
+        quantise_wa(0)
+        weave("vector", 0, 0, BANK)
+        weave("vector", 1, 0, BANK)
+        weave("scalar", 2, 0, BANK)
+        weave("scalar", 3, 0, BANK)
+        quantise_page(0)
+        quantise_page(1)
+        quantise_page(2)
+        quantise_wa(1)
+        quantise_page(3)
+        wr_codes = tile("wr_codes", [P, 2, N], U32, tag="bf3")
+        wr_sc = tile("wr_sc", [P, 2, N], U8)
+        nc.vector.quantize_mx(
+            out=wr_codes[:].rearrange("p a n -> p (a n)").bitcast(FP8X4),
+            scales=wr_sc[:].rearrange("p a n -> p (a n)"),
+            in_=wr_bf[:].rearrange("p a n j -> p (a n j)"),
+        )
 
         a_sb = []
-        a_tags = ["ring2", "ring3", "ring0", "ring1", "ring4"]
+        a_tags = ["ring0", "ring1", "ring4", "ring2", "ring3"]
 
         def project(s):
             a_sb.append(tile("a%d" % s, [P, T], F32, tag=a_tags[s % 5]))
             for c in range(4):
                 cols = slice(c * BANK, (c + 1) * BANK)
-                acc = psum.tile([P, BANK], F32, name="acc", tag="bank%d" % c)
+                acc = psum.tile([P, BANK], F32, name="acc", tag="bank%d" % ((4 * s + c) % 3))
                 nc.tensor.matmul_mx(
                     out=acc[:],
                     lhsT=wa_codes[:, P * s : P * (s + 1)].bitcast(FP8X4),
@@ -244,24 +257,6 @@ def tile_list_lane_agent_update_kernel(
                 in_=z_bf.rearrange("p c t -> p (c t)"),
             )
 
-        wr_bf = [tile("wr_bf%d" % a, [P, N, 4], BF16, tag=("bf3", "wa_codes")[a]) for a in range(2)]
-        wr_codes = tile("wr_codes", [P, 2, N], U32)
-        wr_sc = tile("wr_sc", [P, 2, N], U8)
-
-        def round_wr(engine, a):
-            copy_on(
-                engine,
-                wr_bf[a][:].rearrange("p (c i) j -> p c j i", i=4),
-                wr_raw[:, a, :, :].rearrange("p j (c i) -> p c j i", i=4),
-            )
-
-        def quantise_wr(a):
-            nc.vector.quantize_mx(
-                out=wr_codes[:, a, :].bitcast(FP8X4), scales=wr_sc[:, a, :],
-                in_=wr_bf[a][:].rearrange("p n j -> p (n j)"),
-            )
-
-        round_wr("vector", 0)
         z0 = tile("z0", [P, 4, S], F32, tag="zf0")
         for s in range(4):
             project(s)
@@ -270,7 +265,6 @@ def tile_list_lane_agent_update_kernel(
         round_z("vector", z0_bf[0][:], z0[:, :, 0:BANK])
         for s in range(4, 8):
             project(s)
-        round_wr("scalar", 1)
 
         pieces = [(0, 512), (512, 768), (768, 1024)]
         z1_tags = ["zf1", "gate7_0", "bf2"]
@@ -285,7 +279,7 @@ def tile_list_lane_agent_update_kernel(
 
         def round_piece(engine, n):
             j0, j1 = pieces[n]
-            z1_bf[n] = tile("z1_bf%d" % n, [P, j1 - j0, 4], BF16, tag="bf%d" % (2 + n))
+            z1_bf[n] = tile("z1_bf%d" % n, [P, j1 - j0, 4], BF16, tag=("bf2", "bf4", "bf5")[n])
             round_z(engine, z1_bf[n][:], z1[n][:])
 
         def finish(n):
@@ -312,12 +306,10 @@ def tile_list_lane_agent_update_kernel(
                 nc.sync.dma_start(out[rows, j0:j1], res[:])
 
         pick_piece(0)
-        quantise_wr(0)
         quantise_z(0, 0, BANK, z0_bf[0][:])
         round_piece("scalar", 0)
         round_z("scalar", z0_bf[1][:], z0[:, :, BANK:S])
         pick_piece(1)
-        quantise_wr(1)
         quantise_z(1, *pieces[0], z1_bf[0][:])
         finish(0)
         round_piece("scalar", 1)

@@ -51,7 +51,8 @@ def tile_list_lane_agent_update_kernel(
         for a in range(2):
             nc.sync.dma_start(wl_raw[:, a, :].bitcast(I32), wl_words[a].bitcast(I32))
         for q in range(4):
-            nc.sync.dma_start(tab_sc[32 * q : 32 * q + 8, :].bitcast(I32), tab_scales[:, 4 * q : 4 * q + 4, :].bitcast(I32))
+            nc.sync.dma_start(tab_sc[32 * q : 32 * q + 4, :].bitcast(I32), tab_scales[0, 4 * q : 4 * q + 4, :].bitcast(I32))
+        nc.sync.dma_start(tab_sc[4:20, :].bitcast(I32), tab_scales[1].bitcast(I32))
         tab = []
         for a in range(2):
             tab.append(tile("tab%d" % a, [P, T], I32))
@@ -74,7 +75,7 @@ def tile_list_lane_agent_update_kernel(
         v_sc0 = tile("v_sc0", [P, S], U8)
         nc.vector.tensor_copy(v_sc0[:], tab_sc[:].indirect(idx[:]))
         for q in range(4):
-            nc.scalar.dma_start(v_sc1[32 * q : 32 * q + 4, :].bitcast(I32), v_sc0[32 * q + 4 : 32 * q + 8, :].bitcast(I32))
+            nc.scalar.dma_start(v_sc1[32 * q : 32 * q + 4, :].bitcast(I32), v_sc0[4 + 4 * q : 8 + 4 * q, :].bitcast(I32))
         v_sc = [v_sc0, v_sc1]
         v = [tile("v%d" % a, [P, S], U32) for a in range(2)]
         nc.vector.tensor_copy(v[0][:], tab[0][:].bitcast(U32).indirect(idx[:]))
@@ -138,19 +139,20 @@ def tile_list_lane_agent_update_kernel(
 
         wa_codes = tile("wa_codes", [P, H], U32)
         wa_sc = tile("wa_sc", [P, H], U8)
-        wa_bf = [tile("wa_bf%d" % b, [P, 4 * BANK], BF16, tag=("wabf0", "ring2")[b]) for b in range(2)]
+        wa_bf = [tile("wa_bf%d" % b, [P, 4 * BANK], BF16, tag="wabf%d" % b) for b in range(2)]
 
         def round_wa(b):
-            nc.scalar.copy(
-                wa_bf[b][:].rearrange("p (t m j) -> p m j t", t=4, j=4),
-                wa_raw[b][:].rearrange("p j (m t) -> p m j t", t=4),
+            nc.gpsimd.tensor_scalar(
+                wa_bf[b][:].rearrange("p (t m j) -> p t m j", t=4, j=4),
+                wa_raw[b][:].rearrange("p j (m t) -> p t m j", t=4),
+                1.0, 0.0, ALU.mult, ALU.add,
             )
 
         def quantise_wa(b):
             cols = slice(b * BANK, (b + 1) * BANK)
             nc.vector.quantize_mx(out=wa_codes[:, cols].bitcast(FP8X4), scales=wa_sc[:, cols], in_=wa_bf[b][:])
 
-        stage = [tile("stage%d" % u, [P, 4, T // 2], BF16, tag=("ring3", "wr_raw")[u]) for u in range(2)]
+        stage = [tile("stage%d" % u, [P, 4, T // 2], BF16, tag="zf%d" % u) for u in range(2)]
         page_bf = [tile("page_bf%d" % c, [P, BANK, 4], BF16, tag="bf%d" % c) for c in range(4)]
 
         def scatter(t):
@@ -165,26 +167,28 @@ def tile_list_lane_agent_update_kernel(
         def round_plane(engine, t, u):
             copy_on(engine, stage[u][:, t, :], page[t][:, u * T // 2 : (u + 1) * T // 2])
 
-        def weave(engine, c, c0, c1):
+        def weave(engine, c, e):
             first = (c % 2) * BANK
             copy_on(
                 engine,
-                page_bf[c][:, c0:c1, :].rearrange("p (c i) t -> p c t i", i=4),
-                stage[c // 2][:, :, first + c0 : first + c1].rearrange("p t (c i) -> p c t i", i=4),
+                page_bf[c][:, :, 2 * e : 2 * e + 2],
+                stage[c // 2][:, 2 * e : 2 * e + 2, first : first + BANK].rearrange("p t c -> p c t"),
             )
 
         wr_bf = tile("wr_bf", [P, 2, N, 4], BF16, tag="wl_raw")
         round_wa(0)
         round_wa(1)
         for a in range(2):
-            nc.scalar.copy(
-                wr_bf[:, a, :, :].rearrange("p (c i) j -> p c j i", i=4),
-                wr_raw[:, a, :, :].rearrange("p j (c i) -> p c j i", i=4),
+            nc.gpsimd.tensor_scalar(
+                wr_bf[:, a, :, :], wr_raw[:, a, :, :].rearrange("p j c -> p c j"), 1.0, 0.0, ALU.mult, ALU.add
             )
         for t in range(3):
             scatter(t)
             for u in range(2):
                 round_plane("scalar", t, u)
+            if t == 1:
+                for c in range(4):
+                    weave("scalar", c, 0)
         scatter(3)
         round_plane("vector", 3, 0)
         round_plane("scalar", 3, 1)
@@ -199,15 +203,13 @@ def tile_list_lane_agent_update_kernel(
             )
 
         quantise_wa(0)
-        weave("vector", 0, 0, BANK)
-        weave("vector", 1, 0, BANK)
-        weave("scalar", 2, 0, BANK)
-        weave("scalar", 3, 0, BANK)
-        quantise_page(0)
-        quantise_page(1)
-        quantise_page(2)
+        weave("vector", 0, 1)
+        weave("vector", 1, 1)
+        weave("scalar", 2, 1)
+        weave("scalar", 3, 1)
+        for c in range(4):
+            quantise_page(c)
         quantise_wa(1)
-        quantise_page(3)
         wr_codes = tile("wr_codes", [P, 2, N], U32, tag="bf3")
         wr_sc = tile("wr_sc", [P, 2, N], U8)
         nc.vector.quantize_mx(
@@ -233,7 +235,7 @@ def tile_list_lane_agent_update_kernel(
                     start=True,
                     stop=True,
                 )
-                copy_on("vector" if (s, c) == (0, 3) else "scalar", a_sb[s][:, cols], acc[:])
+                nc.scalar.copy(a_sb[s][:, cols], acc[:])
 
         def pick(s, z_f32, j0, j1):
             g = gate[s][2][:] if j1 - j0 == S else gate[s][j0 // BANK][:, j0 % BANK : j0 % BANK + j1 - j0]

@@ -2,7 +2,7 @@ from contextlib import ExitStack
 
 import concourse.mybir as mybir
 
-K, K2, H, N, T, S = 1024, 512, 1024, 256, 2048, 1024
+H, N, T, S = 1024, 256, 2048, 1024
 FLOPS = 5368709120
 
 F32 = mybir.dt.float32
@@ -18,6 +18,8 @@ ALU = mybir.AluOpType
 
 P = 128
 BANK = 512
+PAGE_BANKS = 3
+PIECES = [(0, 512), (512, 768), (768, 1024)]
 
 
 def tile_list_lane_agent_update_kernel(
@@ -32,6 +34,15 @@ def tile_list_lane_agent_update_kernel(
 
         def tile(name, shape, dtype, tag=None):
             return keep.tile(shape, dtype, name=name, tag=tag or name, align_bytes=64)
+
+        def copy_on(engine, dst, src):
+            if engine == "vector":
+                nc.vector.tensor_copy(dst, src)
+            else:
+                nc.scalar.copy(dst, src)
+
+        def round_on_gpsimd(dst, src):
+            nc.gpsimd.tensor_scalar(dst, src, 1.0, 0.0, ALU.mult, ALU.add)
 
         idx = lists.tile([P, S // 16], U16, name="idx")
         idx2 = lists.tile([P, S // 16], U16, name="idx2")
@@ -53,18 +64,34 @@ def tile_list_lane_agent_update_kernel(
         for q in range(4):
             nc.sync.dma_start(tab_sc[32 * q : 32 * q + 4, :].bitcast(I32), tab_scales[0, 4 * q : 4 * q + 4, :].bitcast(I32))
         nc.sync.dma_start(tab_sc[4:20, :].bitcast(I32), tab_scales[1].bitcast(I32))
-        tab = []
-        for a in range(2):
-            tab.append(tile("tab%d" % a, [P, T], I32))
-            nc.sync.dma_start(tab[a][:], tab_words[a].rearrange("p n i -> p (n i)").bitcast(I32))
+
+        base_rows = base.rearrange("(p t) c -> t p c", t=4)
+        xs_rows = xs.rearrange("(p t) c -> t p c", t=4)
+        wa_rows = wa.rearrange("(p j) c -> p j c", j=4)
+        page = [tile("page%d" % t, [P, T], F32) for t in range(4)]
+        xs_sb = [tile("xs%d" % t, [P, S], F32, tag=("ring0", "ring1", "ring4", "wa_codes")[t]) for t in range(4)]
+        wa_raw = [tile("wa_raw%d" % b, [P, 4, BANK], F32, tag="ring%d" % (2 + b)) for b in range(2)]
+        wr_raw = tile("wr_raw", [P, 2, 4, N], F32)
+        tab = [tile("tab%d" % a, [P, T], I32) for a in range(2)]
+        bl_sb = tile("bl_sb", [P, 2, 4], F32)
+
+        halves = [slice(0, S // 2), slice(S // 2, S)]
+        nc.sync.dma_start(page[0][:], base_rows[0])
+        nc.sync.dma_start(idx2[:], offs2)
+        nc.sync.dma_start(xs_sb[0][:, halves[0]], xs_rows[0][:, halves[0]])
         for q in range(4):
             nc.sync.dma_start(
                 wl_sc_raw[32 * q : 32 * q + 4, :, :].bitcast(I32),
                 wl_scales[:, 4 * q : 4 * q + 4, :].rearrange("a r c -> r a c").bitcast(I32),
             )
-        nc.sync.dma_start(idx2[:], offs2)
-        bl_sb = tile("bl_sb", [P, 2, 4], F32)
+        for a in range(2):
+            nc.sync.dma_start(tab[a][:], tab_words[a].rearrange("p n i -> p (n i)").bitcast(I32))
         nc.sync.dma_start(bl_sb[:], bl.rearrange("(b p t) -> p b t", b=2, t=4))
+        nc.sync.dma_start(xs_sb[0][:, halves[1]], xs_rows[0][:, halves[1]])
+
+        def scatter(t, entries=slice(0, S)):
+            offsets = idx2[:, entries.start // 16 : entries.stop // 16]
+            nc.vector.tensor_copy(page[t][:].indirect(offsets), xs_sb[t][:, entries])
 
         wl_perm = tile("wl_perm", [P, 2, 2 * H], U8)
         for a in range(2):
@@ -74,31 +101,24 @@ def tile_list_lane_agent_update_kernel(
             )
         v_sc0 = tile("v_sc0", [P, S], U8)
         nc.vector.tensor_copy(v_sc0[:], tab_sc[:].indirect(idx[:]))
-        for q in range(4):
-            nc.scalar.dma_start(v_sc1[32 * q : 32 * q + 4, :].bitcast(I32), v_sc0[4 + 4 * q : 8 + 4 * q, :].bitcast(I32))
-        v_sc = [v_sc0, v_sc1]
-        v = [tile("v%d" % a, [P, S], U32) for a in range(2)]
-        nc.vector.tensor_copy(v[0][:], tab[0][:].bitcast(U32).indirect(idx[:]))
+        scatter(0, halves[0])
         wl_sc = tile("wl_sc", [P, 2, H], U8)
         nc.vector.tensor_copy(
             wl_sc[:].rearrange("p a (b t m) -> p (a b) t m", b=2, t=4),
             wl_sc_raw[:].rearrange("p a (b m t) -> p (a b) t m", b=2, t=4),
         )
-        nc.vector.tensor_copy(v[1][:], tab[1][:].bitcast(U32).indirect(idx[:]))
-
-        base_rows = base.rearrange("(p t) c -> t p c", t=4)
-        xs_rows = xs.rearrange("(p t) c -> t p c", t=4)
-        wa_rows = wa.rearrange("(p j) c -> p j c", j=4)
-        page = [tile("page%d" % t, [P, T], F32) for t in range(4)]
-        xs_sb = [tile("xs%d" % t, [P, S], F32, tag=("ring0", "ring1", "ring4", "wa_codes")[t]) for t in range(4)]
-        wa_raw = [tile("wa_raw%d" % b, [P, 4, BANK], F32, tag="ring%d" % (2 + b)) for b in range(2)]
-        wr_raw = tile("wr_raw", [P, 2, 4, N], F32, tag="wr_raw")
+        v = [tile("v%d" % a, [P, S], U32) for a in range(2)]
+        for a in range(2):
+            nc.vector.tensor_copy(v[a][:], tab[a][:].bitcast(U32).indirect(idx[:]))
+        scatter(0, halves[1])
+        for q in range(4):
+            nc.scalar.dma_start(v_sc1[32 * q : 32 * q + 4, :].bitcast(I32), v_sc0[4 + 4 * q : 8 + 4 * q, :].bitcast(I32))
+        v_sc = [v_sc0, v_sc1]
 
         def load_plane(t):
             nc.sync.dma_start(page[t][:], base_rows[t])
             nc.sync.dma_start(xs_sb[t][:], xs_rows[t])
 
-        load_plane(0)
         nc.sync.dma_start(wa_raw[0][:], wa_rows[:, :, 0:BANK])
         load_plane(1)
         nc.sync.dma_start(wa_raw[1][:], wa_rows[:, :, BANK : 2 * BANK])
@@ -117,10 +137,9 @@ def tile_list_lane_agent_update_kernel(
         with nc.allow_non_contiguous_dma(reason="one bias value for each partition"):
             nc.sync.dma_start(bo_sb[:], bo.rearrange("(h p) -> p h", p=P))
 
-        gate = [[tile("gate%d_%d" % (s, h), [P, BANK], F32) for h in range(2)] if s == 7 else None for s in range(8)]
-        for s in range(7):
-            whole = tile("gate%d" % s, [P, S], F32)
-            gate[s] = [whole[:, 0:BANK], whole[:, BANK:S], whole]
+        gate = [tile("gate%d" % s, [P, S], F32) for s in range(7)]
+        gate_half = [[whole[:, 0:BANK], whole[:, BANK:S]] for whole in gate]
+        gate_half.append([tile("gate7_%d" % h, [P, BANK], F32) for h in range(2)])
         for h in range(2):
             for s in range(8):
                 cols = slice(h * BANK, (h + 1) * BANK)
@@ -135,37 +154,17 @@ def tile_list_lane_agent_update_kernel(
                         start=(a == 0),
                         stop=(a == 1),
                     )
-                nc.scalar.activation(gate[s][h][:], acc[:], ACT.Sigmoid, bias=bl_sb[:, s // 4, s % 4 : s % 4 + 1])
+                nc.scalar.activation(gate_half[s][h][:], acc[:], ACT.Sigmoid, bias=bl_sb[:, s // 4, s % 4 : s % 4 + 1])
 
         wa_codes = tile("wa_codes", [P, H], U32)
         wa_sc = tile("wa_sc", [P, H], U8)
         wa_bf = [tile("wa_bf%d" % b, [P, 4 * BANK], BF16, tag="wabf%d" % b) for b in range(2)]
-
-        def round_wa(b):
-            nc.gpsimd.tensor_scalar(
-                wa_bf[b][:].rearrange("p (t m j) -> p t m j", t=4, j=4),
-                wa_raw[b][:].rearrange("p j (m t) -> p t m j", t=4),
-                1.0, 0.0, ALU.mult, ALU.add,
-            )
-
-        def quantise_wa(b):
-            cols = slice(b * BANK, (b + 1) * BANK)
-            nc.vector.quantize_mx(out=wa_codes[:, cols].bitcast(FP8X4), scales=wa_sc[:, cols], in_=wa_bf[b][:])
-
+        wr_bf = tile("wr_bf", [P, 2, N, 4], BF16, tag="wl_raw")
         stage = [tile("stage%d" % u, [P, 4, T // 2], BF16, tag="zf%d" % u) for u in range(2)]
         page_bf = [tile("page_bf%d" % c, [P, BANK, 4], BF16, tag="bf%d" % c) for c in range(4)]
 
-        def scatter(t):
-            nc.vector.tensor_copy(page[t][:].indirect(idx2[:]), xs_sb[t][:])
-
-        def copy_on(engine, dst, src):
-            if engine == "vector":
-                nc.vector.tensor_copy(dst, src)
-            else:
-                nc.scalar.copy(dst, src)
-
-        def round_plane(engine, t, u):
-            copy_on(engine, stage[u][:, t, :], page[t][:, u * T // 2 : (u + 1) * T // 2])
+        def plane_half(t, u):
+            return stage[u][:, t, :], page[t][:, u * T // 2 : (u + 1) * T // 2]
 
         def weave(engine, c, e):
             first = (c % 2) * BANK
@@ -175,40 +174,42 @@ def tile_list_lane_agent_update_kernel(
                 stage[c // 2][:, 2 * e : 2 * e + 2, first : first + BANK].rearrange("p t c -> p c t"),
             )
 
-        wr_bf = tile("wr_bf", [P, 2, N, 4], BF16, tag="wl_raw")
-        round_wa(0)
-        round_wa(1)
-        for a in range(2):
-            nc.gpsimd.tensor_scalar(
-                wr_bf[:, a, :, :], wr_raw[:, a, :, :].rearrange("p j c -> p c j"), 1.0, 0.0, ALU.mult, ALU.add
+        def quantise_wa(b):
+            cols = slice(b * BANK, (b + 1) * BANK)
+            nc.vector.quantize_mx(out=wa_codes[:, cols].bitcast(FP8X4), scales=wa_sc[:, cols], in_=wa_bf[b][:])
+
+        for u in range(2):
+            round_on_gpsimd(*plane_half(0, u))
+        for b in range(2):
+            round_on_gpsimd(
+                wa_bf[b][:].rearrange("p (t m j) -> p t m j", t=4, j=4),
+                wa_raw[b][:].rearrange("p j (m t) -> p t m j", t=4),
             )
-        for t in range(3):
-            scatter(t)
-            for u in range(2):
-                round_plane("scalar", t, u)
-            if t == 1:
-                for c in range(4):
-                    weave("scalar", c, 0)
+        for a in range(2):
+            round_on_gpsimd(wr_bf[:, a, :, :], wr_raw[:, a, :, :].rearrange("p j c -> p c j"))
+        scatter(1)
+        for u in range(2):
+            nc.scalar.copy(*plane_half(1, u))
+        for c in range(4):
+            weave("scalar", c, 0)
+        scatter(2)
+        for u in range(2):
+            nc.scalar.copy(*plane_half(2, u))
         scatter(3)
-        round_plane("vector", 3, 0)
-        round_plane("scalar", 3, 1)
+
+        nc.vector.tensor_copy(*plane_half(3, 0))
+        nc.scalar.copy(*plane_half(3, 1))
         page_codes = tile("page_codes", [P, T], U32)
         page_sc = tile("page_sc", [P, T], U8)
-
-        def quantise_page(c):
+        quantise_wa(0)
+        for c in range(4):
+            weave("vector" if c < 2 else "scalar", c, 1)
+        for c in range(4):
             cols = slice(c * BANK, (c + 1) * BANK)
             nc.vector.quantize_mx(
                 out=page_codes[:, cols].bitcast(FP8X4), scales=page_sc[:, cols],
                 in_=page_bf[c][:].rearrange("p c t -> p (c t)"),
             )
-
-        quantise_wa(0)
-        weave("vector", 0, 1)
-        weave("vector", 1, 1)
-        weave("scalar", 2, 1)
-        weave("scalar", 3, 1)
-        for c in range(4):
-            quantise_page(c)
         quantise_wa(1)
         wr_codes = tile("wr_codes", [P, 2, N], U32, tag="bf3")
         wr_sc = tile("wr_sc", [P, 2, N], U8)
@@ -222,10 +223,10 @@ def tile_list_lane_agent_update_kernel(
         a_tags = ["ring0", "ring1", "ring4", "ring2", "ring3"]
 
         def project(s):
-            a_sb.append(tile("a%d" % s, [P, T], F32, tag=a_tags[s % 5]))
+            a_sb.append(tile("a%d" % s, [P, T], F32, tag=a_tags[s % len(a_tags)]))
             for c in range(4):
                 cols = slice(c * BANK, (c + 1) * BANK)
-                acc = psum.tile([P, BANK], F32, name="acc", tag="bank%d" % ((4 * s + c) % 3))
+                acc = psum.tile([P, BANK], F32, name="acc", tag="bank%d" % ((4 * s + c) % PAGE_BANKS))
                 nc.tensor.matmul_mx(
                     out=acc[:],
                     lhsT=wa_codes[:, P * s : P * (s + 1)].bitcast(FP8X4),
@@ -237,10 +238,9 @@ def tile_list_lane_agent_update_kernel(
                 )
                 nc.scalar.copy(a_sb[s][:, cols], acc[:])
 
-        def pick(s, z_f32, j0, j1):
-            g = gate[s][2][:] if j1 - j0 == S else gate[s][j0 // BANK][:, j0 % BANK : j0 % BANK + j1 - j0]
+        def pick(s, z_f32, j0, j1, gate_cols):
             nc.vector.tensor_tensor(
-                z_f32[:, s % 4, :], a_sb[s][:].indirect(idx3[:, j0 // 16 : j1 // 16]), g, ALU.mult
+                z_f32[:, s % 4, :], a_sb[s][:].indirect(idx3[:, j0 // 16 : j1 // 16]), gate_cols, ALU.mult
             )
 
         z_codes = tile("z_codes", [P, 2, S], U32, tag="page_codes")
@@ -262,30 +262,29 @@ def tile_list_lane_agent_update_kernel(
         z0 = tile("z0", [P, 4, S], F32, tag="zf0")
         for s in range(4):
             project(s)
-            pick(s, z0, 0, S)
+            pick(s, z0, 0, S, gate[s][:])
         z0_bf = [tile("z0_bf%d" % h, [P, BANK, 4], BF16, tag="bf%d" % h) for h in range(2)]
         round_z("vector", z0_bf[0][:], z0[:, :, 0:BANK])
         for s in range(4, 8):
             project(s)
 
-        pieces = [(0, 512), (512, 768), (768, 1024)]
         z1_tags = ["zf1", "gate7_0", "bf2"]
         z1 = {}
         z1_bf = {}
 
         def pick_piece(n):
-            j0, j1 = pieces[n]
+            j0, j1 = PIECES[n]
             z1[n] = tile("z1_%d" % n, [P, 4, j1 - j0], F32, tag=z1_tags[n])
             for s in range(4, 8):
-                pick(s, z1[n], j0, j1)
+                pick(s, z1[n], j0, j1, gate_half[s][j0 // BANK][:, j0 % BANK : j0 % BANK + j1 - j0])
 
         def round_piece(engine, n):
-            j0, j1 = pieces[n]
+            j0, j1 = PIECES[n]
             z1_bf[n] = tile("z1_bf%d" % n, [P, j1 - j0, 4], BF16, tag=("bf2", "bf4", "bf5")[n])
             round_z(engine, z1_bf[n][:], z1[n][:])
 
         def finish(n):
-            j0, j1 = pieces[n]
+            j0, j1 = PIECES[n]
             for h in range(2):
                 rows = slice(h * P, (h + 1) * P)
                 acc = psum.tile([P, j1 - j0], F32, name="acc", tag="bank%d" % ((4 + 2 * n + h) % 8))
@@ -298,10 +297,10 @@ def tile_list_lane_agent_update_kernel(
                 for i, (w, w_sc, x, x_sc) in enumerate(passes):
                     nc.tensor.matmul_mx(
                         out=acc[:], lhsT=w.bitcast(FP8X4), lhsT_scale=w_sc, rhs=x.bitcast(FP8X4), rhs_scale=x_sc,
-                        start=(i == 0), stop=(i == 3),
+                        start=(i == 0), stop=(i == len(passes) - 1),
                     )
                 res = tile("res%d_%d" % (n, h), [P, j1 - j0], F32, tag="wabf%d" % h if n == 0 else None)
-                if n == 2 and h == 1:
+                if n == len(PIECES) - 1 and h == 1:
                     nc.vector.tensor_scalar(res[:], acc[:], bo_sb[:, h : h + 1], None, ALU.add)
                 else:
                     nc.scalar.activation(res[:], acc[:], ACT.Identity, bias=bo_sb[:, h : h + 1])
@@ -312,13 +311,13 @@ def tile_list_lane_agent_update_kernel(
         round_piece("scalar", 0)
         round_z("scalar", z0_bf[1][:], z0[:, :, BANK:S])
         pick_piece(1)
-        quantise_z(1, *pieces[0], z1_bf[0][:])
+        quantise_z(1, *PIECES[0], z1_bf[0][:])
         finish(0)
         round_piece("scalar", 1)
         pick_piece(2)
         quantise_z(0, BANK, S, z0_bf[1][:])
-        quantise_z(1, *pieces[1], z1_bf[1][:])
+        quantise_z(1, *PIECES[1], z1_bf[1][:])
         round_piece("vector", 2)
         finish(1)
-        quantise_z(1, *pieces[2], z1_bf[2][:])
+        quantise_z(1, *PIECES[2], z1_bf[2][:])
         finish(2)

@@ -35,35 +35,28 @@ def tile_list_lane_agent_update_kernel(
         def tile(name, shape, dtype, tag=None):
             return keep.tile(shape, dtype, name=name, tag=tag or name, align_bytes=64)
 
-        def copy_on(engine, dst, src):
+        def round_on(engine, dst, src):
             if engine == "vector":
                 nc.vector.tensor_copy(dst, src)
-            else:
+            elif engine == "scalar":
                 nc.scalar.copy(dst, src)
-
-        def round_on_gpsimd(dst, src):
-            nc.gpsimd.tensor_scalar(dst, src, 1.0, 0.0, ALU.mult, ALU.add)
+            else:
+                nc.gpsimd.tensor_scalar(dst, src, 1.0, 0.0, ALU.mult, ALU.add)
 
         idx = lists.tile([P, S // 16], U16, name="idx")
         idx2 = lists.tile([P, S // 16], U16, name="idx2")
         idx3 = lists.tile([P, S // 16], U16, name="idx3")
 
         tab_sc = tile("tab_sc", [P, T], U8)
-        wl_sc_raw = tile("wl_sc_raw", [P, 2, H], U8)
-        v_sc1 = tile("v_sc1", [P, S], U8)
+        wl_sc_raw = tile("wl_sc_raw", [P, 2, H], U8, tag="bf3")
+        v_sc = [tile("v_sc%d" % a, [P, S], U8) for a in range(2)]
         wo_sc = tile("wo_sc", [P, 2, N], U8)
-        nc.vector.memset(tab_sc[:].bitcast(I32), 0)
+        nc.vector.memset(tab_sc[32:64, :].bitcast(I32), 0)
+        nc.vector.memset(tab_sc[64:P, :].bitcast(I32), 0)
         nc.gpsimd.memset(wl_sc_raw[:].bitcast(I32), 0)
-        nc.vector.memset(v_sc1[:].bitcast(I32), 0)
-        nc.vector.memset(wo_sc[:].bitcast(I32), 0)
-
-        nc.sync.dma_start(idx[:], offs)
-        wl_raw = tile("wl_raw", [P, 2, 2 * H], U8)
         for a in range(2):
-            nc.sync.dma_start(wl_raw[:, a, :].bitcast(I32), wl_words[a].bitcast(I32))
-        for q in range(4):
-            nc.sync.dma_start(tab_sc[32 * q : 32 * q + 4, :].bitcast(I32), tab_scales[0, 4 * q : 4 * q + 4, :].bitcast(I32))
-        nc.sync.dma_start(tab_sc[4:20, :].bitcast(I32), tab_scales[1].bitcast(I32))
+            nc.vector.memset(v_sc[a][:].bitcast(I32), 0)
+        nc.vector.memset(wo_sc[:].bitcast(I32), 0)
 
         base_rows = base.rearrange("(p t) c -> t p c", t=4)
         xs_rows = xs.rearrange("(p t) c -> t p c", t=4)
@@ -74,54 +67,61 @@ def tile_list_lane_agent_update_kernel(
         wr_raw = tile("wr_raw", [P, 2, 4, N], F32)
         tab = [tile("tab%d" % a, [P, T], I32) for a in range(2)]
         bl_sb = tile("bl_sb", [P, 2, 4], F32)
-
+        wl_raw = tile("wl_raw", [P, 2, 2 * H], U8, tag="bf2")
         halves = [slice(0, S // 2), slice(S // 2, S)]
+
+        nc.sync.dma_start(idx[:], offs)
+        nc.sync.dma_start(tab_sc[0:32, :].bitcast(I32), tab_scales.rearrange("a q c -> (a q) c").bitcast(I32))
         nc.sync.dma_start(page[0][:], base_rows[0])
         nc.sync.dma_start(idx2[:], offs2)
         nc.sync.dma_start(xs_sb[0][:, halves[0]], xs_rows[0][:, halves[0]])
+        nc.sync.dma_start(tab[0][:], tab_words[0].rearrange("p n i -> p (n i)").bitcast(I32))
+        nc.sync.dma_start(wl_raw[:].bitcast(I32), wl_words.rearrange("a p c -> p a c").bitcast(I32))
+        nc.sync.dma_start(tab[1][:], tab_words[1].rearrange("p n i -> p (n i)").bitcast(I32))
         for q in range(4):
             nc.sync.dma_start(
                 wl_sc_raw[32 * q : 32 * q + 4, :, :].bitcast(I32),
                 wl_scales[:, 4 * q : 4 * q + 4, :].rearrange("a r c -> r a c").bitcast(I32),
             )
-        for a in range(2):
-            nc.sync.dma_start(tab[a][:], tab_words[a].rearrange("p n i -> p (n i)").bitcast(I32))
-        nc.sync.dma_start(bl_sb[:], bl.rearrange("(b p t) -> p b t", b=2, t=4))
         nc.sync.dma_start(xs_sb[0][:, halves[1]], xs_rows[0][:, halves[1]])
+        nc.sync.dma_start(bl_sb[:], bl.rearrange("(b p t) -> p b t", b=2, t=4))
 
         def scatter(t, entries=slice(0, S)):
             offsets = idx2[:, entries.start // 16 : entries.stop // 16]
             nc.vector.tensor_copy(page[t][:].indirect(offsets), xs_sb[t][:, entries])
 
-        wl_perm = tile("wl_perm", [P, 2, 2 * H], U8)
-        for a in range(2):
-            nc.vector.tensor_copy(
-                wl_perm[:, a, :].bitcast(U16).rearrange("p (b t m) -> p b t m", b=2, t=4),
-                wl_raw[:, a, :].bitcast(U16).rearrange("p (b m t) -> p b t m", b=2, t=4),
-            )
-        v_sc0 = tile("v_sc0", [P, S], U8)
-        nc.vector.tensor_copy(v_sc0[:], tab_sc[:].indirect(idx[:]))
+        v_sc_rows = tile("v_sc_rows", [P, S], U8)
+        nc.vector.tensor_copy(v_sc_rows[:], tab_sc[:].indirect(idx[:]))
         scatter(0, halves[0])
-        wl_sc = tile("wl_sc", [P, 2, H], U8)
-        nc.vector.tensor_copy(
-            wl_sc[:].rearrange("p a (b t m) -> p (a b) t m", b=2, t=4),
-            wl_sc_raw[:].rearrange("p a (b m t) -> p (a b) t m", b=2, t=4),
-        )
         v = [tile("v%d" % a, [P, S], U32) for a in range(2)]
         for a in range(2):
             nc.vector.tensor_copy(v[a][:], tab[a][:].bitcast(U32).indirect(idx[:]))
         scatter(0, halves[1])
-        for q in range(4):
-            nc.scalar.dma_start(v_sc1[32 * q : 32 * q + 4, :].bitcast(I32), v_sc0[4 + 4 * q : 8 + 4 * q, :].bitcast(I32))
-        v_sc = [v_sc0, v_sc1]
+        wl_perm = tile("wl_perm", [P, 2, 2 * H], U8, tag="bf0")
+        for a in range(2):
+            nc.gpsimd.tensor_copy(
+                wl_perm[:, a, :].bitcast(U16).rearrange("p (b t m) -> p b t m", b=2, t=4),
+                wl_raw[:, a, :].bitcast(U16).rearrange("p (b m t) -> p b t m", b=2, t=4),
+            )
+        wl_sc = tile("wl_sc", [P, 2, H], U8, tag="bf1")
+        nc.gpsimd.tensor_copy(
+            wl_sc[:].rearrange("p a (b t m) -> p (a b) t m", b=2, t=4),
+            wl_sc_raw[:].rearrange("p a (b m t) -> p (a b) t m", b=2, t=4),
+        )
+        for a in range(2):
+            for q in range(4):
+                first = 16 * a + 4 * q
+                nc.scalar.dma_start(
+                    v_sc[a][32 * q : 32 * q + 4, :].bitcast(I32), v_sc_rows[first : first + 4, :].bitcast(I32)
+                )
 
         def load_plane(t):
             nc.sync.dma_start(page[t][:], base_rows[t])
             nc.sync.dma_start(xs_sb[t][:], xs_rows[t])
 
-        nc.sync.dma_start(wa_raw[0][:], wa_rows[:, :, 0:BANK])
         load_plane(1)
-        nc.sync.dma_start(wa_raw[1][:], wa_rows[:, :, BANK : 2 * BANK])
+        for b in range(2):
+            nc.sync.dma_start(wa_raw[b][:], wa_rows[:, :, b * BANK : (b + 1) * BANK])
         load_plane(2)
         nc.sync.dma_start(wr_raw[:], wr.rearrange("(a p j) n -> p a j n", a=2, j=4))
         load_plane(3)
@@ -159,51 +159,44 @@ def tile_list_lane_agent_update_kernel(
         wa_codes = tile("wa_codes", [P, H], U32)
         wa_sc = tile("wa_sc", [P, H], U8)
         wa_bf = [tile("wa_bf%d" % b, [P, 4 * BANK], BF16, tag="wabf%d" % b) for b in range(2)]
-        wr_bf = tile("wr_bf", [P, 2, N, 4], BF16, tag="wl_raw")
-        stage = [tile("stage%d" % u, [P, 4, T // 2], BF16, tag="zf%d" % u) for u in range(2)]
+        wr_bf = tile("wr_bf", [P, 2, N, 4], BF16)
         page_bf = [tile("page_bf%d" % c, [P, BANK, 4], BF16, tag="bf%d" % c) for c in range(4)]
 
-        def plane_half(t, u):
-            return stage[u][:, t, :], page[t][:, u * T // 2 : (u + 1) * T // 2]
+        def weave(engine, t, c):
+            src = page[t][:, c * BANK : (c + 1) * BANK]
+            if t == 2:
+                round_on(engine, page_bf[c][:, :, 2:4], src.unsqueeze(2).to_broadcast([P, BANK, 2]))
+            else:
+                round_on(engine, page_bf[c][:, :, t], src)
 
-        def weave(engine, c, e):
-            first = (c % 2) * BANK
-            copy_on(
-                engine,
-                page_bf[c][:, :, 2 * e : 2 * e + 2],
-                stage[c // 2][:, 2 * e : 2 * e + 2, first : first + BANK].rearrange("p t c -> p c t"),
-            )
+        def weave_early(t):
+            for c in range(4):
+                weave("scalar" if c < 2 else "gpsimd", t, c)
 
         def quantise_wa(b):
             cols = slice(b * BANK, (b + 1) * BANK)
             nc.vector.quantize_mx(out=wa_codes[:, cols].bitcast(FP8X4), scales=wa_sc[:, cols], in_=wa_bf[b][:])
 
-        for u in range(2):
-            round_on_gpsimd(*plane_half(0, u))
+        weave_early(0)
+        scatter(1)
+        weave_early(1)
         for b in range(2):
-            round_on_gpsimd(
+            round_on(
+                "gpsimd",
                 wa_bf[b][:].rearrange("p (t m j) -> p t m j", t=4, j=4),
                 wa_raw[b][:].rearrange("p j (m t) -> p t m j", t=4),
             )
-        for a in range(2):
-            round_on_gpsimd(wr_bf[:, a, :, :], wr_raw[:, a, :, :].rearrange("p j c -> p c j"))
-        scatter(1)
-        for u in range(2):
-            nc.scalar.copy(*plane_half(1, u))
-        for c in range(4):
-            weave("scalar", c, 0)
         scatter(2)
-        for u in range(2):
-            nc.scalar.copy(*plane_half(2, u))
+        weave_early(2)
+        for a in range(2):
+            round_on(("gpsimd", "scalar")[a], wr_bf[:, a, :, :], wr_raw[:, a, :, :].rearrange("p j c -> p c j"))
         scatter(3)
 
-        nc.vector.tensor_copy(*plane_half(3, 0))
-        nc.scalar.copy(*plane_half(3, 1))
+        for c in range(4):
+            weave("vector" if c < 2 else "scalar", 3, c)
         page_codes = tile("page_codes", [P, T], U32)
         page_sc = tile("page_sc", [P, T], U8)
         quantise_wa(0)
-        for c in range(4):
-            weave("vector" if c < 2 else "scalar", c, 1)
         for c in range(4):
             cols = slice(c * BANK, (c + 1) * BANK)
             nc.vector.quantize_mx(
@@ -220,7 +213,7 @@ def tile_list_lane_agent_update_kernel(
         )
 
         a_sb = []
-        a_tags = ["ring0", "ring1", "ring4", "ring2", "ring3"]
+        a_tags = ["ring0", "ring1", "ring4", "ring2", "ring3", "page0", "page1", "page2"]
 
         def project(s):
             a_sb.append(tile("a%d" % s, [P, T], F32, tag=a_tags[s % len(a_tags)]))
@@ -247,7 +240,7 @@ def tile_list_lane_agent_update_kernel(
         z_sc = tile("z_sc", [P, 2, S], U8, tag="page_sc")
 
         def round_z(engine, z_bf, z_f32):
-            copy_on(
+            round_on(
                 engine,
                 z_bf.rearrange("p (c i) t -> p c t i", i=4),
                 z_f32.rearrange("p t (c i) -> p c t i", i=4),

@@ -63,7 +63,7 @@ def tile_list_lane_agent_update_kernel(
         wa_rows = wa.rearrange("(p j) c -> p j c", j=4)
         page = [tile("page%d" % t, [P, T], F32) for t in range(4)]
         xs_sb = [tile("xs%d" % t, [P, S], F32, tag=("ring0", "ring1", "ring4", "wa_codes")[t]) for t in range(4)]
-        wa_raw = [tile("wa_raw%d" % b, [P, 4, BANK], F32, tag="ring%d" % (2 + b)) for b in range(2)]
+        wa_raw = [tile("wa_raw%d" % b, [P, 4, BANK], F32) for b in range(2)]
         wr_raw = tile("wr_raw", [P, 2, 4, N], F32)
         tab = [tile("tab%d" % a, [P, T], I32) for a in range(2)]
         bl_sb = tile("bl_sb", [P, 2, 4], F32)
@@ -72,17 +72,17 @@ def tile_list_lane_agent_update_kernel(
 
         nc.sync.dma_start(idx[:], offs)
         nc.sync.dma_start(tab_sc[0:32, :].bitcast(I32), tab_scales.rearrange("a q c -> (a q) c").bitcast(I32))
+        nc.sync.dma_start(wl_raw[:].bitcast(I32), wl_words.rearrange("a p c -> p a c").bitcast(I32))
         nc.sync.dma_start(page[0][:], base_rows[0])
         nc.sync.dma_start(idx2[:], offs2)
         nc.sync.dma_start(xs_sb[0][:, halves[0]], xs_rows[0][:, halves[0]])
         nc.sync.dma_start(tab[0][:], tab_words[0].rearrange("p n i -> p (n i)").bitcast(I32))
-        nc.sync.dma_start(wl_raw[:].bitcast(I32), wl_words.rearrange("a p c -> p a c").bitcast(I32))
-        nc.sync.dma_start(tab[1][:], tab_words[1].rearrange("p n i -> p (n i)").bitcast(I32))
         for q in range(4):
             nc.sync.dma_start(
                 wl_sc_raw[32 * q : 32 * q + 4, :, :].bitcast(I32),
                 wl_scales[:, 4 * q : 4 * q + 4, :].rearrange("a r c -> r a c").bitcast(I32),
             )
+        nc.sync.dma_start(tab[1][:], tab_words[1].rearrange("p n i -> p (n i)").bitcast(I32))
         nc.sync.dma_start(xs_sb[0][:, halves[1]], xs_rows[0][:, halves[1]])
         nc.sync.dma_start(bl_sb[:], bl.rearrange("(b p t) -> p b t", b=2, t=4))
 
@@ -92,22 +92,22 @@ def tile_list_lane_agent_update_kernel(
 
         v_sc_rows = tile("v_sc_rows", [P, S], U8)
         nc.vector.tensor_copy(v_sc_rows[:], tab_sc[:].indirect(idx[:]))
+        wl_perm = [tile("wl_perm%d" % a, [P, 2 * H], U8, tag=("bf0", "wr_bf1")[a]) for a in range(2)]
+        for a in range(2):
+            nc.vector.tensor_copy(
+                wl_perm[a][:].bitcast(U16).rearrange("p (b t m) -> p b t m", b=2, t=4),
+                wl_raw[:, a, :].bitcast(U16).rearrange("p (b m t) -> p b t m", b=2, t=4),
+            )
+        wl_sc = tile("wl_sc", [P, 2, H], U8, tag="bf1")
+        nc.vector.tensor_copy(
+            wl_sc[:].rearrange("p a (b t m) -> p (a b) t m", b=2, t=4),
+            wl_sc_raw[:].rearrange("p a (b m t) -> p (a b) t m", b=2, t=4),
+        )
         scatter(0, halves[0])
         v = [tile("v%d" % a, [P, S], U32) for a in range(2)]
         for a in range(2):
             nc.vector.tensor_copy(v[a][:], tab[a][:].bitcast(U32).indirect(idx[:]))
         scatter(0, halves[1])
-        wl_perm = tile("wl_perm", [P, 2, 2 * H], U8, tag="bf0")
-        for a in range(2):
-            nc.gpsimd.tensor_copy(
-                wl_perm[:, a, :].bitcast(U16).rearrange("p (b t m) -> p b t m", b=2, t=4),
-                wl_raw[:, a, :].bitcast(U16).rearrange("p (b m t) -> p b t m", b=2, t=4),
-            )
-        wl_sc = tile("wl_sc", [P, 2, H], U8, tag="bf1")
-        nc.gpsimd.tensor_copy(
-            wl_sc[:].rearrange("p a (b t m) -> p (a b) t m", b=2, t=4),
-            wl_sc_raw[:].rearrange("p a (b m t) -> p (a b) t m", b=2, t=4),
-        )
         for a in range(2):
             for q in range(4):
                 first = 16 * a + 4 * q
@@ -119,9 +119,9 @@ def tile_list_lane_agent_update_kernel(
             nc.sync.dma_start(page[t][:], base_rows[t])
             nc.sync.dma_start(xs_sb[t][:], xs_rows[t])
 
+        nc.sync.dma_start(wa_raw[0][:], wa_rows[:, :, 0:BANK])
         load_plane(1)
-        for b in range(2):
-            nc.sync.dma_start(wa_raw[b][:], wa_rows[:, :, b * BANK : (b + 1) * BANK])
+        nc.sync.dma_start(wa_raw[1][:], wa_rows[:, :, BANK:H])
         load_plane(2)
         nc.sync.dma_start(wr_raw[:], wr.rearrange("(a p j) n -> p a j n", a=2, j=4))
         load_plane(3)
@@ -147,7 +147,7 @@ def tile_list_lane_agent_update_kernel(
                 for a in range(2):
                     nc.tensor.matmul_mx(
                         out=acc[:],
-                        lhsT=wl_perm[:, a, 2 * P * s : 2 * P * (s + 1)].bitcast(FP4X4),
+                        lhsT=wl_perm[a][:, 2 * P * s : 2 * P * (s + 1)].bitcast(FP4X4),
                         lhsT_scale=wl_sc[:, a, P * s : P * (s + 1)],
                         rhs=v[a][:, cols].bitcast(FP8X4),
                         rhs_scale=v_sc[a][:, cols],
@@ -159,7 +159,7 @@ def tile_list_lane_agent_update_kernel(
         wa_codes = tile("wa_codes", [P, H], U32)
         wa_sc = tile("wa_sc", [P, H], U8)
         wa_bf = [tile("wa_bf%d" % b, [P, 4 * BANK], BF16, tag="wabf%d" % b) for b in range(2)]
-        wr_bf = tile("wr_bf", [P, 2, N, 4], BF16)
+        wr_bf = [tile("wr_bf%d" % a, [P, N, 4], BF16) for a in range(2)]
         page_bf = [tile("page_bf%d" % c, [P, BANK, 4], BF16, tag="bf%d" % c) for c in range(4)]
 
         def weave(engine, t, c):
@@ -177,19 +177,19 @@ def tile_list_lane_agent_update_kernel(
             cols = slice(b * BANK, (b + 1) * BANK)
             nc.vector.quantize_mx(out=wa_codes[:, cols].bitcast(FP8X4), scales=wa_sc[:, cols], in_=wa_bf[b][:])
 
-        weave_early(0)
-        scatter(1)
-        weave_early(1)
         for b in range(2):
             round_on(
                 "gpsimd",
                 wa_bf[b][:].rearrange("p (t m j) -> p t m j", t=4, j=4),
                 wa_raw[b][:].rearrange("p j (m t) -> p t m j", t=4),
             )
+        weave_early(0)
+        scatter(1)
+        weave_early(1)
         scatter(2)
         weave_early(2)
         for a in range(2):
-            round_on(("gpsimd", "scalar")[a], wr_bf[:, a, :, :], wr_raw[:, a, :, :].rearrange("p j c -> p c j"))
+            round_on(("gpsimd", "scalar")[a], wr_bf[a][:], wr_raw[:, a, :, :].rearrange("p j c -> p c j"))
         scatter(3)
 
         for c in range(4):
@@ -206,14 +206,14 @@ def tile_list_lane_agent_update_kernel(
         quantise_wa(1)
         wr_codes = tile("wr_codes", [P, 2, N], U32, tag="bf3")
         wr_sc = tile("wr_sc", [P, 2, N], U8)
-        nc.vector.quantize_mx(
-            out=wr_codes[:].rearrange("p a n -> p (a n)").bitcast(FP8X4),
-            scales=wr_sc[:].rearrange("p a n -> p (a n)"),
-            in_=wr_bf[:].rearrange("p a n j -> p (a n j)"),
-        )
+        for a in range(2):
+            nc.vector.quantize_mx(
+                out=wr_codes[:, a, :].bitcast(FP8X4), scales=wr_sc[:, a, :],
+                in_=wr_bf[a][:].rearrange("p n j -> p (n j)"),
+            )
 
         a_sb = []
-        a_tags = ["ring0", "ring1", "ring4", "ring2", "ring3", "page0", "page1", "page2"]
+        a_tags = ["ring0", "ring1", "ring4", "tab0", "tab1", "page0", "page1", "page2"]
 
         def project(s):
             a_sb.append(tile("a%d" % s, [P, T], F32, tag=a_tags[s % len(a_tags)]))

@@ -48,7 +48,7 @@ def tile_list_lane_agent_update_kernel(
         idx3 = lists.tile([P, S // 16], U16, name="idx3")
 
         tab_sc = tile("tab_sc", [P, T], U8)
-        wl_sc_raw = tile("wl_sc_raw", [P, 2, H], U8, tag="bf3")
+        wl_sc_raw = tile("wl_sc_raw", [P, 2, H], U8)
         v_sc = [tile("v_sc%d" % a, [P, S], U8) for a in range(2)]
         wo_sc = tile("wo_sc", [P, 2, N], U8)
         nc.vector.memset(tab_sc[32:64, :].bitcast(I32), 0)
@@ -61,13 +61,14 @@ def tile_list_lane_agent_update_kernel(
         base_rows = base.rearrange("(p t) c -> t p c", t=4)
         xs_rows = xs.rearrange("(p t) c -> t p c", t=4)
         wa_rows = wa.rearrange("(p j) c -> p j c", j=4)
+        wr_rows = wr.rearrange("(a p j) n -> a p j n", a=2, j=4)
         page = [tile("page%d" % t, [P, T], F32) for t in range(4)]
         xs_sb = [tile("xs%d" % t, [P, S], F32, tag=("ring0", "ring1", "ring4", "wa_codes")[t]) for t in range(4)]
-        wa_raw = [tile("wa_raw%d" % b, [P, 4, BANK], F32) for b in range(2)]
-        wr_raw = tile("wr_raw", [P, 2, 4, N], F32)
+        wa_raw = [tile("wa_raw%d" % b, [P, 4, BANK], F32, tag=("wa_raw0", "bf2")[b]) for b in range(2)]
+        wr_raw = [tile("wr_raw%d" % a, [P, 4, N], F32, tag=("bf3", "wr_raw1")[a]) for a in range(2)]
         tab = [tile("tab%d" % a, [P, T], I32) for a in range(2)]
         bl_sb = tile("bl_sb", [P, 2, 4], F32)
-        wl_raw = tile("wl_raw", [P, 2, 2 * H], U8, tag="bf2")
+        wl_raw = tile("wl_raw", [P, 2, 2 * H], U8)
         halves = [slice(0, S // 2), slice(S // 2, S)]
 
         nc.sync.dma_start(idx[:], offs)
@@ -78,7 +79,7 @@ def tile_list_lane_agent_update_kernel(
         nc.sync.dma_start(xs_sb[0][:, halves[0]], xs_rows[0][:, halves[0]])
         nc.sync.dma_start(tab[0][:], tab_words[0].rearrange("p n i -> p (n i)").bitcast(I32))
         for q in range(4):
-            nc.sync.dma_start(
+            nc.gpsimd.dma_start(
                 wl_sc_raw[32 * q : 32 * q + 4, :, :].bitcast(I32),
                 wl_scales[:, 4 * q : 4 * q + 4, :].rearrange("a r c -> r a c").bitcast(I32),
             )
@@ -92,14 +93,14 @@ def tile_list_lane_agent_update_kernel(
 
         v_sc_rows = tile("v_sc_rows", [P, S], U8)
         nc.vector.tensor_copy(v_sc_rows[:], tab_sc[:].indirect(idx[:]))
-        wl_perm = [tile("wl_perm%d" % a, [P, 2 * H], U8, tag=("bf0", "wr_bf1")[a]) for a in range(2)]
+        wl_perm = [tile("wl_perm%d" % a, [P, 2 * H], U8, tag=("bf0", "wl_perm1")[a]) for a in range(2)]
         for a in range(2):
             nc.vector.tensor_copy(
                 wl_perm[a][:].bitcast(U16).rearrange("p (b t m) -> p b t m", b=2, t=4),
                 wl_raw[:, a, :].bitcast(U16).rearrange("p (b m t) -> p b t m", b=2, t=4),
             )
         wl_sc = tile("wl_sc", [P, 2, H], U8, tag="bf1")
-        nc.vector.tensor_copy(
+        nc.gpsimd.tensor_copy(
             wl_sc[:].rearrange("p a (b t m) -> p (a b) t m", b=2, t=4),
             wl_sc_raw[:].rearrange("p a (b m t) -> p (a b) t m", b=2, t=4),
         )
@@ -122,8 +123,9 @@ def tile_list_lane_agent_update_kernel(
         nc.sync.dma_start(wa_raw[0][:], wa_rows[:, :, 0:BANK])
         load_plane(1)
         nc.sync.dma_start(wa_raw[1][:], wa_rows[:, :, BANK:H])
+        nc.sync.dma_start(wr_raw[0][:], wr_rows[0])
         load_plane(2)
-        nc.sync.dma_start(wr_raw[:], wr.rearrange("(a p j) n -> p a j n", a=2, j=4))
+        nc.sync.dma_start(wr_raw[1][:], wr_rows[1])
         load_plane(3)
         nc.sync.dma_start(idx3[:], offs3)
         wo_sb = tile("wo_sb", [P, 2, N], I32)
@@ -159,7 +161,7 @@ def tile_list_lane_agent_update_kernel(
         wa_codes = tile("wa_codes", [P, H], U32)
         wa_sc = tile("wa_sc", [P, H], U8)
         wa_bf = [tile("wa_bf%d" % b, [P, 4 * BANK], BF16, tag="wabf%d" % b) for b in range(2)]
-        wr_bf = [tile("wr_bf%d" % a, [P, N, 4], BF16) for a in range(2)]
+        wr_bf = tile("wr_bf", [P, 2, N, 4], BF16)
         page_bf = [tile("page_bf%d" % c, [P, BANK, 4], BF16, tag="bf%d" % c) for c in range(4)]
 
         def weave(engine, t, c):
@@ -180,24 +182,24 @@ def tile_list_lane_agent_update_kernel(
         for b in range(2):
             round_on(
                 "gpsimd",
-                wa_bf[b][:].rearrange("p (t m j) -> p t m j", t=4, j=4),
-                wa_raw[b][:].rearrange("p j (m t) -> p t m j", t=4),
+                wa_bf[b][:].rearrange("p (t m j) -> p m t j", t=4, j=4),
+                wa_raw[b][:].rearrange("p j (m t) -> p m t j", t=4),
             )
+        round_on("gpsimd", wr_bf[:, 0, :, :], wr_raw[0][:].rearrange("p j c -> p c j"))
         weave_early(0)
         scatter(1)
         weave_early(1)
         scatter(2)
         weave_early(2)
-        for a in range(2):
-            round_on(("gpsimd", "scalar")[a], wr_bf[a][:], wr_raw[:, a, :, :].rearrange("p j c -> p c j"))
+        round_on("scalar", wr_bf[:, 1, :, :], wr_raw[1][:].rearrange("p j c -> p c j"))
         scatter(3)
 
-        for c in range(4):
-            weave("vector" if c < 2 else "scalar", 3, c)
         page_codes = tile("page_codes", [P, T], U32)
         page_sc = tile("page_sc", [P, T], U8)
-        quantise_wa(0)
         for c in range(4):
+            weave("vector" if c < 2 else "scalar", 3, c)
+            if c == 0:
+                quantise_wa(0)
             cols = slice(c * BANK, (c + 1) * BANK)
             nc.vector.quantize_mx(
                 out=page_codes[:, cols].bitcast(FP8X4), scales=page_sc[:, cols],
@@ -206,20 +208,22 @@ def tile_list_lane_agent_update_kernel(
         quantise_wa(1)
         wr_codes = tile("wr_codes", [P, 2, N], U32, tag="bf3")
         wr_sc = tile("wr_sc", [P, 2, N], U8)
-        for a in range(2):
-            nc.vector.quantize_mx(
-                out=wr_codes[:, a, :].bitcast(FP8X4), scales=wr_sc[:, a, :],
-                in_=wr_bf[a][:].rearrange("p n j -> p (n j)"),
-            )
+        nc.vector.quantize_mx(
+            out=wr_codes[:].rearrange("p a n -> p (a n)").bitcast(FP8X4),
+            scales=wr_sc[:].rearrange("p a n -> p (a n)"),
+            in_=wr_bf[:].rearrange("p a n j -> p (a n j)"),
+        )
 
-        a_sb = []
         a_tags = ["ring0", "ring1", "ring4", "tab0", "tab1", "page0", "page1", "page2"]
 
-        def project(s):
-            a_sb.append(tile("a%d" % s, [P, T], F32, tag=a_tags[s % len(a_tags)]))
-            for c in range(4):
+        a_sb = [tile("a%d" % s, [P, T], F32, tag=a_tags[s]) for s in range(8)]
+        done = []
+
+        def project(banks):
+            for s, c in banks:
                 cols = slice(c * BANK, (c + 1) * BANK)
-                acc = psum.tile([P, BANK], F32, name="acc", tag="bank%d" % ((4 * s + c) % PAGE_BANKS))
+                acc = psum.tile([P, BANK], F32, name="acc", tag="bank%d" % (len(done) % PAGE_BANKS))
+                done.append((s, c))
                 nc.tensor.matmul_mx(
                     out=acc[:],
                     lhsT=wa_codes[:, P * s : P * (s + 1)].bitcast(FP8X4),
@@ -253,13 +257,14 @@ def tile_list_lane_agent_update_kernel(
             )
 
         z0 = tile("z0", [P, 4, S], F32, tag="zf0")
+        project([(0, 0), (1, 0)])
         for s in range(4):
-            project(s)
+            project([(s, c) for c in range(4) if (s, c) not in done])
             pick(s, z0, 0, S, gate[s][:])
         z0_bf = [tile("z0_bf%d" % h, [P, BANK, 4], BF16, tag="bf%d" % h) for h in range(2)]
         round_z("vector", z0_bf[0][:], z0[:, :, 0:BANK])
         for s in range(4, 8):
-            project(s)
+            project([(s, c) for c in range(4)])
 
         z1_tags = ["zf1", "gate7_0", "bf2"]
         z1 = {}

@@ -65,10 +65,10 @@ def tile_list_lane_agent_update_kernel(
         page = [tile("page%d" % t, [P, T], F32) for t in range(4)]
         xs_sb = [tile("xs%d" % t, [P, S], F32, tag=("ring0", "ring1", "ring4", "wa_codes")[t]) for t in range(4)]
         wa_raw = [tile("wa_raw%d" % b, [P, 4, BANK], F32, tag=("wa_raw0", "bf2")[b]) for b in range(2)]
-        wr_raw = [tile("wr_raw%d" % a, [P, 4, N], F32, tag=("bf3", "wr_raw1")[a]) for a in range(2)]
+        wr_raw = [tile("wr_raw%d" % a, [P, 4, N], F32) for a in range(2)]
         tab = [tile("tab%d" % a, [P, T], I32) for a in range(2)]
         bl_sb = tile("bl_sb", [P, 2, 4], F32)
-        wl_raw = tile("wl_raw", [P, 2, 2 * H], U8)
+        wl_raw = tile("wl_raw", [P, 2, 2 * H], U8, tag="bf1")
         halves = [slice(0, S // 2), slice(S // 2, S)]
 
         nc.sync.dma_start(idx[:], offs)
@@ -93,12 +93,11 @@ def tile_list_lane_agent_update_kernel(
 
         v_sc_rows = tile("v_sc_rows", [P, S], U8)
         nc.vector.tensor_copy(v_sc_rows[:], tab_sc[:].indirect(idx[:]))
-        wl_perm = [tile("wl_perm%d" % a, [P, 2 * H], U8, tag=("bf0", "wl_perm1")[a]) for a in range(2)]
-        for a in range(2):
-            nc.vector.tensor_copy(
-                wl_perm[a][:].bitcast(U16).rearrange("p (b t m) -> p b t m", b=2, t=4),
-                wl_raw[:, a, :].bitcast(U16).rearrange("p (b m t) -> p b t m", b=2, t=4),
-            )
+        wl_perm = tile("wl_perm", [P, 2, 2 * H], U8, tag="bf0")
+        nc.vector.tensor_copy(
+            wl_perm[:].bitcast(U16).rearrange("p a (b t m) -> p (a b) t m", b=2, t=4),
+            wl_raw[:].bitcast(U16).rearrange("p a (b m t) -> p (a b) t m", b=2, t=4),
+        )
         wl_sc = tile("wl_sc", [P, 2, H], U8, tag="bf1")
         nc.gpsimd.tensor_copy(
             wl_sc[:].rearrange("p a (b t m) -> p (a b) t m", b=2, t=4),
@@ -123,9 +122,9 @@ def tile_list_lane_agent_update_kernel(
         nc.sync.dma_start(wa_raw[0][:], wa_rows[:, :, 0:BANK])
         load_plane(1)
         nc.sync.dma_start(wa_raw[1][:], wa_rows[:, :, BANK:H])
-        nc.sync.dma_start(wr_raw[0][:], wr_rows[0])
         load_plane(2)
-        nc.sync.dma_start(wr_raw[1][:], wr_rows[1])
+        for a in range(2):
+            nc.sync.dma_start(wr_raw[a][:], wr_rows[a])
         load_plane(3)
         nc.sync.dma_start(idx3[:], offs3)
         wo_sb = tile("wo_sb", [P, 2, N], I32)
@@ -149,7 +148,7 @@ def tile_list_lane_agent_update_kernel(
                 for a in range(2):
                     nc.tensor.matmul_mx(
                         out=acc[:],
-                        lhsT=wl_perm[a][:, 2 * P * s : 2 * P * (s + 1)].bitcast(FP4X4),
+                        lhsT=wl_perm[:, a, 2 * P * s : 2 * P * (s + 1)].bitcast(FP4X4),
                         lhsT_scale=wl_sc[:, a, P * s : P * (s + 1)],
                         rhs=v[a][:, cols].bitcast(FP8X4),
                         rhs_scale=v_sc[a][:, cols],
@@ -160,9 +159,11 @@ def tile_list_lane_agent_update_kernel(
 
         wa_codes = tile("wa_codes", [P, H], U32)
         wa_sc = tile("wa_sc", [P, H], U8)
-        wa_bf = [tile("wa_bf%d" % b, [P, 4 * BANK], BF16, tag="wabf%d" % b) for b in range(2)]
+        wa_bf = [tile("wa_bf%d" % b, [P, 4 * BANK], BF16, tag=("tab1", "wabf1")[b]) for b in range(2)]
         wr_bf = tile("wr_bf", [P, 2, N, 4], BF16)
-        page_bf = [tile("page_bf%d" % c, [P, BANK, 4], BF16, tag="bf%d" % c) for c in range(4)]
+        page_bf = [tile("page_bf%d" % c, [P, BANK, 4], BF16, tag="bf%d" % c) for c in range(2)]
+        right_bf = tile("right_bf", [P, 2 * BANK, 4], BF16, tag="bf2")
+        page_bf.extend([right_bf[:, 0:BANK, :], right_bf[:, BANK : 2 * BANK, :]])
 
         def weave(engine, t, c):
             src = page[t][:, c * BANK : (c + 1) * BANK]
@@ -185,13 +186,13 @@ def tile_list_lane_agent_update_kernel(
                 wa_bf[b][:].rearrange("p (t m j) -> p m t j", t=4, j=4),
                 wa_raw[b][:].rearrange("p j (m t) -> p m t j", t=4),
             )
-        round_on("gpsimd", wr_bf[:, 0, :, :], wr_raw[0][:].rearrange("p j c -> p c j"))
         weave_early(0)
         scatter(1)
         weave_early(1)
         scatter(2)
         weave_early(2)
-        round_on("scalar", wr_bf[:, 1, :, :], wr_raw[1][:].rearrange("p j c -> p c j"))
+        for a in range(2):
+            round_on(("gpsimd", "scalar")[a], wr_bf[:, a, :, :], wr_raw[a][:].rearrange("p j c -> p c j"))
         scatter(3)
 
         page_codes = tile("page_codes", [P, T], U32)
@@ -206,7 +207,7 @@ def tile_list_lane_agent_update_kernel(
                 in_=page_bf[c][:].rearrange("p c t -> p (c t)"),
             )
         quantise_wa(1)
-        wr_codes = tile("wr_codes", [P, 2, N], U32, tag="bf3")
+        wr_codes = tile("wr_codes", [P, 2, N], U32, tag="page3")
         wr_sc = tile("wr_sc", [P, 2, N], U8)
         nc.vector.quantize_mx(
             out=wr_codes[:].rearrange("p a n -> p (a n)").bitcast(FP8X4),

@@ -64,19 +64,19 @@ def tile_list_lane_agent_update_kernel(
         wr_rows = wr.rearrange("(a p j) n -> a p j n", a=2, j=4)
         page = [tile("page%d" % t, [P, T], F32) for t in range(4)]
         xs_sb = [tile("xs%d" % t, [P, S], F32, tag=("ring0", "ring1", "ring4", "wa_codes")[t]) for t in range(4)]
-        wa_raw = [tile("wa_raw%d" % b, [P, 4, BANK], F32, tag=("wa_raw0", "bf2")[b]) for b in range(2)]
-        wr_raw = [tile("wr_raw%d" % a, [P, 4, N], F32) for a in range(2)]
+        wa_raw = [tile("wa_raw%d" % b, [P, 4, BANK], F32, tag="wa_raw%d" % b) for b in range(2)]
+        wr_raw = [tile("wr_raw%d" % a, [P, 4, N], F32, tag=("stage0", "wr_raw1")[a]) for a in range(2)]
         tab = [tile("tab%d" % a, [P, T], I32) for a in range(2)]
         bl_sb = tile("bl_sb", [P, 2, 4], F32)
-        wl_raw = tile("wl_raw", [P, 2, 2 * H], U8, tag="bf1")
+        wl_raw = tile("wl_raw", [P, 2, 2 * H], U8)
         halves = [slice(0, S // 2), slice(S // 2, S)]
 
         nc.sync.dma_start(idx[:], offs)
         nc.sync.dma_start(tab_sc[0:32, :].bitcast(I32), tab_scales.rearrange("a q c -> (a q) c").bitcast(I32))
-        nc.sync.dma_start(wl_raw[:].bitcast(I32), wl_words.rearrange("a p c -> p a c").bitcast(I32))
         nc.sync.dma_start(page[0][:], base_rows[0])
         nc.sync.dma_start(idx2[:], offs2)
         nc.sync.dma_start(xs_sb[0][:, halves[0]], xs_rows[0][:, halves[0]])
+        nc.sync.dma_start(wl_raw[:].bitcast(I32), wl_words.rearrange("a p c -> p a c").bitcast(I32))
         nc.sync.dma_start(tab[0][:], tab_words[0].rearrange("p n i -> p (n i)").bitcast(I32))
         for q in range(4):
             nc.gpsimd.dma_start(
@@ -93,12 +93,12 @@ def tile_list_lane_agent_update_kernel(
 
         v_sc_rows = tile("v_sc_rows", [P, S], U8)
         nc.vector.tensor_copy(v_sc_rows[:], tab_sc[:].indirect(idx[:]))
-        wl_perm = tile("wl_perm", [P, 2, 2 * H], U8, tag="bf0")
-        nc.vector.tensor_copy(
+        wl_perm = tile("wl_perm", [P, 2, 2 * H], U8, tag="stage1")
+        nc.gpsimd.tensor_copy(
             wl_perm[:].bitcast(U16).rearrange("p a (b t m) -> p (a b) t m", b=2, t=4),
             wl_raw[:].bitcast(U16).rearrange("p a (b m t) -> p (a b) t m", b=2, t=4),
         )
-        wl_sc = tile("wl_sc", [P, 2, H], U8, tag="bf1")
+        wl_sc = tile("wl_sc", [P, 2, H], U8)
         nc.gpsimd.tensor_copy(
             wl_sc[:].rearrange("p a (b t m) -> p (a b) t m", b=2, t=4),
             wl_sc_raw[:].rearrange("p a (b m t) -> p (a b) t m", b=2, t=4),
@@ -122,9 +122,9 @@ def tile_list_lane_agent_update_kernel(
         nc.sync.dma_start(wa_raw[0][:], wa_rows[:, :, 0:BANK])
         load_plane(1)
         nc.sync.dma_start(wa_raw[1][:], wa_rows[:, :, BANK:H])
+        nc.sync.dma_start(wr_raw[0][:], wr_rows[0])
         load_plane(2)
-        for a in range(2):
-            nc.sync.dma_start(wr_raw[a][:], wr_rows[a])
+        nc.sync.dma_start(wr_raw[1][:], wr_rows[1])
         load_plane(3)
         nc.sync.dma_start(idx3[:], offs3)
         wo_sb = tile("wo_sb", [P, 2, N], I32)
@@ -157,28 +157,30 @@ def tile_list_lane_agent_update_kernel(
                     )
                 nc.scalar.activation(gate_half[s][h][:], acc[:], ACT.Sigmoid, bias=bl_sb[:, s // 4, s % 4 : s % 4 + 1])
 
-        wa_codes = tile("wa_codes", [P, H], U32)
+        wa_codes = [tile("wa_codes", [P, BANK], U32)]
         wa_sc = tile("wa_sc", [P, H], U8)
-        wa_bf = [tile("wa_bf%d" % b, [P, 4 * BANK], BF16, tag=("tab1", "wabf1")[b]) for b in range(2)]
-        wr_bf = tile("wr_bf", [P, 2, N, 4], BF16)
-        page_bf = [tile("page_bf%d" % c, [P, BANK, 4], BF16, tag="bf%d" % c) for c in range(2)]
-        right_bf = tile("right_bf", [P, 2 * BANK, 4], BF16, tag="bf2")
-        page_bf.extend([right_bf[:, 0:BANK, :], right_bf[:, BANK : 2 * BANK, :]])
+        wa_bf = [tile("wa_bf%d" % b, [P, 4 * BANK], BF16, tag="wabf%d" % b) for b in range(2)]
+        wr_bf = [tile("wr_bf%d" % a, [P, N, 4], BF16) for a in range(2)]
+        stage = [tile("stage%d" % u, [P, 2 + u, T // 2], BF16, tag="stage%d" % u) for u in range(2)]
+        page_bf = [tile("page_bf%d" % c, [P, BANK, 4], BF16, tag="bf%d" % c) for c in range(4)]
 
-        def weave(engine, t, c):
-            src = page[t][:, c * BANK : (c + 1) * BANK]
-            if t == 2:
-                round_on(engine, page_bf[c][:, :, 2:4], src.unsqueeze(2).to_broadcast([P, BANK, 2]))
-            else:
-                round_on(engine, page_bf[c][:, :, t], src)
+        def round_plane(t, u):
+            round_on(("gpsimd", "scalar")[u], stage[u][:, t, :], page[t][:, u * T // 2 : (u + 1) * T // 2])
 
-        def weave_early(t):
-            for c in range(4):
-                weave("scalar" if c < 2 else "gpsimd", t, c)
+        def weave_stage(c):
+            u = c // 2
+            first = (c % 2) * BANK
+            round_on(
+                ("gpsimd", "scalar")[u], page_bf[c][:, :, 0 : 2 + u],
+                stage[u][:, :, first : first + BANK].rearrange("p t c -> p c t"),
+            )
+
+        def page_cols(t, c):
+            return page[t][:, c * BANK : (c + 1) * BANK]
 
         def quantise_wa(b):
             cols = slice(b * BANK, (b + 1) * BANK)
-            nc.vector.quantize_mx(out=wa_codes[:, cols].bitcast(FP8X4), scales=wa_sc[:, cols], in_=wa_bf[b][:])
+            nc.vector.quantize_mx(out=wa_codes[b][:].bitcast(FP8X4), scales=wa_sc[:, cols], in_=wa_bf[b][:])
 
         for b in range(2):
             round_on(
@@ -186,19 +188,27 @@ def tile_list_lane_agent_update_kernel(
                 wa_bf[b][:].rearrange("p (t m j) -> p m t j", t=4, j=4),
                 wa_raw[b][:].rearrange("p j (m t) -> p m t j", t=4),
             )
-        weave_early(0)
-        scatter(1)
-        weave_early(1)
-        scatter(2)
-        weave_early(2)
         for a in range(2):
-            round_on(("gpsimd", "scalar")[a], wr_bf[:, a, :, :], wr_raw[a][:].rearrange("p j c -> p c j"))
+            round_on("gpsimd", wr_bf[a][:], wr_raw[a][:].rearrange("p j c -> p c j"))
+        for u in range(2):
+            round_plane(0, u)
+        scatter(1)
+        for u in range(2):
+            round_plane(1, u)
+        for c in range(2):
+            weave_stage(c)
+        scatter(2)
+        for c in range(2):
+            round_on("gpsimd", page_bf[c][:, :, 2:4], page_cols(2, c).unsqueeze(2).to_broadcast([P, BANK, 2]))
+        round_plane(2, 1)
+        for c in range(2, 4):
+            weave_stage(c)
         scatter(3)
 
         page_codes = tile("page_codes", [P, T], U32)
         page_sc = tile("page_sc", [P, T], U8)
         for c in range(4):
-            weave("vector" if c < 2 else "scalar", 3, c)
+            round_on("vector" if c < 2 else "scalar", page_bf[c][:, :, 3], page_cols(3, c))
             if c == 0:
                 quantise_wa(0)
             cols = slice(c * BANK, (c + 1) * BANK)
@@ -206,14 +216,16 @@ def tile_list_lane_agent_update_kernel(
                 out=page_codes[:, cols].bitcast(FP8X4), scales=page_sc[:, cols],
                 in_=page_bf[c][:].rearrange("p c t -> p (c t)"),
             )
+        late_codes = tile("late_codes", [P, 2, BANK], U32, tag="bf3")
+        wa_codes.append(late_codes[:, 0, :])
         quantise_wa(1)
-        wr_codes = tile("wr_codes", [P, 2, N], U32, tag="page3")
+        wr_codes = late_codes[:, 1, :].rearrange("p (a n) -> p a n", a=2)
         wr_sc = tile("wr_sc", [P, 2, N], U8)
-        nc.vector.quantize_mx(
-            out=wr_codes[:].rearrange("p a n -> p (a n)").bitcast(FP8X4),
-            scales=wr_sc[:].rearrange("p a n -> p (a n)"),
-            in_=wr_bf[:].rearrange("p a n j -> p (a n j)"),
-        )
+        for a in range(2):
+            nc.vector.quantize_mx(
+                out=wr_codes[:, a, :].bitcast(FP8X4), scales=wr_sc[:, a, :],
+                in_=wr_bf[a][:].rearrange("p n j -> p (n j)"),
+            )
 
         a_tags = ["ring0", "ring1", "ring4", "tab0", "tab1", "page0", "page1", "page2"]
 
@@ -227,7 +239,7 @@ def tile_list_lane_agent_update_kernel(
                 done.append((s, c))
                 nc.tensor.matmul_mx(
                     out=acc[:],
-                    lhsT=wa_codes[:, P * s : P * (s + 1)].bitcast(FP8X4),
+                    lhsT=wa_codes[s // 4][:, P * (s % 4) : P * (s % 4 + 1)].bitcast(FP8X4),
                     lhsT_scale=wa_sc[:, P * s : P * (s + 1)],
                     rhs=page_codes[:, cols].bitcast(FP8X4),
                     rhs_scale=page_sc[:, cols],
@@ -286,11 +298,11 @@ def tile_list_lane_agent_update_kernel(
             j0, j1 = PIECES[n]
             for h in range(2):
                 rows = slice(h * P, (h + 1) * P)
-                acc = psum.tile([P, j1 - j0], F32, name="acc", tag="bank%d" % ((4 + 2 * n + h) % 8))
+                acc = psum.tile([P, j1 - j0], F32, name="acc", tag="bank%d" % ((PAGE_BANKS + 2 * n + h) % 8))
                 passes = [
-                    (wo_sb[:, 0, rows], wo_sc[:, 0, rows], z_codes[:, 0, j0:j1], z_sc[:, 0, j0:j1]),
                     (wr_codes[:, 0, rows], wr_sc[:, 0, rows], v[0][:, j0:j1], v_sc[0][:, j0:j1]),
                     (wr_codes[:, 1, rows], wr_sc[:, 1, rows], v[1][:, j0:j1], v_sc[1][:, j0:j1]),
+                    (wo_sb[:, 0, rows], wo_sc[:, 0, rows], z_codes[:, 0, j0:j1], z_sc[:, 0, j0:j1]),
                     (wo_sb[:, 1, rows], wo_sc[:, 1, rows], z_codes[:, 1, j0:j1], z_sc[:, 1, j0:j1]),
                 ]
                 for i, (w, w_sc, x, x_sc) in enumerate(passes):
@@ -307,16 +319,17 @@ def tile_list_lane_agent_update_kernel(
 
         pick_piece(0)
         quantise_z(0, 0, BANK, z0_bf[0][:])
+        round_z("scalar", z0_bf[1][:, 0 : BANK // 2, :], z0[:, :, slice(*PIECES[1])])
         round_piece("scalar", 0)
-        round_z("scalar", z0_bf[1][:], z0[:, :, BANK:S])
+        round_z("scalar", z0_bf[1][:, BANK // 2 : BANK, :], z0[:, :, slice(*PIECES[2])])
         pick_piece(1)
         quantise_z(1, *PIECES[0], z1_bf[0][:])
         finish(0)
         round_piece("scalar", 1)
         pick_piece(2)
         quantise_z(0, BANK, S, z0_bf[1][:])
-        quantise_z(1, *PIECES[1], z1_bf[1][:])
         round_piece("vector", 2)
+        quantise_z(1, *PIECES[1], z1_bf[1][:])
         finish(1)
         quantise_z(1, *PIECES[2], z1_bf[2][:])
         finish(2)

@@ -138,9 +138,7 @@ def tile_list_lane_agent_update_kernel(
         with nc.allow_non_contiguous_dma(reason="one bias value for each partition"):
             nc.sync.dma_start(bo_sb[:], bo.rearrange("(h p) -> p h", p=P))
 
-        gate = [tile("gate%d" % s, [P, S], F32) for s in range(7)]
-        gate_half = [[whole[:, 0:BANK], whole[:, BANK:S]] for whole in gate]
-        gate_half.append([tile("gate7_%d" % h, [P, BANK], F32) for h in range(2)])
+        gate = [tile("gate%d" % s, [P, S], F32) for s in range(8)]
         for h in range(2):
             for s in range(8):
                 cols = slice(h * BANK, (h + 1) * BANK)
@@ -155,7 +153,7 @@ def tile_list_lane_agent_update_kernel(
                         start=(a == 0),
                         stop=(a == 1),
                     )
-                nc.scalar.activation(gate_half[s][h][:], acc[:], ACT.Sigmoid, bias=bl_sb[:, s // 4, s % 4 : s % 4 + 1])
+                nc.scalar.activation(gate[s][:, cols], acc[:], ACT.Sigmoid, bias=bl_sb[:, s // 4, s % 4 : s % 4 + 1])
 
         wa_codes = [tile("wa_codes", [P, BANK], U32)]
         wa_sc = tile("wa_sc", [P, H], U8)
@@ -248,88 +246,78 @@ def tile_list_lane_agent_update_kernel(
                 )
                 nc.scalar.copy(a_sb[s][:, cols], acc[:])
 
-        def pick(s, z_f32, j0, j1, gate_cols):
+        def pick(s, j0, j1):
             nc.vector.tensor_tensor(
-                z_f32[:, s % 4, :], a_sb[s][:].indirect(idx3[:, j0 // 16 : j1 // 16]), gate_cols, ALU.mult
+                z_f32[s // 4][:, s % 4, j0:j1], a_sb[s][:].indirect(idx3[:, j0 // 16 : j1 // 16]),
+                gate[s][:, j0:j1], ALU.mult,
             )
 
         z_codes = tile("z_codes", [P, 2, S], U32, tag="page_codes")
         z_sc = tile("z_sc", [P, 2, S], U8, tag="page_sc")
 
-        def round_z(engine, z_bf, z_f32):
+        z_f32 = [tile("z%d" % b, [P, 4, S], F32, tag=("zf0", "wa_raw0")[b]) for b in range(2)]
+
+        def round_z(engine, b, n):
+            j0, j1 = PIECES[n]
             round_on(
                 engine,
-                z_bf.rearrange("p (c i) t -> p c t i", i=4),
-                z_f32.rearrange("p t (c i) -> p c t i", i=4),
+                z_bf[b, n].rearrange("p (c i) t -> p c t i", i=4),
+                z_f32[b][:, :, j0:j1].rearrange("p t (c i) -> p c t i", i=4),
             )
 
-        def quantise_z(b, j0, j1, z_bf):
+        def quantise_z(b, n):
+            j0, j1 = PIECES[n]
             nc.vector.quantize_mx(
                 out=z_codes[:, b, j0:j1].bitcast(FP8X4), scales=z_sc[:, b, j0:j1],
-                in_=z_bf.rearrange("p c t -> p (c t)"),
+                in_=z_bf[b, n].rearrange("p c t -> p (c t)"),
             )
 
-        z0 = tile("z0", [P, 4, S], F32, tag="zf0")
-        project([(0, 0), (1, 0)])
-        for s in range(4):
-            project([(s, c) for c in range(4) if (s, c) not in done])
-            pick(s, z0, 0, S, gate[s][:])
-        z0_bf = [tile("z0_bf%d" % h, [P, BANK, 4], BF16, tag="bf%d" % h) for h in range(2)]
-        round_z("vector", z0_bf[0][:], z0[:, :, 0:BANK])
-        for s in range(4, 8):
-            project([(s, c) for c in range(4)])
-
-        z1_tags = ["zf1", "gate7_0", "bf2"]
-        z1 = {}
-        z1_bf = {}
-
-        def pick_piece(n):
-            j0, j1 = PIECES[n]
-            z1[n] = tile("z1_%d" % n, [P, 4, j1 - j0], F32, tag=z1_tags[n])
-            for s in range(4, 8):
-                pick(s, z1[n], j0, j1, gate_half[s][j0 // BANK][:, j0 % BANK : j0 % BANK + j1 - j0])
-
-        def round_piece(engine, n):
-            j0, j1 = PIECES[n]
-            z1_bf[n] = tile("z1_bf%d" % n, [P, j1 - j0, 4], BF16, tag=("bf2", "bf4", "bf5")[n])
-            round_z(engine, z1_bf[n][:], z1[n][:])
+        results = {}
 
         def finish(n):
             j0, j1 = PIECES[n]
+            results[n] = tile("res%d" % n, [P, 2, j1 - j0], F32, tag=("res0", "bf2", "res2")[n])
             for h in range(2):
                 rows = slice(h * P, (h + 1) * P)
                 acc = psum.tile([P, j1 - j0], F32, name="acc", tag="bank%d" % ((PAGE_BANKS + 2 * n + h) % 8))
-                passes = [
-                    (wr_codes[:, 0, rows], wr_sc[:, 0, rows], v[0][:, j0:j1], v_sc[0][:, j0:j1]),
-                    (wr_codes[:, 1, rows], wr_sc[:, 1, rows], v[1][:, j0:j1], v_sc[1][:, j0:j1]),
-                    (wo_sb[:, 0, rows], wo_sc[:, 0, rows], z_codes[:, 0, j0:j1], z_sc[:, 0, j0:j1]),
-                    (wo_sb[:, 1, rows], wo_sc[:, 1, rows], z_codes[:, 1, j0:j1], z_sc[:, 1, j0:j1]),
+                passes = [(wr_codes[:, a, rows], wr_sc[:, a, rows], v[a][:, j0:j1], v_sc[a][:, j0:j1]) for a in range(2)]
+                passes = passes + [
+                    (wo_sb[:, b, rows], wo_sc[:, b, rows], z_codes[:, b, j0:j1], z_sc[:, b, j0:j1])
+                    for b in (0, 1)
                 ]
                 for i, (w, w_sc, x, x_sc) in enumerate(passes):
                     nc.tensor.matmul_mx(
                         out=acc[:], lhsT=w.bitcast(FP8X4), lhsT_scale=w_sc, rhs=x.bitcast(FP8X4), rhs_scale=x_sc,
                         start=(i == 0), stop=(i == len(passes) - 1),
                     )
-                res = tile("res%d_%d" % (n, h), [P, j1 - j0], F32, tag="wabf%d" % h if n == 0 else None)
-                if n == len(PIECES) - 1 and h == 1:
-                    nc.vector.tensor_scalar(res[:], acc[:], bo_sb[:, h : h + 1], None, ALU.add)
+                res = results[n][:, h, :]
+                if n > 0 and h == 1:
+                    nc.vector.tensor_scalar(res, acc[:], bo_sb[:, h : h + 1], None, ALU.add)
                 else:
-                    nc.scalar.activation(res[:], acc[:], ACT.Identity, bias=bo_sb[:, h : h + 1])
-                nc.sync.dma_start(out[rows, j0:j1], res[:])
+                    nc.scalar.activation(res, acc[:], ACT.Identity, bias=bo_sb[:, h : h + 1])
+                nc.sync.dma_start(out[rows, j0:j1], res)
 
-        pick_piece(0)
-        quantise_z(0, 0, BANK, z0_bf[0][:])
-        round_z("scalar", z0_bf[1][:, 0 : BANK // 2, :], z0[:, :, slice(*PIECES[1])])
-        round_piece("scalar", 0)
-        round_z("scalar", z0_bf[1][:, BANK // 2 : BANK, :], z0[:, :, slice(*PIECES[2])])
-        pick_piece(1)
-        quantise_z(1, *PIECES[0], z1_bf[0][:])
+        project([(0, 0), (1, 0)])
+        for s in range(8):
+            project([(s, c) for c in range(4) if (s, c) not in done])
+            if s < 7:
+                pick(s, 0, S)
+        for piece in PIECES:
+            pick(7, *piece)
+        wide = [tile("z_wide%d" % b, [P, BANK, 4], BF16, tag=("bf0", "bf2")[b]) for b in range(2)]
+        short0 = tile("z_short0", [P, BANK, 4], BF16, tag="bf1")
+        z_bf = {(0, 0): wide[0][:], (1, 0): wide[1][:], (0, 1): short0[:, 0:256, :], (0, 2): short0[:, 256:BANK, :]}
+        for b, n in ((0, 0), (0, 1), (1, 0), (0, 2)):
+            round_z("scalar", b, n)
+        for b, n in ((0, 0), (0, 1), (1, 0)):
+            quantise_z(b, n)
         finish(0)
-        round_piece("scalar", 1)
-        pick_piece(2)
-        quantise_z(0, BANK, S, z0_bf[1][:])
-        round_piece("vector", 2)
-        quantise_z(1, *PIECES[1], z1_bf[1][:])
+        short1 = tile("z_short1", [P, BANK, 4], BF16, tag="bf2")
+        z_bf[1, 1] = short1[:, 0:256, :]
+        z_bf[1, 2] = short1[:, 256:BANK, :]
+        for n in (1, 2):
+            round_z("vector", 1, n)
+        for b, n in ((1, 1), (0, 2), (1, 2)):
+            quantise_z(b, n)
         finish(1)
-        quantise_z(1, *PIECES[2], z1_bf[2][:])
         finish(2)

@@ -19,7 +19,9 @@ ALU = mybir.AluOpType
 P = 128
 BANK = 512
 PAGE_BANKS = 3
+CHUNK_ORDER = (0, 2, 1, 3)
 PIECES = [(0, 512), (512, 768), (768, 1024)]
+SUMS = [(0, 512), (512, 768), (768, 896), (896, 1024)]
 
 
 def tile_list_lane_agent_update_kernel(
@@ -156,9 +158,10 @@ def tile_list_lane_agent_update_kernel(
                 nc.scalar.activation(gate[s][:, cols], acc[:], ACT.Sigmoid, bias=bl_sb[:, s // 4, s % 4 : s % 4 + 1])
 
         wa_codes = [tile("wa_codes", [P, BANK], U32)]
-        wa_sc = tile("wa_sc", [P, H], U8)
-        wa_bf = [tile("wa_bf%d" % b, [P, 4 * BANK], BF16, tag="wabf%d" % b) for b in range(2)]
-        wr_bf = [tile("wr_bf%d" % a, [P, N, 4], BF16) for a in range(2)]
+        wa_sc = tile("wa_sc", [P, H + 2 * N], U8)
+        late_bf = tile("late_bf", [P, 2, 4 * BANK], BF16)
+        wa_bf = [tile("wa_bf0", [P, 4 * BANK], BF16), late_bf[:, 0, :]]
+        wr_bf = late_bf[:, 1, :].rearrange("p (a n j) -> p a n j", a=2, j=4)
         stage = [tile("stage%d" % u, [P, 2 + u, T // 2], BF16, tag="stage%d" % u) for u in range(2)]
         page_bf = [tile("page_bf%d" % c, [P, BANK, 4], BF16, tag="bf%d" % c) for c in range(4)]
 
@@ -183,11 +186,11 @@ def tile_list_lane_agent_update_kernel(
         for b in range(2):
             round_on(
                 "gpsimd",
-                wa_bf[b][:].rearrange("p (t m j) -> p m t j", t=4, j=4),
+                wa_bf[b][:, :].rearrange("p (t m j) -> p m t j", t=4, j=4),
                 wa_raw[b][:].rearrange("p j (m t) -> p m t j", t=4),
             )
         for a in range(2):
-            round_on("gpsimd", wr_bf[a][:], wr_raw[a][:].rearrange("p j c -> p c j"))
+            round_on("gpsimd", wr_bf[:, a], wr_raw[a][:].rearrange("p j c -> p c j"))
         for u in range(2):
             round_plane(0, u)
         scatter(1)
@@ -205,25 +208,28 @@ def tile_list_lane_agent_update_kernel(
 
         page_codes = tile("page_codes", [P, T], U32)
         page_sc = tile("page_sc", [P, T], U8)
-        for c in range(4):
-            round_on("vector" if c < 2 else "scalar", page_bf[c][:, :, 3], page_cols(3, c))
-            if c == 0:
-                quantise_wa(0)
+        def quantise_page(c):
             cols = slice(c * BANK, (c + 1) * BANK)
             nc.vector.quantize_mx(
                 out=page_codes[:, cols].bitcast(FP8X4), scales=page_sc[:, cols],
                 in_=page_bf[c][:].rearrange("p c t -> p (c t)"),
             )
-        late_codes = tile("late_codes", [P, 2, BANK], U32, tag="bf3")
+
+        for c in range(4):
+            round_on("vector" if c < 2 else "scalar", page_bf[c][:, :, 3], page_cols(3, c))
+            if c == 0:
+                quantise_wa(0)
+                quantise_page(0)
+        for c in CHUNK_ORDER[1:]:
+            quantise_page(c)
+        late_codes = tile("late_codes", [P, 2, BANK], U32, tag="bf1")
         wa_codes.append(late_codes[:, 0, :])
-        quantise_wa(1)
         wr_codes = late_codes[:, 1, :].rearrange("p (a n) -> p a n", a=2)
-        wr_sc = tile("wr_sc", [P, 2, N], U8)
-        for a in range(2):
-            nc.vector.quantize_mx(
-                out=wr_codes[:, a, :].bitcast(FP8X4), scales=wr_sc[:, a, :],
-                in_=wr_bf[a][:].rearrange("p n j -> p (n j)"),
-            )
+        wr_sc = wa_sc[:, H : H + 2 * N].rearrange("p (a n) -> p a n", a=2)
+        nc.vector.quantize_mx(
+            out=late_codes[:].rearrange("p b c -> p (b c)").bitcast(FP8X4), scales=wa_sc[:, BANK : H + 2 * N],
+            in_=late_bf[:].rearrange("p b c -> p (b c)"),
+        )
 
         a_tags = ["ring0", "ring1", "ring4", "tab0", "tab1", "page0", "page1", "page2"]
 
@@ -257,12 +263,13 @@ def tile_list_lane_agent_update_kernel(
 
         z_f32 = [tile("z%d" % b, [P, 4, S], F32, tag=("zf0", "wa_raw0")[b]) for b in range(2)]
 
-        def round_z(engine, b, n):
+        def round_z(engine, b, n, first=0, last=None):
             j0, j1 = PIECES[n]
+            last = j1 - j0 if last is None else last
             round_on(
                 engine,
-                z_bf[b, n].rearrange("p (c i) t -> p c t i", i=4),
-                z_f32[b][:, :, j0:j1].rearrange("p t (c i) -> p c t i", i=4),
+                z_bf[b, n][:, first:last, :].rearrange("p (c i) t -> p c t i", i=4),
+                z_f32[b][:, :, j0 + first : j0 + last].rearrange("p t (c i) -> p c t i", i=4),
             )
 
         def quantise_z(b, n):
@@ -275,8 +282,8 @@ def tile_list_lane_agent_update_kernel(
         results = {}
 
         def finish(n):
-            j0, j1 = PIECES[n]
-            results[n] = tile("res%d" % n, [P, 2, j1 - j0], F32, tag=("res0", "bf2", "res2")[n])
+            j0, j1 = SUMS[n]
+            results[n] = tile("res%d" % n, [P, 2, j1 - j0], F32, tag=("res0", "res1", "bf2", "res3")[n])
             for h in range(2):
                 rows = slice(h * P, (h + 1) * P)
                 acc = psum.tile([P, j1 - j0], F32, name="acc", tag="bank%d" % ((PAGE_BANKS + 2 * n + h) % 8))
@@ -291,7 +298,7 @@ def tile_list_lane_agent_update_kernel(
                         start=(i == 0), stop=(i == len(passes) - 1),
                     )
                 res = results[n][:, h, :]
-                if n > 0 and h == 1:
+                if n > 1 and h == 1:
                     nc.vector.tensor_scalar(res, acc[:], bo_sb[:, h : h + 1], None, ALU.add)
                 else:
                     nc.scalar.activation(res, acc[:], ACT.Identity, bias=bo_sb[:, h : h + 1])
@@ -299,11 +306,11 @@ def tile_list_lane_agent_update_kernel(
 
         project([(0, 0), (1, 0)])
         for s in range(8):
-            project([(s, c) for c in range(4) if (s, c) not in done])
+            project([(s, c) for c in CHUNK_ORDER if (s, c) not in done])
             if s < 7:
                 pick(s, 0, S)
-        for piece in PIECES:
-            pick(7, *piece)
+        for h in range(2):
+            pick(7, h * BANK, (h + 1) * BANK)
         wide = [tile("z_wide%d" % b, [P, BANK, 4], BF16, tag=("bf0", "bf2")[b]) for b in range(2)]
         short0 = tile("z_short0", [P, BANK, 4], BF16, tag="bf1")
         z_bf = {(0, 0): wide[0][:], (1, 0): wide[1][:], (0, 1): short0[:, 0:256, :], (0, 2): short0[:, 256:BANK, :]}
@@ -311,13 +318,18 @@ def tile_list_lane_agent_update_kernel(
             round_z("scalar", b, n)
         for b, n in ((0, 0), (0, 1), (1, 0)):
             quantise_z(b, n)
-        finish(0)
         short1 = tile("z_short1", [P, BANK, 4], BF16, tag="bf2")
         z_bf[1, 1] = short1[:, 0:256, :]
         z_bf[1, 2] = short1[:, 256:BANK, :]
-        for n in (1, 2):
-            round_z("vector", 1, n)
-        for b, n in ((1, 1), (0, 2), (1, 2)):
+        round_z("vector", 1, 1)
+        round_z("vector", 1, 2)
+        finish(0)
+        for b, n in ((1, 1), (0, 2)):
             quantise_z(b, n)
-        finish(1)
-        finish(2)
+        for j0, j1 in SUMS[2:]:
+            nc.vector.quantize_mx(
+                out=z_codes[:, 1, j0:j1].bitcast(FP8X4), scales=z_sc[:, 1, j0:j1],
+                in_=short1[:, j0 - BANK : j1 - BANK, :].rearrange("p c t -> p (c t)"),
+            )
+        for n in range(1, 4):
+            finish(n)

@@ -19,6 +19,7 @@ ALU = mybir.AluOpType
 P = 128
 BANK = 512
 PAGE_BANKS = 3
+GATE_BANKS = 4
 CHUNK_ORDER = (0, 2, 1, 3)
 PIECES = [(0, 512), (512, 768), (768, 1024)]
 SUMS = [(0, 512), (512, 768), (768, 896), (896, 1024)]
@@ -67,18 +68,19 @@ def tile_list_lane_agent_update_kernel(
         page = [tile("page%d" % t, [P, T], F32) for t in range(4)]
         xs_sb = [tile("xs%d" % t, [P, S], F32, tag=("ring0", "ring1", "ring4", "wa_codes")[t]) for t in range(4)]
         wa_raw = [tile("wa_raw%d" % b, [P, 4, BANK], F32, tag="wa_raw%d" % b) for b in range(2)]
-        wr_raw = [tile("wr_raw%d" % a, [P, 4, N], F32, tag=("stage0", "wr_raw1")[a]) for a in range(2)]
+        wr_first = [tile("wr_first%d" % u, [P, 4, N // 2], F32, tag="bf%d" % u) for u in range(2)]
+        wr_second = tile("wr_second", [P, 4, N], F32)
         tab = [tile("tab%d" % a, [P, T], I32) for a in range(2)]
         bl_sb = tile("bl_sb", [P, 2, 4], F32)
         wl_raw = tile("wl_raw", [P, 2, 2 * H], U8)
-        halves = [slice(0, S // 2), slice(S // 2, S)]
+        parts = [slice(0, S // 4), slice(S // 4, S)]
 
         nc.sync.dma_start(idx[:], offs)
         nc.sync.dma_start(tab_sc[0:32, :].bitcast(I32), tab_scales.rearrange("a q c -> (a q) c").bitcast(I32))
         nc.sync.dma_start(page[0][:], base_rows[0])
         nc.sync.dma_start(idx2[:], offs2)
-        nc.sync.dma_start(xs_sb[0][:, halves[0]], xs_rows[0][:, halves[0]])
-        nc.sync.dma_start(wl_raw[:].bitcast(I32), wl_words.rearrange("a p c -> p a c").bitcast(I32))
+        for part in parts:
+            nc.sync.dma_start(xs_sb[0][:, part], xs_rows[0][:, part])
         nc.sync.dma_start(tab[0][:], tab_words[0].rearrange("p n i -> p (n i)").bitcast(I32))
         for q in range(4):
             nc.gpsimd.dma_start(
@@ -86,7 +88,7 @@ def tile_list_lane_agent_update_kernel(
                 wl_scales[:, 4 * q : 4 * q + 4, :].rearrange("a r c -> r a c").bitcast(I32),
             )
         nc.sync.dma_start(tab[1][:], tab_words[1].rearrange("p n i -> p (n i)").bitcast(I32))
-        nc.sync.dma_start(xs_sb[0][:, halves[1]], xs_rows[0][:, halves[1]])
+        nc.sync.dma_start(wl_raw[:].bitcast(I32), wl_words.rearrange("a p c -> p a c").bitcast(I32))
         nc.sync.dma_start(bl_sb[:], bl.rearrange("(b p t) -> p b t", b=2, t=4))
 
         def scatter(t, entries=slice(0, S)):
@@ -95,21 +97,22 @@ def tile_list_lane_agent_update_kernel(
 
         v_sc_rows = tile("v_sc_rows", [P, S], U8)
         nc.vector.tensor_copy(v_sc_rows[:], tab_sc[:].indirect(idx[:]))
-        wl_perm = tile("wl_perm", [P, 2, 2 * H], U8, tag="stage1")
-        nc.gpsimd.tensor_copy(
-            wl_perm[:].bitcast(U16).rearrange("p a (b t m) -> p (a b) t m", b=2, t=4),
-            wl_raw[:].bitcast(U16).rearrange("p a (b m t) -> p (a b) t m", b=2, t=4),
-        )
         wl_sc = tile("wl_sc", [P, 2, H], U8)
         nc.gpsimd.tensor_copy(
             wl_sc[:].rearrange("p a (b t m) -> p (a b) t m", b=2, t=4),
             wl_sc_raw[:].rearrange("p a (b m t) -> p (a b) t m", b=2, t=4),
         )
-        scatter(0, halves[0])
+        wl_perm = [tile("wl_perm%d" % a, [P, 2 * H], U8, tag="stage%d" % (2 + a)) for a in range(2)]
+        for a in range(2):
+            nc.gpsimd.tensor_copy(
+                wl_perm[a][:].bitcast(U16).rearrange("p (b t m) -> p b t m", b=2, t=4),
+                wl_raw[:, a, :].bitcast(U16).rearrange("p (b m t) -> p b t m", b=2, t=4),
+            )
+        for part in parts:
+            scatter(0, part)
         v = [tile("v%d" % a, [P, S], U32) for a in range(2)]
         for a in range(2):
             nc.vector.tensor_copy(v[a][:], tab[a][:].bitcast(U32).indirect(idx[:]))
-        scatter(0, halves[1])
         for a in range(2):
             for q in range(4):
                 first = 16 * a + 4 * q
@@ -121,12 +124,13 @@ def tile_list_lane_agent_update_kernel(
             nc.sync.dma_start(page[t][:], base_rows[t])
             nc.sync.dma_start(xs_sb[t][:], xs_rows[t])
 
-        nc.sync.dma_start(wa_raw[0][:], wa_rows[:, :, 0:BANK])
         load_plane(1)
-        nc.sync.dma_start(wa_raw[1][:], wa_rows[:, :, BANK:H])
-        nc.sync.dma_start(wr_raw[0][:], wr_rows[0])
+        for b in range(2):
+            nc.sync.dma_start(wa_raw[b][:], wa_rows[:, :, b * BANK : (b + 1) * BANK])
         load_plane(2)
-        nc.sync.dma_start(wr_raw[1][:], wr_rows[1])
+        for u in range(2):
+            nc.sync.dma_start(wr_first[u][:], wr_rows[0][:, :, u * P : (u + 1) * P])
+        nc.sync.dma_start(wr_second[:], wr_rows[1])
         load_plane(3)
         nc.sync.dma_start(idx3[:], offs3)
         wo_sb = tile("wo_sb", [P, 2, N], I32)
@@ -144,11 +148,11 @@ def tile_list_lane_agent_update_kernel(
         for h in range(2):
             for s in range(8):
                 cols = slice(h * BANK, (h + 1) * BANK)
-                acc = psum.tile([P, BANK], F32, name="acc", tag="bank%d" % s)
+                acc = psum.tile([P, BANK], F32, name="acc", tag="bank%d" % (s % GATE_BANKS))
                 for a in range(2):
                     nc.tensor.matmul_mx(
                         out=acc[:],
-                        lhsT=wl_perm[:, a, 2 * P * s : 2 * P * (s + 1)].bitcast(FP4X4),
+                        lhsT=wl_perm[a][:, 2 * P * s : 2 * P * (s + 1)].bitcast(FP4X4),
                         lhsT_scale=wl_sc[:, a, P * s : P * (s + 1)],
                         rhs=v[a][:, cols].bitcast(FP8X4),
                         rhs_scale=v_sc[a][:, cols],
@@ -162,18 +166,18 @@ def tile_list_lane_agent_update_kernel(
         late_bf = tile("late_bf", [P, 2, 4 * BANK], BF16)
         wa_bf = [tile("wa_bf0", [P, 4 * BANK], BF16), late_bf[:, 0, :]]
         wr_bf = late_bf[:, 1, :].rearrange("p (a n j) -> p a n j", a=2, j=4)
-        stage = [tile("stage%d" % u, [P, 2 + u, T // 2], BF16, tag="stage%d" % u) for u in range(2)]
-        page_bf = [tile("page_bf%d" % c, [P, BANK, 4], BF16, tag="bf%d" % c) for c in range(4)]
+        stage_left = tile("stage_left", [P, 2, 2 * BANK], BF16, tag="wa_raw1")
+        stage = [stage_left[:, :, 0:BANK], stage_left[:, :, BANK : 2 * BANK]]
+        stage = stage + [tile("stage%d" % c, [P, 3, BANK], BF16)[:] for c in (2, 3)]
+        page_bf = [tile("page_bf%d" % c, [P, BANK, 4], BF16, tag="bf%d" % c)[:] for c in range(4)]
 
-        def round_plane(t, u):
-            round_on(("gpsimd", "scalar")[u], stage[u][:, t, :], page[t][:, u * T // 2 : (u + 1) * T // 2])
+        def stage_chunk(t, c):
+            round_on("gpsimd" if c < 2 else "scalar", stage[c][:, t, :], page[t][:, c * BANK : (c + 1) * BANK])
 
         def weave_stage(c):
-            u = c // 2
-            first = (c % 2) * BANK
+            planes = 2 if c < 2 else 3
             round_on(
-                ("gpsimd", "scalar")[u], page_bf[c][:, :, 0 : 2 + u],
-                stage[u][:, :, first : first + BANK].rearrange("p t c -> p c t"),
+                "gpsimd" if c < 2 else "scalar", page_bf[c][:, :, 0:planes], stage[c].rearrange("p t c -> p c t")
             )
 
         def page_cols(t, c):
@@ -189,30 +193,34 @@ def tile_list_lane_agent_update_kernel(
                 wa_bf[b][:, :].rearrange("p (t m j) -> p m t j", t=4, j=4),
                 wa_raw[b][:].rearrange("p j (m t) -> p m t j", t=4),
             )
-        for a in range(2):
-            round_on("gpsimd", wr_bf[:, a], wr_raw[a][:].rearrange("p j c -> p c j"))
-        for u in range(2):
-            round_plane(0, u)
+        round_on("gpsimd", stage_left[:, 0, :], page[0][:, 0 : 2 * BANK])
+        for c in (2, 3):
+            stage_chunk(0, c)
         scatter(1)
+        for c in range(4):
+            stage_chunk(1, c)
         for u in range(2):
-            round_plane(1, u)
+            round_on("gpsimd", wr_bf[:, 0, u * P : (u + 1) * P, :], wr_first[u][:].rearrange("p j c -> p c j"))
+        round_on("scalar", wr_bf[:, 1], wr_second[:].rearrange("p j c -> p c j"))
         for c in range(2):
             weave_stage(c)
         scatter(2)
         for c in range(2):
             round_on("gpsimd", page_bf[c][:, :, 2:4], page_cols(2, c).unsqueeze(2).to_broadcast([P, BANK, 2]))
-        round_plane(2, 1)
+        for c in (2, 3):
+            stage_chunk(2, c)
         for c in range(2, 4):
             weave_stage(c)
         scatter(3)
 
-        page_codes = tile("page_codes", [P, T], U32)
+        left_codes = tile("left_codes", [P, 2, BANK], U32, tag="page_codes")
+        page_codes = {c: left_codes[:, c, :] for c in range(2)}
         page_sc = tile("page_sc", [P, T], U8)
+
         def quantise_page(c):
-            cols = slice(c * BANK, (c + 1) * BANK)
             nc.vector.quantize_mx(
-                out=page_codes[:, cols].bitcast(FP8X4), scales=page_sc[:, cols],
-                in_=page_bf[c][:].rearrange("p c t -> p (c t)"),
+                out=page_codes[c].bitcast(FP8X4), scales=page_sc[:, c * BANK : (c + 1) * BANK],
+                in_=page_bf[c].rearrange("p c t -> p (c t)"),
             )
 
         for c in range(4):
@@ -220,6 +228,9 @@ def tile_list_lane_agent_update_kernel(
             if c == 0:
                 quantise_wa(0)
                 quantise_page(0)
+        right_codes = tile("right_codes", [P, 2, BANK], U32, tag="bf0")
+        page_codes[2] = right_codes[:, 0, :]
+        page_codes[3] = right_codes[:, 1, :]
         for c in CHUNK_ORDER[1:]:
             quantise_page(c)
         late_codes = tile("late_codes", [P, 2, BANK], U32, tag="bf1")
@@ -245,7 +256,7 @@ def tile_list_lane_agent_update_kernel(
                     out=acc[:],
                     lhsT=wa_codes[s // 4][:, P * (s % 4) : P * (s % 4 + 1)].bitcast(FP8X4),
                     lhsT_scale=wa_sc[:, P * s : P * (s + 1)],
-                    rhs=page_codes[:, cols].bitcast(FP8X4),
+                    rhs=page_codes[c].bitcast(FP8X4),
                     rhs_scale=page_sc[:, cols],
                     start=True,
                     stop=True,

@@ -327,20 +327,19 @@ def tile_list_lane_agent_update_kernel(
         z_bf = {(0, 0): wide[0][:], (1, 0): wide[1][:], (0, 1): short0[:, 0:256, :], (0, 2): short0[:, 256:BANK, :]}
         for b, n in ((0, 0), (0, 1), (1, 0), (0, 2)):
             round_z("scalar", b, n)
-        for b, n in ((0, 0), (0, 1), (1, 0)):
-            quantise_z(b, n)
-        short1 = tile("z_short1", [P, BANK, 4], BF16, tag="bf2")
-        z_bf[1, 1] = short1[:, 0:256, :]
-        z_bf[1, 2] = short1[:, 256:BANK, :]
+        for n in range(2):
+            quantise_z(0, n)
+        z_bf[1, 1] = tile("z1_middle", [P, 256, 4], BF16, tag="bf0")[:]
         round_z("vector", 1, 1)
+        for n in range(2):
+            quantise_z(1, n)
+        z_bf[1, 2] = tile("z1_last", [P, 256, 4], BF16, tag="bf2")[:]
         round_z("vector", 1, 2)
-        finish(0)
-        for b, n in ((1, 1), (0, 2)):
-            quantise_z(b, n)
+        quantise_z(0, 2)
         for j0, j1 in SUMS[2:]:
             nc.vector.quantize_mx(
                 out=z_codes[:, 1, j0:j1].bitcast(FP8X4), scales=z_sc[:, 1, j0:j1],
-                in_=short1[:, j0 - BANK : j1 - BANK, :].rearrange("p c t -> p (c t)"),
+                in_=z_bf[1, 2][:, j0 - 768 : j1 - 768, :].rearrange("p c t -> p (c t)"),
             )
-        for n in range(1, 4):
+        for n in (1, 0, 2, 3):
             finish(n)

@@ -18,11 +18,19 @@ ALU = mybir.AluOpType
 
 P = 128
 BANK = 512
+KIB = 1024
 PAGE_BANKS = 3
 GATE_BANKS = 4
 CHUNK_ORDER = (0, 2, 1, 3)
+FIRST_BANKS = [(0, 0), (1, 0), (0, 2), (1, 2), (0, 1), (0, 3)]
 PIECES = [(0, 512), (512, 768), (768, 1024)]
 SUMS = [(0, 512), (512, 768), (768, 896), (896, 1024)]
+AREAS = [
+    ("page", 32), ("tab", 16), ("wa_raw", 16), ("xs", 16), ("z1", 16), ("gate", 32), ("v", 8), ("v_sc", 2),
+    ("v_rows", 1), ("tab_sc", 2), ("wl_raw", 4), ("wl", 4), ("wl_sc_raw", 2), ("wl_sc", 2), ("wr_raw", 8),
+    ("late_bf", 8), ("wa_bf", 4), ("page_bf", 16), ("page_codes", 8), ("page_sc", 2), ("wa_codes", 4),
+    ("wa_sc", 2), ("wo", 2), ("wo_sc", 1), ("bias", 1), ("z_codes", 8), ("z_sc", 2), ("z_bf", 8),
+]
 
 
 def tile_list_lane_agent_update_kernel(
@@ -34,9 +42,10 @@ def tile_list_lane_agent_update_kernel(
         lists = ctx.enter_context(tc.tile_pool(name="lists", bufs=1))
         keep = ctx.enter_context(tc.tile_pool(name="keep", bufs=1))
         psum = ctx.enter_context(tc.psum_pool(name="psum", bufs=1))
+        area_start = {name: KIB * sum(size for other, size in AREAS[:i]) for i, (name, kib) in enumerate(AREAS)}
 
-        def tile(name, shape, dtype, tag=None):
-            return keep.tile(shape, dtype, name=name, tag=tag or name, align_bytes=64)
+        def tile(name, shape, dtype, area, at=0):
+            return keep.tile(shape, dtype, name=name, tag=name, align_bytes=64, offset=area_start[area] + at)
 
         def round_on(engine, dst, src):
             if engine == "vector":
@@ -50,10 +59,10 @@ def tile_list_lane_agent_update_kernel(
         idx2 = lists.tile([P, S // 16], U16, name="idx2")
         idx3 = lists.tile([P, S // 16], U16, name="idx3")
 
-        tab_sc = tile("tab_sc", [P, T], U8)
-        wl_sc_raw = tile("wl_sc_raw", [P, 2, H], U8)
-        v_sc = [tile("v_sc%d" % a, [P, S], U8) for a in range(2)]
-        wo_sc = tile("wo_sc", [P, 2, N], U8)
+        tab_sc = tile("tab_sc", [P, T], U8, "tab_sc")
+        wl_sc_raw = tile("wl_sc_raw", [P, 2, H], U8, "wl_sc_raw")
+        v_sc = [tile("v_sc%d" % a, [P, S], U8, "v_sc", a * KIB) for a in range(2)]
+        wo_sc = tile("wo_sc", [P, 2, N], U8, "wo_sc")
         nc.vector.memset(tab_sc[32:64, :].bitcast(I32), 0)
         nc.vector.memset(tab_sc[64:P, :].bitcast(I32), 0)
         nc.gpsimd.memset(wl_sc_raw[:].bitcast(I32), 0)
@@ -65,86 +74,105 @@ def tile_list_lane_agent_update_kernel(
         xs_rows = xs.rearrange("(p t) c -> t p c", t=4)
         wa_rows = wa.rearrange("(p j) c -> p j c", j=4)
         wr_rows = wr.rearrange("(a p j) n -> a p j n", a=2, j=4)
-        page = [tile("page%d" % t, [P, T], F32) for t in range(4)]
-        xs_sb = [tile("xs%d" % t, [P, S], F32, tag=("ring0", "ring1", "ring4", "wa_codes")[t]) for t in range(4)]
-        wa_raw = [tile("wa_raw%d" % b, [P, 4, BANK], F32, tag="wa_raw%d" % b) for b in range(2)]
-        wr_first = [tile("wr_first%d" % u, [P, 4, N // 2], F32, tag="bf%d" % u) for u in range(2)]
-        wr_second = tile("wr_second", [P, 4, N], F32)
-        tab = [tile("tab%d" % a, [P, T], I32) for a in range(2)]
-        bl_sb = tile("bl_sb", [P, 2, 4], F32)
-        wl_raw = tile("wl_raw", [P, 2, 2 * H], U8)
-        parts = [slice(0, S // 4), slice(S // 4, S)]
+        page = [tile("page%d" % t, [P, T], F32, "page", 8 * KIB * t) for t in range(4)]
+        parts = [[slice(0, S // 4), slice(S // 4, S)]] + [[slice(0, S)]] * 3
+        xs_sb = [
+            [tile("xs%d_%d" % (t, u), [P, part.stop - part.start], F32, "xs", 4 * (S * t + part.start))
+             for u, part in enumerate(parts[t])]
+            for t in range(3)
+        ]
+        xs_sb.append([tile("xs_last", [P, S], F32, "wa_codes")])
+        wa_raw = [tile("wa_raw%d" % b, [P, 4, BANK], F32, "wa_raw", 8 * KIB * b) for b in range(2)]
+        wr_raw = [tile("wr_raw%d" % a, [P, 4, N], F32, "wr_raw", 4 * KIB * a) for a in range(2)]
+        tab = [tile("tab%d" % a, [P, T], I32, "tab", 8 * KIB * a) for a in range(2)]
+        bl_sb = tile("bl_sb", [P, 2, 4], F32, "bias")
+        bo_sb = tile("bo_sb", [P, 2], F32, "bias", 64)
+        wl_raw = tile("wl_raw", [P, 2, 2 * H], U8, "wl_raw")
+        wo_sb = tile("wo_sb", [P, 2, N], I32, "wo")
+
+        def load_xs(t, u):
+            nc.sync.dma_start(xs_sb[t][u][:], xs_rows[t][:, parts[t][u]])
+
+        def load_tab(a):
+            nc.sync.dma_start(tab[a][:], tab_words[a].rearrange("p n i -> p (n i)").bitcast(I32))
 
         nc.sync.dma_start(idx[:], offs)
         nc.sync.dma_start(tab_sc[0:32, :].bitcast(I32), tab_scales.rearrange("a q c -> (a q) c").bitcast(I32))
         nc.sync.dma_start(page[0][:], base_rows[0])
         nc.sync.dma_start(idx2[:], offs2)
-        for part in parts:
-            nc.sync.dma_start(xs_sb[0][:, part], xs_rows[0][:, part])
-        nc.sync.dma_start(tab[0][:], tab_words[0].rearrange("p n i -> p (n i)").bitcast(I32))
+        load_xs(0, 0)
+        load_xs(0, 1)
+        load_tab(0)
         for q in range(4):
             nc.gpsimd.dma_start(
                 wl_sc_raw[32 * q : 32 * q + 4, :, :].bitcast(I32),
                 wl_scales[:, 4 * q : 4 * q + 4, :].rearrange("a r c -> r a c").bitcast(I32),
             )
-        nc.sync.dma_start(tab[1][:], tab_words[1].rearrange("p n i -> p (n i)").bitcast(I32))
         nc.sync.dma_start(wl_raw[:].bitcast(I32), wl_words.rearrange("a p c -> p a c").bitcast(I32))
+        load_tab(1)
         nc.sync.dma_start(bl_sb[:], bl.rearrange("(b p t) -> p b t", b=2, t=4))
 
-        def scatter(t, entries=slice(0, S)):
-            offsets = idx2[:, entries.start // 16 : entries.stop // 16]
-            nc.vector.tensor_copy(page[t][:].indirect(offsets), xs_sb[t][:, entries])
+        def scatter(t):
+            for u, part in enumerate(parts[t]):
+                offsets = idx2[:, part.start // 16 : part.stop // 16]
+                nc.vector.tensor_copy(page[t][:].indirect(offsets), xs_sb[t][u][:])
 
-        v_sc_rows = tile("v_sc_rows", [P, S], U8)
+        v_sc_rows = tile("v_sc_rows", [P, S], U8, "v_rows")
         nc.vector.tensor_copy(v_sc_rows[:], tab_sc[:].indirect(idx[:]))
-        wl_sc = tile("wl_sc", [P, 2, H], U8)
-        nc.gpsimd.tensor_copy(
-            wl_sc[:].rearrange("p a (b t m) -> p (a b) t m", b=2, t=4),
-            wl_sc_raw[:].rearrange("p a (b m t) -> p (a b) t m", b=2, t=4),
-        )
-        wl_perm = [tile("wl_perm%d" % a, [P, 2 * H], U8, tag="stage%d" % (2 + a)) for a in range(2)]
-        for a in range(2):
-            nc.gpsimd.tensor_copy(
-                wl_perm[a][:].bitcast(U16).rearrange("p (b t m) -> p b t m", b=2, t=4),
-                wl_raw[:, a, :].bitcast(U16).rearrange("p (b m t) -> p b t m", b=2, t=4),
-            )
-        for part in parts:
-            scatter(0, part)
-        v = [tile("v%d" % a, [P, S], U32) for a in range(2)]
-        for a in range(2):
-            nc.vector.tensor_copy(v[a][:], tab[a][:].bitcast(U32).indirect(idx[:]))
         for a in range(2):
             for q in range(4):
                 first = 16 * a + 4 * q
                 nc.scalar.dma_start(
                     v_sc[a][32 * q : 32 * q + 4, :].bitcast(I32), v_sc_rows[first : first + 4, :].bitcast(I32)
                 )
+        wl_sc = tile("wl_sc", [P, 2, H], U8, "wl_sc")
+        nc.gpsimd.tensor_copy(
+            wl_sc[:].rearrange("p a (b t m) -> p (a b) t m", b=2, t=4),
+            wl_sc_raw[:].rearrange("p a (b m t) -> p (a b) t m", b=2, t=4),
+        )
+        wl_perm = [tile("wl_perm%d" % a, [P, 2 * H], U8, "wl", 2 * KIB * a) for a in range(2)]
+        for a in range(2):
+            nc.scalar.copy(
+                wl_perm[a][:].bitcast(U16).rearrange("p (b t m i) -> p b m t i", b=2, t=4, i=2),
+                wl_raw[:, a, :].bitcast(U16).rearrange("p (b m i t) -> p b m t i", b=2, t=4, i=2),
+            )
+        scatter(0)
+        v = [tile("v%d" % a, [P, S], U32, "v", 4 * KIB * a) for a in range(2)]
+        for a in range(2):
+            nc.vector.tensor_copy(v[a][:], tab[a][:].bitcast(U32).indirect(idx[:]))
 
-        def load_plane(t):
+        for t in (1, 2):
             nc.sync.dma_start(page[t][:], base_rows[t])
-            nc.sync.dma_start(xs_sb[t][:], xs_rows[t])
-
-        load_plane(1)
-        for b in range(2):
-            nc.sync.dma_start(wa_raw[b][:], wa_rows[:, :, b * BANK : (b + 1) * BANK])
-        load_plane(2)
-        for u in range(2):
-            nc.sync.dma_start(wr_first[u][:], wr_rows[0][:, :, u * P : (u + 1) * P])
-        nc.sync.dma_start(wr_second[:], wr_rows[1])
-        load_plane(3)
+            load_xs(t, 0)
+            nc.sync.dma_start(wa_raw[t - 1][:], wa_rows[:, :, (t - 1) * BANK : t * BANK])
+        nc.sync.dma_start(page[3][:], base_rows[3])
+        load_xs(3, 0)
+        for a in range(2):
+            nc.sync.dma_start(wr_raw[a][:], wr_rows[a])
         nc.sync.dma_start(idx3[:], offs3)
-        wo_sb = tile("wo_sb", [P, 2, N], I32)
         nc.sync.dma_start(wo_sb[:], wo_words.rearrange("a p n i -> p a (n i)").bitcast(I32))
         for q in range(4):
             nc.sync.dma_start(
                 wo_sc[32 * q : 32 * q + 4, :, :].bitcast(I32),
                 wo_scales[:, 4 * q : 4 * q + 4, :].rearrange("a r c -> r a c").bitcast(I32),
             )
-        bo_sb = tile("bo_sb", [P, 2], F32)
         with nc.allow_non_contiguous_dma(reason="one bias value for each partition"):
             nc.sync.dma_start(bo_sb[:], bo.rearrange("(h p) -> p h", p=P))
 
-        gate = [tile("gate%d" % s, [P, S], F32) for s in range(8)]
+        page_bf = [tile("page_bf%d" % c, [P, BANK, 4], BF16, "page_bf", 4 * KIB * c) for c in range(4)]
+
+        def weave(engine, t, c, first=0, last=BANK, both=False):
+            src = page[t][:, c * BANK + first : c * BANK + last]
+            if both:
+                round_on(engine, page_bf[c][:, first:last, t : t + 2],
+                         src.unsqueeze(2).to_broadcast([P, last - first, 2]))
+            else:
+                round_on(engine, page_bf[c][:, first:last, t], src)
+
+        for c in range(4):
+            weave("gpsimd", 0, c)
+
+        gate = [tile("gate%d" % s, [P, S], F32, "gate", 4 * KIB * s) for s in range(8)]
         for h in range(2):
             for s in range(8):
                 cols = slice(h * BANK, (h + 1) * BANK)
@@ -161,79 +189,47 @@ def tile_list_lane_agent_update_kernel(
                     )
                 nc.scalar.activation(gate[s][:, cols], acc[:], ACT.Sigmoid, bias=bl_sb[:, s // 4, s % 4 : s % 4 + 1])
 
-        wa_codes = [tile("wa_codes", [P, BANK], U32)]
-        wa_sc = tile("wa_sc", [P, H + 2 * N], U8)
-        late_bf = tile("late_bf", [P, 2, 4 * BANK], BF16)
-        wa_bf = [tile("wa_bf0", [P, 4 * BANK], BF16), late_bf[:, 0, :]]
+        late_bf = tile("late_bf", [P, 2, 4 * BANK], BF16, "late_bf")
+        wa_bf = [tile("wa_bf0", [P, 4 * BANK], BF16, "wa_bf")[:], late_bf[:, 0, :]]
         wr_bf = late_bf[:, 1, :].rearrange("p (a n j) -> p a n j", a=2, j=4)
-        stage_left = tile("stage_left", [P, 2, 2 * BANK], BF16, tag="wa_raw1")
-        stage = [stage_left[:, :, 0:BANK], stage_left[:, :, BANK : 2 * BANK]]
-        stage = stage + [tile("stage%d" % c, [P, 3, BANK], BF16)[:] for c in (2, 3)]
-        page_bf = [tile("page_bf%d" % c, [P, BANK, 4], BF16, tag="bf%d" % c)[:] for c in range(4)]
-
-        def stage_chunk(t, c):
-            round_on("gpsimd" if c < 2 else "scalar", stage[c][:, t, :], page[t][:, c * BANK : (c + 1) * BANK])
-
-        def weave_stage(c):
-            planes = 2 if c < 2 else 3
-            round_on(
-                "gpsimd" if c < 2 else "scalar", page_bf[c][:, :, 0:planes], stage[c].rearrange("p t c -> p c t")
-            )
-
-        def page_cols(t, c):
-            return page[t][:, c * BANK : (c + 1) * BANK]
-
-        def quantise_wa(b):
-            cols = slice(b * BANK, (b + 1) * BANK)
-            nc.vector.quantize_mx(out=wa_codes[b][:].bitcast(FP8X4), scales=wa_sc[:, cols], in_=wa_bf[b][:])
-
         for b in range(2):
             round_on(
-                "gpsimd",
-                wa_bf[b][:, :].rearrange("p (t m j) -> p m t j", t=4, j=4),
+                "scalar",
+                wa_bf[b].rearrange("p (t m j) -> p m t j", t=4, j=4),
                 wa_raw[b][:].rearrange("p j (m t) -> p m t j", t=4),
             )
-        round_on("gpsimd", stage_left[:, 0, :], page[0][:, 0 : 2 * BANK])
-        for c in (2, 3):
-            stage_chunk(0, c)
         scatter(1)
         for c in range(4):
-            stage_chunk(1, c)
-        for u in range(2):
-            round_on("gpsimd", wr_bf[:, 0, u * P : (u + 1) * P, :], wr_first[u][:].rearrange("p j c -> p c j"))
-        round_on("scalar", wr_bf[:, 1], wr_second[:].rearrange("p j c -> p c j"))
-        for c in range(2):
-            weave_stage(c)
+            weave("gpsimd", 1, c, both=c >= 2)
         scatter(2)
-        for c in range(2):
-            round_on("gpsimd", page_bf[c][:, :, 2:4], page_cols(2, c).unsqueeze(2).to_broadcast([P, BANK, 2]))
-        for c in (2, 3):
-            stage_chunk(2, c)
-        for c in range(2, 4):
-            weave_stage(c)
+        for c in range(4):
+            weave("gpsimd" if c < 2 else "scalar", 2, c, both=c != 2)
+        for a in range(2):
+            round_on(("gpsimd", "scalar")[a], wr_bf[:, a], wr_raw[a][:].rearrange("p j c -> p c j"))
         scatter(3)
 
-        left_codes = tile("left_codes", [P, 2, BANK], U32, tag="page_codes")
-        page_codes = {c: left_codes[:, c, :] for c in range(2)}
-        page_sc = tile("page_sc", [P, T], U8)
+        wa_codes = [tile("wa_codes0", [P, BANK], U32, "wa_codes")[:]]
+        wa_sc = tile("wa_sc", [P, H + 2 * N], U8, "wa_sc")
+        page_codes = [tile("page_codes%d" % c, [P, BANK], U32, "page_codes", 2 * KIB * c) for c in range(4)]
+        page_sc = tile("page_sc", [P, T], U8, "page_sc")
 
         def quantise_page(c):
             nc.vector.quantize_mx(
-                out=page_codes[c].bitcast(FP8X4), scales=page_sc[:, c * BANK : (c + 1) * BANK],
-                in_=page_bf[c].rearrange("p c t -> p (c t)"),
+                out=page_codes[c][:].bitcast(FP8X4), scales=page_sc[:, c * BANK : (c + 1) * BANK],
+                in_=page_bf[c][:].rearrange("p c t -> p (c t)"),
             )
 
-        for c in range(4):
-            round_on("vector" if c < 2 else "scalar", page_bf[c][:, :, 3], page_cols(3, c))
-            if c == 0:
-                quantise_wa(0)
-                quantise_page(0)
-        right_codes = tile("right_codes", [P, 2, BANK], U32, tag="bf0")
-        page_codes[2] = right_codes[:, 0, :]
-        page_codes[3] = right_codes[:, 1, :]
-        for c in CHUNK_ORDER[1:]:
-            quantise_page(c)
-        late_codes = tile("late_codes", [P, 2, BANK], U32, tag="bf1")
+        weave("scalar", 3, 2)
+        weave("scalar", 3, 3, first=BANK // 2)
+        weave("vector", 3, 0)
+        nc.vector.quantize_mx(out=wa_codes[0].bitcast(FP8X4), scales=wa_sc[:, 0:BANK], in_=wa_bf[0])
+        quantise_page(0)
+        weave("vector", 3, 1)
+        quantise_page(2)
+        weave("vector", 3, 3, last=BANK // 2)
+        quantise_page(1)
+        quantise_page(3)
+        late_codes = tile("late_codes", [P, 2, BANK], U32, "page_bf", 4 * KIB)
         wa_codes.append(late_codes[:, 0, :])
         wr_codes = late_codes[:, 1, :].rearrange("p (a n) -> p a n", a=2)
         wr_sc = wa_sc[:, H : H + 2 * N].rearrange("p (a n) -> p a n", a=2)
@@ -242,9 +238,10 @@ def tile_list_lane_agent_update_kernel(
             in_=late_bf[:].rearrange("p b c -> p (b c)"),
         )
 
-        a_tags = ["ring0", "ring1", "ring4", "tab0", "tab1", "page0", "page1", "page2"]
-
-        a_sb = [tile("a%d" % s, [P, T], F32, tag=a_tags[s]) for s in range(8)]
+        a_places = [("page", 0), ("page", 1), ("page", 2), ("tab", 0), ("tab", 1), ("wa_raw", 0), ("wa_raw", 1),
+                    ("page", 3)]
+        a_sb = [tile("a%d" % s, [P, T], F32, area, 8 * KIB * i) for s, (area, i) in enumerate(a_places)]
+        z_f32 = [tile("z%d" % b, [P, 4, S], F32, ("xs", "z1")[b]) for b in range(2)]
         done = []
 
         def project(banks):
@@ -256,7 +253,7 @@ def tile_list_lane_agent_update_kernel(
                     out=acc[:],
                     lhsT=wa_codes[s // 4][:, P * (s % 4) : P * (s % 4 + 1)].bitcast(FP8X4),
                     lhsT_scale=wa_sc[:, P * s : P * (s + 1)],
-                    rhs=page_codes[c].bitcast(FP8X4),
+                    rhs=page_codes[c][:].bitcast(FP8X4),
                     rhs_scale=page_sc[:, cols],
                     start=True,
                     stop=True,
@@ -269,32 +266,38 @@ def tile_list_lane_agent_update_kernel(
                 gate[s][:, j0:j1], ALU.mult,
             )
 
-        z_codes = tile("z_codes", [P, 2, S], U32, tag="page_codes")
-        z_sc = tile("z_sc", [P, 2, S], U8, tag="page_sc")
+        project(FIRST_BANKS)
+        for s in range(8):
+            project([(s, c) for c in CHUNK_ORDER if (s, c) not in done])
+            if s < 7:
+                pick(s, 0, S)
+        for h in range(2):
+            pick(7, h * BANK, (h + 1) * BANK)
 
-        z_f32 = [tile("z%d" % b, [P, 4, S], F32, tag=("zf0", "wa_raw0")[b]) for b in range(2)]
+        z_codes = tile("z_codes", [P, 2, S], U32, "z_codes")
+        z_sc = tile("z_sc", [P, 2, S], U8, "z_sc")
+        z_bf = {}
 
-        def round_z(engine, b, n, first=0, last=None):
+        def round_z(engine, b, n, area, at):
             j0, j1 = PIECES[n]
-            last = j1 - j0 if last is None else last
+            z_bf[b, n] = tile("z_bf%d_%d" % (b, n), [P, j1 - j0, 4], BF16, area, at)
             round_on(
                 engine,
-                z_bf[b, n][:, first:last, :].rearrange("p (c i) t -> p c t i", i=4),
-                z_f32[b][:, :, j0 + first : j0 + last].rearrange("p t (c i) -> p c t i", i=4),
+                z_bf[b, n][:].rearrange("p (c i) t -> p c t i", i=4),
+                z_f32[b][:, :, j0:j1].rearrange("p t (c i) -> p c t i", i=4),
             )
 
-        def quantise_z(b, n):
-            j0, j1 = PIECES[n]
+        def quantise_z(b, n, j0=None, j1=None):
+            start = PIECES[n][0]
+            j0, j1 = PIECES[n] if j0 is None else (j0, j1)
             nc.vector.quantize_mx(
                 out=z_codes[:, b, j0:j1].bitcast(FP8X4), scales=z_sc[:, b, j0:j1],
-                in_=z_bf[b, n].rearrange("p c t -> p (c t)"),
+                in_=z_bf[b, n][:, j0 - start : j1 - start, :].rearrange("p c t -> p (c t)"),
             )
-
-        results = {}
 
         def finish(n):
             j0, j1 = SUMS[n]
-            results[n] = tile("res%d" % n, [P, 2, j1 - j0], F32, tag=("res0", "res1", "bf2", "res3")[n])
+            result = tile("res%d" % n, [P, 2, j1 - j0], F32, "wr_raw", 8 * j0)
             for h in range(2):
                 rows = slice(h * P, (h + 1) * P)
                 acc = psum.tile([P, j1 - j0], F32, name="acc", tag="bank%d" % ((PAGE_BANKS + 2 * n + h) % 8))
@@ -308,38 +311,25 @@ def tile_list_lane_agent_update_kernel(
                         out=acc[:], lhsT=w.bitcast(FP8X4), lhsT_scale=w_sc, rhs=x.bitcast(FP8X4), rhs_scale=x_sc,
                         start=(i == 0), stop=(i == len(passes) - 1),
                     )
-                res = results[n][:, h, :]
+                res = result[:, h, :]
                 if n > 1 and h == 1:
                     nc.vector.tensor_scalar(res, acc[:], bo_sb[:, h : h + 1], None, ALU.add)
                 else:
                     nc.scalar.activation(res, acc[:], ACT.Identity, bias=bo_sb[:, h : h + 1])
                 nc.sync.dma_start(out[rows, j0:j1], res)
 
-        project([(0, 0), (1, 0)])
-        for s in range(8):
-            project([(s, c) for c in CHUNK_ORDER if (s, c) not in done])
-            if s < 7:
-                pick(s, 0, S)
-        for h in range(2):
-            pick(7, h * BANK, (h + 1) * BANK)
-        wide = [tile("z_wide%d" % b, [P, BANK, 4], BF16, tag=("bf0", "bf2")[b]) for b in range(2)]
-        short0 = tile("z_short0", [P, BANK, 4], BF16, tag="bf1")
-        z_bf = {(0, 0): wide[0][:], (1, 0): wide[1][:], (0, 1): short0[:, 0:256, :], (0, 2): short0[:, 256:BANK, :]}
-        for b, n in ((0, 0), (0, 1), (1, 0), (0, 2)):
-            round_z("scalar", b, n)
+        round_z("scalar", 0, 0, "page_codes", 4 * KIB)
+        round_z("scalar", 0, 1, "page_codes", 0)
+        round_z("scalar", 1, 0, "z_bf", 0)
+        round_z("scalar", 0, 2, "page_codes", 2 * KIB)
         for n in range(2):
             quantise_z(0, n)
-        z_bf[1, 1] = tile("z1_middle", [P, 256, 4], BF16, tag="bf0")[:]
-        round_z("vector", 1, 1)
+        round_z("vector", 1, 1, "page_codes", 4 * KIB)
         for n in range(2):
             quantise_z(1, n)
-        z_bf[1, 2] = tile("z1_last", [P, 256, 4], BF16, tag="bf2")[:]
-        round_z("vector", 1, 2)
+        round_z("vector", 1, 2, "z_bf", 0)
         quantise_z(0, 2)
         for j0, j1 in SUMS[2:]:
-            nc.vector.quantize_mx(
-                out=z_codes[:, 1, j0:j1].bitcast(FP8X4), scales=z_sc[:, 1, j0:j1],
-                in_=z_bf[1, 2][:, j0 - 768 : j1 - 768, :].rearrange("p c t -> p (c t)"),
-            )
+            quantise_z(1, 2, j0, j1)
         for n in (1, 0, 2, 3):
             finish(n)

@@ -22,7 +22,7 @@ KIB = 1024
 PAGE_BANKS = 3
 GATE_BANKS = 4
 CHUNK_ORDER = (0, 2, 1, 3)
-FIRST_BANKS = [(0, 0), (1, 0), (0, 2), (1, 2), (0, 1), (0, 3)]
+FIRST_BANKS = [(0, 0), (1, 0), (0, 2), (0, 1), (0, 3)]
 PIECES = [(0, 512), (512, 768), (768, 1024)]
 SUMS = [(0, 512), (512, 768), (768, 896), (896, 1024)]
 AREAS = [

@@ -23,8 +23,7 @@ PAGE_BANKS = 3
 GATE_BANKS = 4
 CHUNK_ORDER = (0, 2, 1, 3)
 FIRST_BANKS = [(0, 0), (1, 0), (0, 2), (0, 1), (0, 3)]
-PIECES = [(0, 512), (512, 768), (768, 1024)]
-SUMS = [(0, 512), (512, 768), (768, 896), (896, 1024)]
+SUMS = [(0, 256), (256, 512), (512, 768), (768, 896), (896, 1024)]
 AREAS = [
     ("page", 32), ("tab", 16), ("wa_raw", 16), ("xs", 16), ("z1", 16), ("gate", 32), ("v", 8), ("v_sc", 2),
     ("v_rows", 1), ("tab_sc", 2), ("wl_raw", 4), ("wl", 4), ("wl_sc_raw", 2), ("wl_sc", 2), ("wr_raw", 8),
@@ -173,21 +172,27 @@ def tile_list_lane_agent_update_kernel(
             weave("gpsimd", 0, c)
 
         gate = [tile("gate%d" % s, [P, S], F32, "gate", 4 * KIB * s) for s in range(8)]
+        def make_gate(s, j0, j1, bank):
+            acc = psum.tile([P, j1 - j0], F32, name="acc", tag="bank%d" % bank)
+            for a in range(2):
+                nc.tensor.matmul_mx(
+                    out=acc[:],
+                    lhsT=wl_perm[a][:, 2 * P * s : 2 * P * (s + 1)].bitcast(FP4X4),
+                    lhsT_scale=wl_sc[:, a, P * s : P * (s + 1)],
+                    rhs=v[a][:, j0:j1].bitcast(FP8X4),
+                    rhs_scale=v_sc[a][:, j0:j1],
+                    start=(a == 0),
+                    stop=(a == 1),
+                )
+            nc.scalar.activation(gate[s][:, j0:j1], acc[:], ACT.Sigmoid, bias=bl_sb[:, s // 4, s % 4 : s % 4 + 1])
+
         for h in range(2):
             for s in range(8):
-                cols = slice(h * BANK, (h + 1) * BANK)
-                acc = psum.tile([P, BANK], F32, name="acc", tag="bank%d" % (s % GATE_BANKS))
-                for a in range(2):
-                    nc.tensor.matmul_mx(
-                        out=acc[:],
-                        lhsT=wl_perm[a][:, 2 * P * s : 2 * P * (s + 1)].bitcast(FP4X4),
-                        lhsT_scale=wl_sc[:, a, P * s : P * (s + 1)],
-                        rhs=v[a][:, cols].bitcast(FP8X4),
-                        rhs_scale=v_sc[a][:, cols],
-                        start=(a == 0),
-                        stop=(a == 1),
-                    )
-                nc.scalar.activation(gate[s][:, cols], acc[:], ACT.Sigmoid, bias=bl_sb[:, s // 4, s % 4 : s % 4 + 1])
+                if (s, h) == (6, 1):
+                    make_gate(s, 512, 768, s % GATE_BANKS)
+                    make_gate(s, 768, 896, GATE_BANKS)
+                else:
+                    make_gate(s, h * BANK, (h + 1) * BANK, s % GATE_BANKS)
 
         late_bf = tile("late_bf", [P, 2, 4 * BANK], BF16, "late_bf")
         wa_bf = [tile("wa_bf0", [P, 4 * BANK], BF16, "wa_bf")[:], late_bf[:, 0, :]]
@@ -241,7 +246,14 @@ def tile_list_lane_agent_update_kernel(
         a_places = [("page", 0), ("page", 1), ("page", 2), ("tab", 0), ("tab", 1), ("wa_raw", 0), ("wa_raw", 1),
                     ("page", 3)]
         a_sb = [tile("a%d" % s, [P, T], F32, area, 8 * KIB * i) for s, (area, i) in enumerate(a_places)]
-        z_f32 = [tile("z%d" % b, [P, 4, S], F32, ("xs", "z1")[b]) for b in range(2)]
+        z_whole = tile("z0", [P, 4, S], F32, "xs")
+        z_halves = [tile("z1_%d" % h, [P, 4, BANK], F32, "z1", 8 * KIB * h) for h in range(2)]
+
+        def z_f32(b, planes, j0, j1):
+            if b == 0:
+                return z_whole[:, planes, j0:j1]
+            return z_halves[j0 // BANK][:, planes, j0 % BANK : j0 % BANK + j1 - j0]
+
         done = []
 
         def project(banks):
@@ -262,37 +274,40 @@ def tile_list_lane_agent_update_kernel(
 
         def pick(s, j0, j1):
             nc.vector.tensor_tensor(
-                z_f32[s // 4][:, s % 4, j0:j1], a_sb[s][:].indirect(idx3[:, j0 // 16 : j1 // 16]),
+                z_f32(s // 4, s % 4, j0, j1), a_sb[s][:].indirect(idx3[:, j0 // 16 : j1 // 16]),
                 gate[s][:, j0:j1], ALU.mult,
             )
 
         project(FIRST_BANKS)
         for s in range(8):
             project([(s, c) for c in CHUNK_ORDER if (s, c) not in done])
-            if s < 7:
+            if s < 4:
                 pick(s, 0, S)
+            elif s < 6:
+                for h in range(2):
+                    pick(s, h * BANK, (h + 1) * BANK)
+        make_gate(6, 896, S, len(done) % PAGE_BANKS)
         for h in range(2):
-            pick(7, h * BANK, (h + 1) * BANK)
+            for s in (6, 7):
+                pick(s, h * BANK, (h + 1) * BANK)
 
         z_codes = tile("z_codes", [P, 2, S], U32, "z_codes")
         z_sc = tile("z_sc", [P, 2, S], U8, "z_sc")
         z_bf = {}
 
-        def round_z(engine, b, n, area, at):
-            j0, j1 = PIECES[n]
-            z_bf[b, n] = tile("z_bf%d_%d" % (b, n), [P, j1 - j0, 4], BF16, area, at)
+        def round_z(engine, b, j0, j1, area, at):
+            z_bf[b, j0] = tile("z_bf%d_%d" % (b, j0), [P, j1 - j0, 4], BF16, area, at)
             round_on(
                 engine,
-                z_bf[b, n][:].rearrange("p (c i) t -> p c t i", i=4),
-                z_f32[b][:, :, j0:j1].rearrange("p t (c i) -> p c t i", i=4),
+                z_bf[b, j0][:].rearrange("p (c i) t -> p c t i", i=4),
+                z_f32(b, slice(0, 4), j0, j1).rearrange("p t (c i) -> p c t i", i=4),
             )
 
-        def quantise_z(b, n, j0=None, j1=None):
-            start = PIECES[n][0]
-            j0, j1 = PIECES[n] if j0 is None else (j0, j1)
+        def quantise_z(b, j0, j1):
+            start = max(j for other, j in z_bf if other == b and j <= j0)
             nc.vector.quantize_mx(
                 out=z_codes[:, b, j0:j1].bitcast(FP8X4), scales=z_sc[:, b, j0:j1],
-                in_=z_bf[b, n][:, j0 - start : j1 - start, :].rearrange("p c t -> p (c t)"),
+                in_=z_bf[b, start][:, j0 - start : j1 - start, :].rearrange("p c t -> p (c t)"),
             )
 
         def finish(n):
@@ -312,24 +327,26 @@ def tile_list_lane_agent_update_kernel(
                         start=(i == 0), stop=(i == len(passes) - 1),
                     )
                 res = result[:, h, :]
-                if n > 1 and h == 1:
+                if n > 2 and h == 1:
                     nc.vector.tensor_scalar(res, acc[:], bo_sb[:, h : h + 1], None, ALU.add)
                 else:
                     nc.scalar.activation(res, acc[:], ACT.Identity, bias=bo_sb[:, h : h + 1])
                 nc.sync.dma_start(out[rows, j0:j1], res)
 
-        round_z("scalar", 0, 0, "page_codes", 4 * KIB)
-        round_z("scalar", 0, 1, "page_codes", 0)
-        round_z("scalar", 1, 0, "z_bf", 0)
-        round_z("scalar", 0, 2, "page_codes", 2 * KIB)
-        for n in range(2):
-            quantise_z(0, n)
-        round_z("vector", 1, 1, "page_codes", 4 * KIB)
-        for n in range(2):
-            quantise_z(1, n)
-        round_z("vector", 1, 2, "z_bf", 0)
-        quantise_z(0, 2)
-        for j0, j1 in SUMS[2:]:
-            quantise_z(1, 2, j0, j1)
-        for n in (1, 0, 2, 3):
+        round_z("scalar", 0, 0, 512, "page_codes", 4 * KIB)
+        round_z("scalar", 1, 0, 512, "z_bf", 0)
+        round_z("scalar", 0, 512, 768, "page_codes", 0)
+        round_z("scalar", 0, 768, 896, "page_codes", 2 * KIB)
+        for j0, j1 in SUMS[:2]:
+            for b in range(2):
+                quantise_z(b, j0, j1)
+        round_z("vector", 1, 512, 768, "z1", 0)
+        for b in range(2):
+            quantise_z(b, 512, 768)
+        round_z("vector", 1, 768, 1024, "z_bf", 0)
+        round_z("vector", 0, 896, 1024, "z_bf", 2 * KIB)
+        for j0, j1 in SUMS[3:]:
+            for b in range(2):
+                quantise_z(b, j0, j1)
+        for n in range(len(SUMS)):
             finish(n)

@@ -331,7 +331,10 @@ def tile_list_lane_agent_update_kernel(
                     nc.vector.tensor_scalar(res, acc[:], bo_sb[:, h : h + 1], None, ALU.add)
                 else:
                     nc.scalar.activation(res, acc[:], ACT.Identity, bias=bo_sb[:, h : h + 1])
-                nc.sync.dma_start(out[rows, j0:j1], res)
+                if n < 3:
+                    nc.sync.dma_start(out[rows, j0:j1], res)
+            if n >= 3:
+                nc.sync.dma_start(out.rearrange("(h p) j -> p h j", p=P)[:, :, j0:j1], result[:])
 
         round_z("scalar", 0, 0, 512, "page_codes", 4 * KIB)
         round_z("scalar", 1, 0, 512, "z_bf", 0)

from contextlib import ExitStack

import concourse.mybir as mybir

H, N, T, S = 1024, 256, 2048, 1024
FLOPS = 5368709120

F32 = mybir.dt.float32
BF16 = mybir.dt.bfloat16
I32 = mybir.dt.int32
U32 = mybir.dt.uint32
U16 = mybir.dt.uint16
U8 = mybir.dt.uint8
FP8X4 = mybir.dt.float8_e4m3fn_x4
FP4X4 = mybir.dt.float4_e2m1fn_x4
ACT = mybir.ActivationFunctionType
ALU = mybir.AluOpType

P = 128
BANK = 512
KIB = 1024
PAGE_BANKS = 3
GATE_BANKS = 4
CHUNK_ORDER = (0, 2, 1, 3)
FIRST_BANKS = [(0, 0), (1, 0), (0, 2), (0, 1), (0, 3)]
SUMS = [(0, 256), (256, 512), (512, 768), (768, 896), (896, 1024)]
AREAS = [
    ("page", 32), ("tab", 16), ("wa_raw", 16), ("xs", 16), ("z1", 16), ("gate", 32), ("v", 8), ("v_sc", 2),
    ("v_rows", 1), ("tab_sc", 2), ("wl_raw", 4), ("wl", 4), ("wl_sc_raw", 2), ("wl_sc", 2), ("wr_raw", 8),
    ("late_bf", 8), ("wa_bf", 4), ("page_bf", 16), ("page_codes", 8), ("page_sc", 2), ("wa_codes", 4),
    ("wa_sc", 2), ("wo", 2), ("wo_sc", 1), ("bias", 1), ("z_codes", 8), ("z_sc", 2), ("z_bf", 8),
]


def tile_list_lane_agent_update_kernel(
    tc, tab_words, tab_scales, offs, xs, base, offs2, offs3, wa,
    wl_words, wl_scales, bl, wo_words, wo_scales, wr, bo, out,
):
    nc = tc.nc
    with ExitStack() as ctx:
        lists = ctx.enter_context(tc.tile_pool(name="lists", bufs=1))
        keep = ctx.enter_context(tc.tile_pool(name="keep", bufs=1))
        psum = ctx.enter_context(tc.psum_pool(name="psum", bufs=1))
        area_start = {name: KIB * sum(size for other, size in AREAS[:i]) for i, (name, kib) in enumerate(AREAS)}

        def tile(name, shape, dtype, area, at=0):
            return keep.tile(shape, dtype, name=name, tag=name, align_bytes=64, offset=area_start[area] + at)

        def round_on(engine, dst, src):
            if engine == "vector":
                nc.vector.tensor_copy(dst, src)
            elif engine == "scalar":
                nc.scalar.copy(dst, src)
            else:
                nc.gpsimd.tensor_scalar(dst, src, 1.0, 0.0, ALU.mult, ALU.add)

        idx = lists.tile([P, S // 16], U16, name="idx")
        idx2 = lists.tile([P, S // 16], U16, name="idx2")
        idx3 = lists.tile([P, S // 16], U16, name="idx3")

        tab_sc = tile("tab_sc", [P, T], U8, "tab_sc")
        wl_sc_raw = tile("wl_sc_raw", [P, 2, H], U8, "wl_sc_raw")
        v_sc = [tile("v_sc%d" % a, [P, S], U8, "v_sc", a * KIB) for a in range(2)]
        wo_sc = tile("wo_sc", [P, 2, N], U8, "wo_sc")
        nc.vector.memset(tab_sc[32:64, :].bitcast(I32), 0)
        nc.vector.memset(tab_sc[64:P, :].bitcast(I32), 0)
        nc.gpsimd.memset(wl_sc_raw[:].bitcast(I32), 0)
        for a in range(2):
            nc.vector.memset(v_sc[a][:].bitcast(I32), 0)
        nc.vector.memset(wo_sc[:].bitcast(I32), 0)

        base_rows = base.rearrange("(p t) c -> t p c", t=4)
        xs_rows = xs.rearrange("(p t) c -> t p c", t=4)
        wa_rows = wa.rearrange("(p j) c -> p j c", j=4)
        wr_rows = wr.rearrange("(a p j) n -> a p j n", a=2, j=4)
        page = [tile("page%d" % t, [P, T], F32, "page", 8 * KIB * t) for t in range(4)]
        parts = [[slice(0, S // 4), slice(S // 4, S)]] + [[slice(0, S)]] * 3
        xs_sb = [
            [tile("xs%d_%d" % (t, u), [P, part.stop - part.start], F32, "xs", 4 * (S * t + part.start))
             for u, part in enumerate(parts[t])]
            for t in range(3)
        ]
        xs_sb.append([tile("xs_last", [P, S], F32, "wa_codes")])
        wa_raw = [tile("wa_raw%d" % b, [P, 4, BANK], F32, "wa_raw", 8 * KIB * b) for b in range(2)]
        wr_raw = [tile("wr_raw%d" % a, [P, 4, N], F32, "wr_raw", 4 * KIB * a) for a in range(2)]
        tab = [tile("tab%d" % a, [P, T], I32, "tab", 8 * KIB * a) for a in range(2)]
        bl_sb = tile("bl_sb", [P, 2, 4], F32, "bias")
        bo_sb = tile("bo_sb", [P, 2], F32, "bias", 64)
        wl_raw = tile("wl_raw", [P, 2, 2 * H], U8, "wl_raw")
        wo_sb = tile("wo_sb", [P, 2, N], I32, "wo")

        def load_xs(t, u):
            nc.sync.dma_start(xs_sb[t][u][:], xs_rows[t][:, parts[t][u]])

        def load_tab(a):
            nc.sync.dma_start(tab[a][:], tab_words[a].rearrange("p n i -> p (n i)").bitcast(I32))

        nc.sync.dma_start(idx[:], offs)
        nc.sync.dma_start(tab_sc[0:32, :].bitcast(I32), tab_scales.rearrange("a q c -> (a q) c").bitcast(I32))
        nc.sync.dma_start(page[0][:], base_rows[0])
        nc.sync.dma_start(idx2[:], offs2)
        load_xs(0, 0)
        load_xs(0, 1)
        load_tab(0)
        for q in range(4):
            nc.gpsimd.dma_start(
                wl_sc_raw[32 * q : 32 * q + 4, :, :].bitcast(I32),
                wl_scales[:, 4 * q : 4 * q + 4, :].rearrange("a r c -> r a c").bitcast(I32),
            )
        nc.sync.dma_start(wl_raw[:].bitcast(I32), wl_words.rearrange("a p c -> p a c").bitcast(I32))
        load_tab(1)
        nc.sync.dma_start(bl_sb[:], bl.rearrange("(b p t) -> p b t", b=2, t=4))

        def scatter(t):
            for u, part in enumerate(parts[t]):
                offsets = idx2[:, part.start // 16 : part.stop // 16]
                nc.vector.tensor_copy(page[t][:].indirect(offsets), xs_sb[t][u][:])

        v_sc_rows = tile("v_sc_rows", [P, S], U8, "v_rows")
        nc.vector.tensor_copy(v_sc_rows[:], tab_sc[:].indirect(idx[:]))
        for a in range(2):
            for q in range(4):
                first = 16 * a + 4 * q
                nc.scalar.dma_start(
                    v_sc[a][32 * q : 32 * q + 4, :].bitcast(I32), v_sc_rows[first : first + 4, :].bitcast(I32)
                )
        wl_sc = tile("wl_sc", [P, 2, H], U8, "wl_sc")
        nc.gpsimd.tensor_copy(
            wl_sc[:].rearrange("p a (b t m) -> p (a b) t m", b=2, t=4),
            wl_sc_raw[:].rearrange("p a (b m t) -> p (a b) t m", b=2, t=4),
        )
        wl_perm = [tile("wl_perm%d" % a, [P, 2 * H], U8, "wl", 2 * KIB * a) for a in range(2)]
        for a in range(2):
            nc.scalar.copy(
                wl_perm[a][:].bitcast(U16).rearrange("p (b t m i) -> p b m t i", b=2, t=4, i=2),
                wl_raw[:, a, :].bitcast(U16).rearrange("p (b m i t) -> p b m t i", b=2, t=4, i=2),
            )
        scatter(0)
        v = [tile("v%d" % a, [P, S], U32, "v", 4 * KIB * a) for a in range(2)]
        for a in range(2):
            nc.vector.tensor_copy(v[a][:], tab[a][:].bitcast(U32).indirect(idx[:]))

        for t in (1, 2):
            nc.sync.dma_start(page[t][:], base_rows[t])
            load_xs(t, 0)
            nc.sync.dma_start(wa_raw[t - 1][:], wa_rows[:, :, (t - 1) * BANK : t * BANK])
        nc.sync.dma_start(page[3][:], base_rows[3])
        load_xs(3, 0)
        for a in range(2):
            nc.sync.dma_start(wr_raw[a][:], wr_rows[a])
        nc.sync.dma_start(idx3[:], offs3)
        nc.sync.dma_start(wo_sb[:], wo_words.rearrange("a p n i -> p a (n i)").bitcast(I32))
        for q in range(4):
            nc.sync.dma_start(
                wo_sc[32 * q : 32 * q + 4, :, :].bitcast(I32),
                wo_scales[:, 4 * q : 4 * q + 4, :].rearrange("a r c -> r a c").bitcast(I32),
            )
        with nc.allow_non_contiguous_dma(reason="one bias value for each partition"):
            nc.sync.dma_start(bo_sb[:], bo.rearrange("(h p) -> p h", p=P))

        page_bf = [tile("page_bf%d" % c, [P, BANK, 4], BF16, "page_bf", 4 * KIB * c) for c in range(4)]

        def weave(engine, t, c, first=0, last=BANK, both=False):
            src = page[t][:, c * BANK + first : c * BANK + last]
            if both:
                round_on(engine, page_bf[c][:, first:last, t : t + 2],
                         src.unsqueeze(2).to_broadcast([P, last - first, 2]))
            else:
                round_on(engine, page_bf[c][:, first:last, t], src)

        for c in range(4):
            weave("gpsimd", 0, c)

        gate = [tile("gate%d" % s, [P, S], F32, "gate", 4 * KIB * s) for s in range(8)]
        def make_gate(s, j0, j1, bank):
            acc = psum.tile([P, j1 - j0], F32, name="acc", tag="bank%d" % bank)
            for a in range(2):
                nc.tensor.matmul_mx(
                    out=acc[:],
                    lhsT=wl_perm[a][:, 2 * P * s : 2 * P * (s + 1)].bitcast(FP4X4),
                    lhsT_scale=wl_sc[:, a, P * s : P * (s + 1)],
                    rhs=v[a][:, j0:j1].bitcast(FP8X4),
                    rhs_scale=v_sc[a][:, j0:j1],
                    start=(a == 0),
                    stop=(a == 1),
                )
            nc.scalar.activation(gate[s][:, j0:j1], acc[:], ACT.Sigmoid, bias=bl_sb[:, s // 4, s % 4 : s % 4 + 1])

        for h in range(2):
            for s in range(8):
                if (s, h) == (6, 1):
                    make_gate(s, 512, 768, s % GATE_BANKS)
                    make_gate(s, 768, 896, GATE_BANKS)
                else:
                    make_gate(s, h * BANK, (h + 1) * BANK, s % GATE_BANKS)

        late_bf = tile("late_bf", [P, 2, 4 * BANK], BF16, "late_bf")
        wa_bf = [tile("wa_bf0", [P, 4 * BANK], BF16, "wa_bf")[:], late_bf[:, 0, :]]
        wr_bf = late_bf[:, 1, :].rearrange("p (a n j) -> p a n j", a=2, j=4)
        for b in range(2):
            round_on(
                "scalar",
                wa_bf[b].rearrange("p (t m j) -> p m t j", t=4, j=4),
                wa_raw[b][:].rearrange("p j (m t) -> p m t j", t=4),
            )
        scatter(1)
        for c in range(4):
            weave("gpsimd", 1, c, both=c >= 2)
        scatter(2)
        for c in range(4):
            weave("gpsimd" if c < 2 else "scalar", 2, c, both=c != 2)
        for a in range(2):
            round_on(("gpsimd", "scalar")[a], wr_bf[:, a], wr_raw[a][:].rearrange("p j c -> p c j"))
        scatter(3)

        wa_codes = [tile("wa_codes0", [P, BANK], U32, "wa_codes")[:]]
        wa_sc = tile("wa_sc", [P, H + 2 * N], U8, "wa_sc")
        page_codes = [tile("page_codes%d" % c, [P, BANK], U32, "page_codes", 2 * KIB * c) for c in range(4)]
        page_sc = tile("page_sc", [P, T], U8, "page_sc")

        def quantise_page(c):
            nc.vector.quantize_mx(
                out=page_codes[c][:].bitcast(FP8X4), scales=page_sc[:, c * BANK : (c + 1) * BANK],
                in_=page_bf[c][:].rearrange("p c t -> p (c t)"),
            )

        weave("scalar", 3, 2)
        weave("scalar", 3, 3, first=BANK // 2)
        weave("vector", 3, 0)
        nc.vector.quantize_mx(out=wa_codes[0].bitcast(FP8X4), scales=wa_sc[:, 0:BANK], in_=wa_bf[0])
        quantise_page(0)
        weave("vector", 3, 1)
        quantise_page(2)
        weave("vector", 3, 3, last=BANK // 2)
        quantise_page(1)
        quantise_page(3)
        late_codes = tile("late_codes", [P, 2, BANK], U32, "page_bf", 4 * KIB)
        wa_codes.append(late_codes[:, 0, :])
        wr_codes = late_codes[:, 1, :].rearrange("p (a n) -> p a n", a=2)
        wr_sc = wa_sc[:, H : H + 2 * N].rearrange("p (a n) -> p a n", a=2)
        nc.vector.quantize_mx(
            out=late_codes[:].rearrange("p b c -> p (b c)").bitcast(FP8X4), scales=wa_sc[:, BANK : H + 2 * N],
            in_=late_bf[:].rearrange("p b c -> p (b c)"),
        )

        a_places = [("page", 0), ("page", 1), ("page", 2), ("tab", 0), ("tab", 1), ("wa_raw", 0), ("wa_raw", 1),
                    ("page", 3)]
        a_sb = [tile("a%d" % s, [P, T], F32, area, 8 * KIB * i) for s, (area, i) in enumerate(a_places)]
        z_whole = tile("z0", [P, 4, S], F32, "xs")
        z_halves = [tile("z1_%d" % h, [P, 4, BANK], F32, "z1", 8 * KIB * h) for h in range(2)]

        def z_f32(b, planes, j0, j1):
            if b == 0:
                return z_whole[:, planes, j0:j1]
            return z_halves[j0 // BANK][:, planes, j0 % BANK : j0 % BANK + j1 - j0]

        done = []

        def project(banks):
            for s, c in banks:
                cols = slice(c * BANK, (c + 1) * BANK)
                acc = psum.tile([P, BANK], F32, name="acc", tag="bank%d" % (len(done) % PAGE_BANKS))
                done.append((s, c))
                nc.tensor.matmul_mx(
                    out=acc[:],
                    lhsT=wa_codes[s // 4][:, P * (s % 4) : P * (s % 4 + 1)].bitcast(FP8X4),
                    lhsT_scale=wa_sc[:, P * s : P * (s + 1)],
                    rhs=page_codes[c][:].bitcast(FP8X4),
                    rhs_scale=page_sc[:, cols],
                    start=True,
                    stop=True,
                )
                nc.scalar.copy(a_sb[s][:, cols], acc[:])

        def pick(s, j0, j1):
            nc.vector.tensor_tensor(
                z_f32(s // 4, s % 4, j0, j1), a_sb[s][:].indirect(idx3[:, j0 // 16 : j1 // 16]),
                gate[s][:, j0:j1], ALU.mult,
            )

        project(FIRST_BANKS)
        for s in range(8):
            project([(s, c) for c in CHUNK_ORDER if (s, c) not in done])
            if s < 4:
                pick(s, 0, S)
            elif s < 6:
                for h in range(2):
                    pick(s, h * BANK, (h + 1) * BANK)
        make_gate(6, 896, S, len(done) % PAGE_BANKS)
        for h in range(2):
            for s in (6, 7):
                pick(s, h * BANK, (h + 1) * BANK)

        z_codes = tile("z_codes", [P, 2, S], U32, "z_codes")
        z_sc = tile("z_sc", [P, 2, S], U8, "z_sc")
        z_bf = {}

        def round_z(engine, b, j0, j1, area, at):
            z_bf[b, j0] = tile("z_bf%d_%d" % (b, j0), [P, j1 - j0, 4], BF16, area, at)
            round_on(
                engine,
                z_bf[b, j0][:].rearrange("p (c i) t -> p c t i", i=4),
                z_f32(b, slice(0, 4), j0, j1).rearrange("p t (c i) -> p c t i", i=4),
            )

        def quantise_z(b, j0, j1):
            start = max(j for other, j in z_bf if other == b and j <= j0)
            nc.vector.quantize_mx(
                out=z_codes[:, b, j0:j1].bitcast(FP8X4), scales=z_sc[:, b, j0:j1],
                in_=z_bf[b, start][:, j0 - start : j1 - start, :].rearrange("p c t -> p (c t)"),
            )

        def finish(n):
            j0, j1 = SUMS[n]
            result = tile("res%d" % n, [P, 2, j1 - j0], F32, "wr_raw", 8 * j0)
            for h in range(2):
                rows = slice(h * P, (h + 1) * P)
                acc = psum.tile([P, j1 - j0], F32, name="acc", tag="bank%d" % ((PAGE_BANKS + 2 * n + h) % 8))
                passes = [(wr_codes[:, a, rows], wr_sc[:, a, rows], v[a][:, j0:j1], v_sc[a][:, j0:j1]) for a in range(2)]
                passes = passes + [
                    (wo_sb[:, b, rows], wo_sc[:, b, rows], z_codes[:, b, j0:j1], z_sc[:, b, j0:j1])
                    for b in (0, 1)
                ]
                for i, (w, w_sc, x, x_sc) in enumerate(passes):
                    nc.tensor.matmul_mx(
                        out=acc[:], lhsT=w.bitcast(FP8X4), lhsT_scale=w_sc, rhs=x.bitcast(FP8X4), rhs_scale=x_sc,
                        start=(i == 0), stop=(i == len(passes) - 1),
                    )
                res = result[:, h, :]
                if n > 2 and h == 1:
                    nc.vector.tensor_scalar(res, acc[:], bo_sb[:, h : h + 1], None, ALU.add)
                else:
                    nc.scalar.activation(res, acc[:], ACT.Identity, bias=bo_sb[:, h : h + 1])
                if n < 3:
                    nc.sync.dma_start(out[rows, j0:j1], res)
            if n >= 3:
                nc.sync.dma_start(out.rearrange("(h p) j -> p h j", p=P)[:, :, j0:j1], result[:])

        round_z("scalar", 0, 0, 512, "page_codes", 4 * KIB)
        round_z("scalar", 1, 0, 512, "z_bf", 0)
        round_z("scalar", 0, 512, 768, "page_codes", 0)
        round_z("scalar", 0, 768, 896, "page_codes", 2 * KIB)
        for j0, j1 in SUMS[:2]:
            for b in range(2):
                quantise_z(b, j0, j1)
        round_z("vector", 1, 512, 768, "z1", 0)
        for b in range(2):
            quantise_z(b, 512, 768)
        round_z("vector", 1, 768, 1024, "z_bf", 0)
        round_z("vector", 0, 896, 1024, "z_bf", 2 * KIB)
        for j0, j1 in SUMS[3:]:
            for b in range(2):
                quantise_z(b, j0, j1)
        for n in range(len(SUMS)):
            finish(n)
